import numpy as np, ml_dtypes
CORES = [16,32,48,64,80]
N = 5
BF = ml_dtypes.bfloat16
V, B, L, CAP, RO = 816, 1024, 256, 64, 5
W, NB = N * V, N * B
def by_good(a):
    return np.ascontiguousarray(a.reshape(N, 8, 16, -1).transpose(1, 0, 3, 2)).reshape(8, -1, 16)
def by_rank(a):
    return np.ascontiguousarray(a.reshape(8, N, -1, 16).transpose(1, 0, 3, 2)).reshape(N, 128, -1)
def money(rng, lo, hi):
    return (0.5 + 0.5 * rng.random((8, NB, 16))) * np.exp2(rng.integers(lo, hi, (8, NB, 1)))
def rooms(rng):
    n = rng.choice(np.array([0, 1, 2, 3, 6, 16]), (8, W, 1), p=[0.1, 0.35, 0.25, 0.15, 0.1, 0.05])
    return np.argsort(rng.random((8, W, 16)), axis=-1) < n
def lodge(rng, room, stay, first, old, fixed=()):
    H = np.where(room, 0, NB + 1).astype(np.int64); hold = np.full((8, NB), W, np.int64)
    for g in range(8):
        h = H[g].reshape(-1).copy(); free = room[g].reshape(-1).copy(); st = stay[g].copy()
        for m, x, s, b, sign in fixed:
            if m == g: h[16 * x + s] = sign * (b + 1); free[16 * x + s] = False; st[b] = False; hold[g, b] = x
        key = np.where(free, rng.random(16 * W) + np.repeat(first[g], 16), 1e9)
        names = rng.permutation(np.flatnonzero(st)); n = min(len(names), int(np.count_nonzero(free)))
        names = names[:n]; pl = np.argsort(key)[:n]
        h[pl] = (names + 1) * np.where(rng.random(n) < old[g][pl // 16], -1, 1); hold[g, names] = pl // 16
        H[g] = h.reshape(W, 16)
    return H, hold
def parts(rng):
    n = W // 8; hot = np.argsort(rng.random((8, W)), axis=1)[:, :n]; F = rng.integers(0, W, (8, NB, 16)); first = np.ones((8, W))
    for g in range(8):
        F[g] = np.where(rng.random((NB, 16)) < 0.5, hot[g][rng.integers(0, n, (NB, 16))], F[g]); first[g, hot[g]] = 0.0
    U = rng.integers(1, 16, (8, NB, 16)); A = rng.random((8, W, 16), dtype=np.float32) * np.float32(0.75) + np.float32(0.25)
    return F, U, A, money(rng, -1, 2), rooms(rng), rng.random((8, NB)) < 0.42, first, rng.random((8, W))
def pack(F, U, M, A, H, hold):
    return {"ft": by_rank(F).astype(np.int32), "ut": by_rank(U).astype(np.float32).astype(BF), "mon": by_rank(M).astype(np.float32).astype(BF), "al": by_rank(A).astype(np.float32),
            "hn": by_rank(H).astype(np.int32), "hb": np.ascontiguousarray(hold.reshape(8, N, B).transpose(1, 0, 2)).astype(np.int32)}
def chain(n, k):
    c = np.float32(1.0)
    for i in range(n): c = c * np.float32(0.9375)
    return c if k == 0 else np.nextafter(c, np.float32(0.0 if k < 0 else 2.0))
def pair(rng, i):
    u = 2 ** int(rng.integers(0, 4)); c = (0.6 + 0.39 * rng.random(4096)).astype(np.float32); w = c.astype(np.float64)
    if i == 0:
        ux, uy = ((15, 13), (9, 15), (13, 11), (11, 9))[int(rng.integers(0, 4))]; lo, hi = 0.5 * max(ux, uy) + 0.01, min(ux, uy) - 0.01
        p = lo + (hi - lo) * rng.random(4096); a = (p * float(ux) ** -1.0).astype(np.float32); b = (p * float(uy) ** -1.0).astype(np.float32)
        k = np.flatnonzero((np.float32(ux) * a == np.float32(uy) * b) & (ux * a.astype(np.float64) < uy * b.astype(np.float64)))[:16]
        return ux, uy, a[k], b[k], False
    if i == 1:
        r = c * np.float32(0.9375); k = np.flatnonzero(r.astype(np.float64) > w * 0.9375)[:16]
        return u, u, c[k], r[k], True
    if i == 2:
        r = c * np.float32(0.9375) * np.float32(0.9375); k = np.flatnonzero(r > (w * 0.87890625).astype(np.float32))[:16]
        return u, u, c[k], r[k], True
    if i == 3:
        a = (rng.integers(2 ** 21, 2 ** 22, 16) * 2.0 ** -24).astype(np.float32)
        return u, u, a, np.nextafter(a, np.float32(1.0)), False
    if i == 4:
        j = rng.integers(3100000, 5500000, 16); a = (j * 2.0 ** -24).astype(np.float32); low = rng.permutation(16) >= int(rng.integers(8, 16))
        return 15, 5, np.where(low, a * np.float32(0.75), a), (3 * j * 2.0 ** -24).astype(np.float32), False
    a = c[:16].copy(); k = int(rng.integers(0, 16)); a[k] = np.nextafter(a[k], np.float32(0.0))
    return u, u, a, c[:16].copy(), False
def setup_inputs(rng):
    F, U, A, M, room, stay, first, old = parts(rng)
    H, hold = lodge(rng, room, stay, first, old)
    return pack(F, U, M, A, H, hold)
def setup_inputs_spread(rng):
    F, U, A, M, room, stay, first, old = parts(rng)
    A = np.clip(np.exp2(-1.5 * (rng.random((8, W, 1)) + rng.random((8, W, 16)))), 0.125, 1.0); M = money(rng, -1, 3)
    F = np.minimum((W * rng.random(F.shape) ** 3).astype(np.int64), W - 1); F[1::2] = W - 1 - F[1::2]
    U = np.minimum(np.exp2(4 * rng.random(U.shape)).astype(np.int64), 15)
    first = np.tile(np.arange(W) * (8.0 / W), (8, 1)); first[1::2] = first[1::2, ::-1]
    H, hold = lodge(rng, room, stay, first, old)
    return pack(F, U, M, A, H, hold)
def setup_inputs_ends(rng):
    F, U, A, M, room, stay, first, old = parts(rng)
    e = rng.random((8, N, B)) < 0.72; e[:, :, B - 1] = True
    F = np.where(e.reshape(8, NB, 1), (W - 1) * rng.integers(0, 2, F.shape), rng.integers(0, W, F.shape))
    U = 1 + 14 * rng.integers(0, 2, U.shape); A = np.where(rng.random(A.shape) < 0.5, 0.125, 1.0)
    A[::2, 0] = 1.0; A[::2, W - 1] = 1.0
    for i in range(16): A[:, W - 2 - i] = 0.125; A[:, W - 2 - i, i] = 1.0
    b = np.arange(7, NB, 32); F[:, b] = W - 2 - np.argsort(rng.random((8, len(b), 16)), axis=-1); U[:, b] = 15
    M = np.where(rng.random(M.shape) < 0.5, 0.25, 4.0)
    stay = rng.random((8, NB)) < 0.36; room[:, 0] = False; room[:, 0, :N] = True; fixed = []
    for g in range(8):
        z = (g % N) * V + V - 1; room[g, z] = False; room[g, z, 15] = True
        if g % 4 == 0: room[g, 0, N] = True; fixed.append((g, 0, N, NB - 1, 1))
        else: fixed.append((g, z, 15, NB - 1, -1))
        for q in range(N): fixed.append((g, 0, q, q * B, 1 if g % 4 == 0 else 1 - 2 * int(rng.integers(0, 2))))
    H, hold = lodge(rng, room, stay, first, old, fixed)
    return pack(F, U, M, A, H, hold)
def setup_inputs_corners(rng):
    F, U, A, M, room, stay, first, old = parts(rng)
    n = rng.choice(np.array([0, 1, 1, 2, 8, 15, 16]), (8, W, 1)); kind = rng.integers(0, 3, (8, W, 1)); i = np.arange(16)
    room = np.where(kind == 0, i < n, np.where(kind == 1, i >= 16 - n, np.argsort(rng.random((8, W, 16)), axis=-1) < n))
    first = 2.0 * n[:, :, 0]; old = rng.choice(np.array([0.0, 0.5, 1.0]), (8, W)); stay = np.ones((8, NB), bool)
    F = np.where(rng.random(F.shape) < 0.1, V * rng.integers(0, N, F.shape) + (V - 1) * rng.integers(0, 2, F.shape), F)
    sh = int(rng.integers(0, 8)); counts = [0, 1, 2, 3, L - 1, L, L + 1, B]
    for g in range(8):
        for q in range(N):
            hm = np.sort(rng.permutation(B)[:counts[(g + q + sh) % 8]]); stay[g, q * B + hm] = False
            lane = hm[:L]; o = (q + 1 + rng.permutation(N - 1)) % N; rest = np.append(o[3:], q)
            to = np.concatenate([np.repeat(o[0], CAP), np.repeat(o[1], CAP + 1), np.repeat(o[2], CAP - 1), rng.choice(rest, L - 3 * CAP)])
            to = rng.permutation(to[:len(lane)])
            v = rng.integers(0, V, (len(lane), 16))
            if g % 2: v = rng.integers(0, 24, v.shape) + (V - 24) * rng.integers(0, 2, v.shape)
            F[g, q * B + lane] = V * to[:, None] + v
    z = rng.random(M.shape)
    M = np.where(z < 0.5, 4.0, np.where(z < 0.7, 0.25, M))
    H, hold = lodge(rng, room, stay, first, old)
    return pack(F, U, M, A, H, hold)
def setup_inputs_crowd(rng):
    F, U, A, M, room, stay, first, old = parts(rng)
    for g, x, y, c in ((0, W - 1, 0, chain(RO - 1, -1)), (1, 0, W - 1, chain(RO - 1, 0)), (2, V, V - 1, chain(RO - 1, 1)), (3, W - 1, V // 2, chain(1, 0))):
        stay[g] = False; F[g] = x; F[g, :, 0] = y; U[g] = 15; A[g, x] = 1.0; A[g, y] = c; room[g, x] = False; room[g, y] = False
        if g == 3: room[g, x, 15] = True
        if g >= 2:
            for q in range(N):
                b = q * B + np.arange(int(rng.integers(0, L)), B, L); F[g, b] = rng.integers(0, W, (len(b), 16)); U[g, b] = rng.integers(1, 16, (len(b), 16))
    few = rng.permutation(W)[:4]; F[4] = few[rng.integers(0, 4, F[4].shape)]; first[4, few] = -1.0
    one = V * np.arange(N) + rng.integers(0, V, N); F[5] = one[rng.integers(0, N, F[5].shape)]; first[5, one] = -1.0
    owner = int(rng.integers(0, N)); home = (owner + 1 + int(rng.integers(0, N - 1))) % N
    pv = owner * V + rng.permutation(V); xs, rest = pv[:N * CAP], pv[N * CAP:]; sl = rng.integers(0, 16, N * CAP); held = home * B + CAP + rng.permutation(B - CAP)[:N * CAP]
    bs = (B * np.arange(N)[:, None] + np.arange(CAP)).reshape(-1)
    for g in (6, 7): stay[g, bs] = False; F[g, bs] = xs[:, None]; room[g, xs] = False
    room[7, rest[:N]] = False
    for q in range(N):
        b = q * B + np.arange(CAP, L); stay[7, b] = False
        F[7, b] = np.append(rng.permutation(np.delete(rest, q))[:L - CAP - 1], rest[q])[:, None]
    room[6, xs, sl] = True; fixed = [(6, int(xs[i]), int(sl[i]), int(held[i]), -1) for i in range(N * CAP)]
    H, hold = lodge(rng, room, stay, first, old, fixed)
    return pack(F, U, M, A, H, hold)
def setup_inputs_calm(rng):
    F, U, A, M, room, stay, first, old = parts(rng); ce = -(-L // N)
    for g in range(4):
        po = [o * V + rng.permutation(V) for o in range(N)]
        for o in range(N):
            sp = po[o][:N * ce]; room[g, sp] = False; room[g, sp, rng.integers(0, 16, len(sp))] = True; first[g, sp] = 50.0
        for q in range(N):
            hm = np.sort(rng.permutation(B)[:L + (g + q) % 4]); stay[g, q * B:(q + 1) * B] = True; stay[g, q * B + hm] = False
            for j in range(L): F[g, q * B + hm[j]] = po[(j + q) % N][q * ce + j // N]
            for r in range(len(hm) - L):
                x, y = po[(q + 1) % N][N * ce + 2 * r], po[(q + 1) % N][N * ce + 2 * r + 1]; b = q * B + hm[L + r]
                room[g, x] = False; room[g, y] = False; F[g, b] = x; F[g, b, 0] = y; U[g, b] = 15
                A[g, x] = 1.0; A[g, y] = chain(1 + (r + q + g) % (RO - 2), int(rng.integers(-1, 2)))
    lo = np.resize(np.array([0, 2, L, 1, 3, L - 1]), N); hi = np.resize(np.array([1, 3, 0, 2, B - L, B - L - 1]), N); S = 8 * (B // L + 1)
    for g in (4, 5):
        pv = np.argsort(rng.random((N, V)), axis=1); turn = rng.permutation(N); stay[g] = True
        for q in range(N):
            n, m = (int(lo[turn[q]]), B - L) if g == 4 else (L, int(hi[turn[q]]))
            b = np.concatenate([rng.permutation(L)[:n], L + rng.permutation(B - L)[:m]]); o = b % N; i = (b + 4) % L
            x = o * V + pv[o, np.where(i < 8, 1 + S * q + 8 * ((b + 4) // L) + i, 0)]
            stay[g, q * B + b] = False; F[g, q * B + b] = x[:, None]; room[g, x] = False
    home = int(rng.integers(0, N)); pv = np.argsort(rng.random((N, V)), axis=1); i = np.arange(B)
    goods = (i % N) * V + pv[i % N, i // N]; held = home * B + rng.permutation(B); sl = rng.integers(0, 16, B)
    stay[6, home * B:(home + 1) * B] = False; room[6, goods] = False; room[6, goods, sl] = True
    fixed = [(6, int(goods[j]), int(sl[j]), int(held[j]), -1) for j in range(B)]
    for j in range(N - 1):
        q = (home + 1 + j) % N; w = goods[j * L:(j + 1) * L]
        stay[6, q * B:q * B + L] = False; F[6, q * B + np.arange(len(w))] = w[:, None]
    xy = rng.permutation(W)[:N * 48].reshape(N, 24, 2); stay[7] = True; room[7, xy.reshape(-1)] = False; first[7, xy.reshape(-1)] = 50.0
    for q in range(N):
        hm = q * B + rng.permutation(B)[:24]; stay[7, hm] = False
        for j in range(24):
            x, y = int(xy[q, j, 0]), int(xy[q, j, 1]); b = int(hm[j]); ux, uy, ax, ay, shut = pair(rng, j % 6)
            F[7, b] = y; F[7, b, 0] = x; U[7, b] = uy; U[7, b, 0] = ux; A[7, x] = ax; A[7, y] = ay
            room[7, y, int(rng.integers(0, 16))] = True
            if not shut: room[7, x, int(rng.integers(0, 16))] = True
    H, hold = lodge(rng, room, stay, first, old, fixed)
    return pack(F, U, M, A, H, hold)
def check_ranges(d):
    bad = []
    for k, lo, hi in (("ft", 0, W - 1), ("ut", 1, 15), ("mon", 0.25, 4.0), ("al", 0.125, 1.0), ("hn", -NB, NB + 1), ("hb", 0, W)):
        v = np.asarray(d[k]).astype(np.float64)
        if not np.all((v >= lo) & (v <= hi)): bad.append("range of " + k)
    u = np.asarray(d["ut"]).astype(np.float64)
    if not np.all(u == np.rint(u)): bad.append("ut isn't whole")
    if not bad:
        H = np.abs(by_good(np.asarray(d["hn"])).astype(np.int64)); hb = np.asarray(d["hb"]).astype(np.int64).transpose(1, 0, 2).reshape(8, NB)
        for g in range(8):
            held = (H[g] > 0) & (H[g] <= NB); names = H[g][held] - 1; hold = np.full(NB, W, np.int64); hold[names] = np.nonzero(held)[0]
            if np.any(np.bincount(names, minlength=NB) > 1) or np.any(hold != hb[g]): bad.append("hn and hb of market %d" % g)
    return bad
def reference(ft, ut, mon, al, hn, hb):
    F = by_good(ft).astype(np.int64); U = by_good(ut).astype(np.float32); M = by_good(mon).astype(np.float64)
    A = by_good(al).astype(np.float32); H = by_good(hn).astype(np.int64)
    hold = np.ascontiguousarray(hb.transpose(1, 0, 2)).astype(np.int64).reshape(8, NB)
    for t in range(RO):
        order = (np.arange(B) + t * L) % B
        for g in range(8):
            goods, who, best = [], [], []
            for q in range(N):
                o = q * B + order; o = o[hold[g, o] == W][:L]; j = np.arange(len(o))
                fk = F[g, o]; e = U[g, o][:, :, None] * A[g][fk]
                top = e == np.max(e, axis=1, keepdims=True)
                k = np.argmax(np.add.reduce(top.astype(np.int64), axis=2), axis=1)
                x = fk[j, k]; to = ((x // V)[:, None] == np.arange(N)).astype(np.int64)
                ok = np.add.reduce(to * (np.add.accumulate(to, axis=0) - to), axis=1) < CAP
                goods.append(x[ok]); who.append(o[ok]); best.append(top[j, k][ok])
            x, at = np.unique(np.concatenate(goods), return_index=True)
            b = np.concatenate(who)[at]; m = np.concatenate(best)[at]; h = H[g, x]
            grade = np.where(h == 0, 0, np.where(h < 0, 16, 32)) + np.arange(16)
            s = np.argmin(grade, axis=1); fits = np.min(grade, axis=1) < 32
            r = np.flatnonzero(fits); out = h[r, s[r]]
            hold[g, -out[out < 0] - 1] = W
            h[r, s[r]] = b[r] + 1; hold[g, b[r]] = x[r]
            r = np.flatnonzero(~fits); h[r] = np.where(h[r] <= NB, -h[r], h[r])
            H[g, x] = h
            A[g, x[r]] = np.where(m[r], A[g, x[r]] * np.float32(0.9375), A[g, x[r]])
    P = np.stack([np.where((hold[g] < W)[:, None], M[g] * A[g][np.minimum(hold[g], W - 1)].astype(np.float64), 0.0) for g in range(8)])
    return {"yal": by_rank(A), "yh": by_rank(H).astype(np.float32), "yp": by_rank(P).astype(np.float32)}

def check_inputs(d):
    bad = list(check_ranges(d))
    if not bad:
        for name, y in reference(**d).items():
            for q in range(N):
                v = np.abs(np.asarray(y[q], np.float64)); s = np.sqrt(np.mean(v * v))
                if v.max() > 9 * s or s < 2.0 ** -3: bad.append('%s of rank %d is uneven or too small' % (name, q))
    return bad

@@ -1,0 +1,554 @@
+import math
+from concourse.bass import DstId, RemoteDMATransfer
+from concourse.mybir import AluOpType, ActivationFunctionType
+
+Op, AF = AluOpType, ActivationFunctionType
+N, V, B, L, CAP, RO = 5, 816, 1024, 256, 64, 5
+VS = V + CAP
+ZC = N * VS
+AW = ZC + 16
+AD = AW
+S = N * CAP
+TW = 768 + 1056
+UW = 16 * 360
+TAG = 8192
+NPC = 4
+PW = V // NPC
+CHUNKS = ((0, 32, 0), (32, 32, 512), (64, 32, 1024), (96, 32, 1536), (128, 64, 0), (192, 64, 1024))
+
+f32, bf, f16, i32, u16 = "float32", "bfloat16", "float16", "int32", "uint16"
+
+
+def _sb(shape, d):
+    return ("sbuf", [128] + list(shape), d)
+
+
+SCRATCH = {
+    "A": _sb([AD + N * N * CAP], f32), "H": _sb([VS + S], f32), "U": _sb([UW], i32),
+    "W": _sb([2064], f32), "F": _sb([2064], bf), "IOTA": _sb([TW], f32),
+    "TX": _sb([TW], f32), "TU": _sb([TW], bf), "xg": _sb([256], f32), "acc2": _sb([20], f32),
+    "TOW": _sb([TW], bf), "monb": _sb([B], bf),
+    "G": _sb([2048], f32), "E": _sb([4096], f32), "MX": _sb([2048], f32), "TOP": _sb([4096], bf), "E3": _sb([20, S], bf), "TRIM": _sb([S], bf),
+    "RST": _sb([B], bf), "DM": _sb([B], bf),
+    "SEL": _sb([16, 128], bf), "SELH": _sb([16, 128], f16), "BRD": _sb([16, 128], bf), "MAT": _sb([10, 128], bf),
+    "cI": _sb([8], i32), "cF": _sb([8], f32), "cB": _sb([8], bf), "EQ": _sb([32], f32), "J16": _sb([16], f32),
+    "JB": _sb([16], f32), "I256": _sb([256], bf), "C16": _sb([B], bf), "DEF": _sb([S], f32),
+    "DMP": _sb([6, 20], f32), "RS64": _sb([384], bf), "cs": _sb([384], bf),
+    "ST": _sb([64], i32), "Y": _sb([64], i32), "X2": _sb([128], i32), "X1": _sb([64], i32), "sa": _sb([64], i32),
+    "hl": _sb([64], bf), "inc": _sb([64], bf), "P": _sb([72], f32), "junk": _sb([1024], bf), "acc": _sb([16], f32),
+    "cL": _sb([16], u16), "c16": _sb([16], bf), "cmp": _sb([256], bf), "bL": _sb([16], u16),
+    "FO": _sb([256], u16), "ug": _sb([256], bf), "dg": _sb([3, 256], bf), "ow": _sb([256], bf),
+    "b8": _sb([256], f32), "w": _sb([256], bf), "Z2": _sb([1024], bf), "x16": _sb([S], u16),
+    "ind": _sb([256], bf), "q1": _sb([256], f16),
+    "pay": _sb([256], f32), "slot": _sb([16], u16),
+    "pa": _sb([20], i32), "pb": _sb([20], i32), "pc": _sb([N, 20], i32), "tkf": _sb([16], f32), "tk": _sb([16], u16),
+    "fc": _sb([256], bf),
+    "LM": _sb([RO, N, 20], i32), "FL": _sb([RO, N, S], bf), "LU": _sb([RO, 256], i32), "OA": _sb([RO, N, 24], u16),
+    "UX": _sb([RO, 360], i32), "XA": _sb([N, 20], u16), "sgn": _sb([S], bf),
+    "XO": _sb([20], u16), "XOf": _sb([20], f32), "NO": _sb([20], u16), "xd": _sb([2, 20], f32), "Hc": _sb([S], f32), "EO": _sb([2, S], bf),
+    "Z": _sb([3 * S], bf), "yhi": _sb([S], bf), "ylo": _sb([S], bf), "s60": _sb([80], f32),
+    "ev": _sb([20], f32), "gg": _sb([40], f32), "cc": _sb([40], f32), "n2": _sb([40], f32), "n3": _sb([40], f32),
+    "hI": _sb([40], i32), "h2": _sb([40], f32), "n4": _sb([40], f32), "n5": _sb([40], f32), "uL": _sb([40], u16),
+    "VAL": _sb([2 * S], f32), "g2": _sb([2, 20], f32), "o2": _sb([2, 20], f32), "o3": _sb([2, 20], f32),
+    "hL": _sb([20], u16), "nm": _sb([S], f32), "u2": _sb([S], f32), "u3": _sb([S], f32),
+    "hold": _sb([64], u16),
+    "PU0": ("psum", [128, 1024], f32), "PU1": ("psum", [128, 1024], f32),
+    "PA": ("psum", [128, 512], f32), "PB": ("psum", [128, 512], f32), "PC": ("psum", [128, 512], f32),
+    "PD": ("psum", [128, 512], f32),
+}
+SEMAPHORES = (["sv", "sa", "sp", "sg", "sent", "feed", "ag", "dal", "dft", "dut", "dhb", "dhn", "dmon", "dz", "dout", "dc", "dyh"]
+              + ["%s%d" % (k, t) for k in ("ea", "eb", "eu", "eo", "dx") for t in range(RO)])
+PSUM = ("U0", "U1", "U2", "U3", "PA", "PB", "PC", "PD")
+
+
+def _senders(core, topo):
+    out, seen = [core], {topo.addr(core)[2]}
+    for c in topo.cores_of(core):
+        if topo.addr(c)[2] not in seen:
+            seen.add(topo.addr(c)[2])
+            out.append(c)
+    return out[:NPC]
+
+
+def _mask(engs):
+    m = 0
+    for e in engs:
+        m |= 1 << e
+    return m
+
+
+def _spread(g, T, topo, core, dsts, srcs, outs, sem):
+    eng = topo.engines(core, dsts[0])
+    k = len(eng) // 4
+    tr = []
+    for i, d in enumerate(dsts):
+        rid, pid, _ = topo.addr(d)
+        tr.append(RemoteDMATransfer(dst_ids=[DstId(rid=rid, pnc=pid)], dma_engine_mask=_mask(eng[len(eng) - k * (i + 1):len(eng) - k * i]),
+                                    remote_sem=sem, src=srcs[i], dst=outs[i]))
+    g.remote_dma_fused(tr, local_sem=T.sem["sent"])
+    return k
+
+
+def helper_program(g, core, T, topo, q, piece):
+    peers = [T.cores[(q + 1 + i) % N] for i in range(N - 1)]
+    g.wait_ge(T.sem["feed"], len(topo.engines(T.cores[q], core)) // 4)
+    ap = T.A[:, q * VS + piece * PW:q * VS + (piece + 1) * PW]
+    k = _spread(g, T, topo, core, peers, [ap] * 4, [ap] * 4, T.sem["ag"])
+    g.wait_ge(T.sem["sent"], 4 * k)
+
+
+def rank_program(g, core, T, topo):
+    me = T.rank_of(core)
+    if me is None:
+        for q in range(N):
+            s = _senders(T.cores[q], topo)
+            if core in s:
+                helper_program(g, core, T, topo, q, s.index(core))
+        return
+    peers_r = [(me + 1 + i) % N for i in range(N - 1)]
+    peers = [T.cores[r] for r in peers_r]
+    KE = len(topo.engines(core, peers[0])) // 4
+    Q = {"v": g.vector, "a": g.scalar, "p": g.tensor, "g": g, "s": g.sync}
+    cnt = {"v": 0, "a": 0, "p": 0, "g": 0}
+    seen = {k: {} for k in Q}
+    wr, rd, total = {}, {}, {}
+
+    def need(e, dep):
+        sem, val, src = dep
+        if src == "p" and e == "p":
+            return
+        if seen[e].get(sem, 0) < val:
+            Q[e].wait_ge(T.sem[sem], val)
+            seen[e][sem] = val
+
+    def deps(e, R, Wr):
+        ds = []
+        for k in R:
+            ds += wr.get(k, [])
+            if k in PSUM:
+                ds += [d for d in rd.get(k, []) if d[2] != e]
+        for k in Wr:
+            ds += wr.get(k, []) + rd.get(k, [])
+        best = {}
+        for d in ds:
+            if d[0] not in best or best[d[0]][1] < d[1]:
+                best[d[0]] = d
+        for d in best.values():
+            need(e, d)
+
+    def note(me_dep, R, Wr):
+        for k in R:
+            rd.setdefault(k, []).append(me_dep)
+        for k in Wr:
+            wr[k] = [me_dep]
+            rd[k] = []
+
+    def op(e, fn, R, Wr, inc=True):
+        deps(e, R, Wr)
+        ins = fn()
+        if inc:
+            cnt[e] += 1
+            ins.then_inc(T.sem["s" + e], 1)
+            note(("s" + e, cnt[e], e), R, Wr)
+        else:
+            note(("s" + e, cnt[e] + 1, e), R, Wr)
+
+    def dma(e, out, in_, sem, R, Wr, final=None):
+        deps(e, R, Wr)
+        Q[e].dma_start(out, in_).then_inc(T.sem[sem], 16)
+        total[sem] = total.get(sem, 0) + 16
+        note((sem, final or total[sem], "dma"), R, Wr)
+
+    def send(dsts, srcs, outs, sem, R):
+        deps("g", R, [])
+        k = _spread(g, T, topo, core, dsts, srcs, outs, T.sem[sem])
+        total["sent"] = total.get("sent", 0) + k * len(dsts)
+
+    def arrive(key, sem, val):
+        wr.setdefault(key, []).append((sem, val, "net"))
+        total[sem] = val
+
+    v, a, p = g.vector, g.scalar, g.tensor
+
+    def ts(out, in0, s1, o0, R, Wr, s2=None, o1=None):
+        if o1 is None:
+            op("v", lambda: v.tensor_scalar(out, in0, s1, None, o0), R, Wr)
+        else:
+            op("v", lambda: v.tensor_scalar(out, in0, s1, s2, o0, o1), R, Wr)
+
+    def tt(out, in0, in1, o, R, Wr):
+        op("v", lambda: v.tensor_tensor(out, in0, in1, o), R, Wr)
+
+    def cp(out, in_, R, Wr):
+        op("v", lambda: v.tensor_copy(out, in_), R, Wr)
+
+    def ms(out, c, Wr):
+        op("v", lambda: v.memset(out, c), [], Wr)
+
+    def scan(out, d0, d1, init, o0, o1, R, Wr):
+        op("v", lambda: v.tensor_tensor_scan(out, d0, d1, init, o0, o1), R, Wr)
+
+    def act(out, in_, R, Wr, func=AF.Copy, **kw):
+        op("a", lambda: a.activation(out, in_, func, **kw), R, Wr)
+
+    def mm(out, lhsT, rhs, st, sp, R, Wr, inc=None):
+        op("p", lambda: p.matmul(out, lhsT, rhs, st, sp), R, Wr, inc=sp if inc is None else inc)
+
+    def sel16(out, rhs_of, R, Wr, first=True, mat=T.SEL):
+        for r in range(16):
+            mm(out, mat[:, r, :], rhs_of(r), first and r == 0, r == 15, R + ["SEL", "SELH"], Wr)
+
+    def iota(out, pat, base, cm, Wr, small=True):
+        if small:
+            op("g", lambda: g.iota(out, pat, base, cm, allow_small_or_imprecise_dtypes=True), [], Wr)
+        else:
+            op("g", lambda: g.iota(out, pat, base, cm), [], Wr)
+
+    A, H, U, IO = T.A, T.H, T.U, T.IOTA
+    own = slice(me * VS, me * VS + V)
+    REL, BLK, IDN, D2M, NUP, L1, L2, B4, TM2, TMP = [T.MAT[:, i, :] for i in range(10)]
+    rcol, g16, ebias, pw4 = T.cF[:, 0:1], T.cF[:, 1:2], T.cF[:, 2:3], T.cB[:, 0:1]
+    ftI, hbI, hnI, owI = U[:, 0:B], U[:, B:2 * B], U[:, 2 * B:2 * B + V], U[:, 3 * B:4 * B]
+
+    h = V // 2
+    dma("s", A[:, me * VS:me * VS + h], T.al[:, 0:h], "dal", [], ["Aown"], final=32)
+    dma("a", A[:, me * VS + h:me * VS + V], T.al[:, h:V], "dal", [], ["Aown2"], final=32)
+    dma("s", ftI, T.ft[:], "dft", [], ["ftI"])
+    for r in range(16):
+        dma("s" if r % 2 else "a", U[r:128:16, B:2 * B], T.hb[:], "dhb", [], ["hbI%d" % r], final=256)
+    dma("a", T.TU[:, 0:B], T.ut[:], "dut", [], ["TU"], final=32)
+    dma("s", T.TU[:, B:TW], T.ut[:, 0:TW - B], "dut", [], ["TU2"], final=32)
+    dma("s", hnI, T.hn[:], "dhn", [], ["hnI"])
+    dma("s", T.monb[:], T.mon[:], "dmon", [], ["monb"])
+
+    iota(T.cI[:, 0:1], [[0, 1]], 0, 1, ["cI"], small=False)
+    iota(TMP, [[1, 128]], 0, 0, ["TMP"])
+    iota(T.C16[:], [[0, 64], [1, 16]], 0, 0, ["C16"])
+    snd = _senders(core, topo)
+    pc = [A[:, me * VS + i * PW:me * VS + (i + 1) * PW] for i in range(NPC)]
+    send(snd[1:], pc[1:], pc[1:], "feed", ["Aown", "Aown2"])
+    send(peers, [pc[0]] * 4, [pc[0]] * 4, "ag", [])
+    iota(IO[:, 0:B], [[1, B]], 0, 0, ["IO"])
+    iota(IO[:, B:TW], [[1, TW - B]], 0, 0, ["IO2"])
+
+    ts(T.cI[:, 1:2], T.cI[:, 0:1], 15, Op.bitwise_and, ["cI"], ["cI1"])
+    ts(T.cI[:, 2:3], T.cI[:, 0:1], 112, Op.bitwise_and, ["cI"], ["cI2"])
+    cp(T.cF[:, 0:2], T.cI[:, 1:3], ["cI1", "cI2"], ["cF"])
+    ts(ebias, rcol, 136.0, Op.add, ["cF"], ["eb"], -math.log(2.0), Op.mult)
+    ts(T.cF[:, 3:4], rcol, 192.0, Op.add, ["cF"], ["c128"])
+    act(pw4, rcol, ["cF"], ["pw4"], func=AF.Exp, scale=-math.log(4.0))
+    act(T.cF[:, 4:5], pw4, ["pw4"], ["pw4f"])
+    ts(REL, TMP, g16, Op.subtract, ["TMP", "cF"], ["REL"])
+    ts(IDN, REL, rcol, Op.is_equal, ["REL"], ["IDN"])
+    ts(TM2, REL, 0.0, Op.is_ge, ["REL"], ["TM2"])
+    ts(BLK, REL, 16.0, Op.is_lt, ["REL"], ["BLK"])
+    tt(BLK, BLK, TM2, Op.mult, ["TM2", "BLK"], ["BLK"])
+    ts(NUP, REL, rcol, Op.is_lt, ["REL"], ["NUP"], -1.0, Op.mult)
+    tt(NUP, NUP, BLK, Op.mult, ["NUP", "BLK"], ["NUP"])
+    ts(T.EQ[:, 0:16], TMP[:, 0:16], rcol, Op.is_equal, ["TMP", "cF"], ["EQ"])
+    ms(T.RS64[:], 1.0, ["RS64"])
+    ms(T.RS64[:, 0:384:64], 0.0, ["RS64"])
+    ts(T.DM[:], T.C16[:], rcol, Op.is_equal, ["C16", "cF"], ["DM"])
+    act(T.PU1[:], T.DM[:], ["DM"], ["U2", "U3"])
+    for k in range(16):
+        act(T.BRD[:, k, :], BLK, ["BLK", "EQ"], ["BRD"] if k == 15 else [], scale=T.EQ[:, k:k + 1])
+    ts(T.RST[:], T.C16[:], 0.0, Op.is_gt, ["C16"], ["RST"])
+    for r in range(16):
+        ts(T.SEL[:, r, :], REL, float(r), Op.is_equal, ["REL"], ["SEL"] if r == 15 else [])
+    ts(T.TOW[:, 0:B], ftI, 1.0 / V, Op.mult, ["ftI"], ["TOW"], 0.5 / V + 191.5, Op.add)
+    act(T.PU0[:], T.TOW[:, 0:B], ["TOW"], ["U0", "U1"], func=AF.Identity, scale=float(CAP), bias=-192.0 * CAP)
+    t0, t1 = T.G[:, 0:B], T.G[:, B:2 * B]
+    tt(t0, hbI, T.PU1[:], Op.mult, ["hbI%d" % r for r in range(16)] + ["U2", "U3"], ["G0", "G512"])
+    scan(t1, T.RST[:], t0, 0.0, Op.mult, Op.add, ["G0", "RST"], ["G1024", "G1536"])
+    ts(T.inc[:], T.G[:, B + 15:2 * B:16], 1.0 / V, Op.mult, ["G1024"], ["inc"], 0.5 / V + 191.5, Op.add)
+    ts(T.J16[:], TMP[:, 0:16], 16.0, Op.mult, ["TMP", "cF"], ["J16a"], rcol, Op.add)
+    ts(T.sa[:], T.inc[:], -192.0, Op.add, ["inc"], ["sa"], float(CAP), Op.mult)
+    ts(T.JB[:], T.J16[:], 0.5, Op.add, ["J16a"], ["JB"])
+    tt(T.ST[:], T.sa[:], T.G[:, B + 15:2 * B:16], Op.add, ["sa", "G1024"], ["ST"])
+
+    def late_start(part):
+        if part == 0:
+            tt(T.TX[:, 0:B], ftI, T.PU0[:], Op.add, ["U0", "U1", "ftI"], ["TX"])
+            act(T.TX[:, B:TW], T.TX[:, 0:TW - B], ["TX"], ["TX2"])
+        if part == 1:
+            cp(T.I256[:], IO[:, 0:256], ["IO"], ["I256"])
+            ms(A[:, ZC:AW], 0.0, ["Az"])
+            for o in range(N):
+                ms(A[:, o * VS + V:(o + 1) * VS], 1.0, ["As%d" % o])
+        if part == 2:
+            ts(D2M, IDN, 2.0, Op.mult, ["IDN"], ["D2M"])
+            tt(D2M, D2M, BLK, Op.subtract, ["D2M", "BLK"], ["D2M"])
+        if part == 3:
+            act(T.TOW[:, B:TW], T.TOW[:, 0:TW - B], ["TOW"], ["TOW2"])
+        if part == 5:
+            cp(T.SELH[:], T.SEL[:], ["SEL"], ["SELH"])
+        if part == 7:
+            ms(T.F[:, 0:512], 1.0, ["F"])
+            ts(T.TRIM[:], T.C16[:, 0:S], rcol, Op.is_gt, ["C16", "cF"], ["TRIM"])
+        if part == 4:
+            act(T.J16[:], T.J16[:], ["J16a"], ["J16a", "J16"], scale=16.0)
+            act(B4, BLK, ["BLK"], ["B4"], scale=-4.0)
+            act(L1, D2M, ["D2M", "pw4f"], ["L1"], scale=T.cF[:, 4:5])
+            act(L2, L1, ["L1"], ["L2"], scale=2.0 ** -32)
+            base = T.acc2[:]
+            act(base, IO[:, 0:20], ["IO", "cF"], ["DMP0"], func=AF.Identity, scale=16.0, bias=rcol)
+            for i, c in enumerate((N * B - 7.5, N * B + S - 7.5, AD + me * S, VS, N * B + TAG + 1)):
+                act(T.DMP[:, i, :], base, ["DMP0"], [], func=AF.Identity, bias=float(c))
+            for q in range(N):
+                act(T.DMP[:, 5, 4 * q:4 * q + 4], T.acc2[:, 4 * q:4 * q + 4], ["DMP0"], ["DMP"] if q == N - 1 else [], func=AF.Identity,
+                    bias=float(N * B + S - q * B))
+            for o in range(N):
+                act(T.DEF[:, o * CAP:(o + 1) * CAP], IO[:, 0:CAP], ["IO"], ["DEF"] if o == N - 1 else [], func=AF.Identity, bias=float(o * VS + V))
+        if part == 6:
+            ts(T.PU0[:, 0:V], hnI, 5120.5, Op.is_lt, ["hnI"], ["U0", "U1"], 2.0 ** -32, Op.max)
+            tt(H[:, 0:V], hnI, T.PU0[:, 0:V], Op.mult, ["hnI", "U0", "U1"], ["H"])
+            ms(H[:, V:VS + S], 2.0 ** -20, ["Hd"])
+            act(T.MX[:, 0:V], T.PU0[:, 0:V], ["U0", "U1"], ["MX0", "MX512"], func=AF.Identity, scale=-5121.0, bias=5121.0)
+            dma("s", T.yh[:], T.MX[:, 0:V], "dc", ["MX0", "MX512"], ["yh"])
+            ms(T.UX[:, RO - 1, :], 0, ["UX%d" % (RO - 1)])
+            dma("s", U[0:128:18, :], T.UX[:, RO - 1, :], "dz", ["UX%d" % (RO - 1)], ["U", "ftI", "hnI"] + ["hbI%d" % r for r in range(16)])
+
+    def a_scatter(t, o):
+        tt(A[:].indirect(T.OA[:, t, o, 0:20]), T.E[:, S * o:S * o + S], T.E[:, 2048 + S * o:2048 + S * o + S], Op.mult,
+           ["OA%d" % t, "OAo%d" % t, "old%d" % o, "ff%d" % o, "E0", "E1", "E2", "E3", "E4", "E5"], ["A"])
+
+    def new_state(t):
+        tt(T.X2[:], T.LU[:, t, 0:128], T.LU[:, t, 128:256], Op.max, ["LU%d" % t], ["X2"])
+        tt(T.X1[:], T.X2[:, 0:64], T.X2[:, 64:128], Op.max, ["X2"], ["X1"])
+        tt(T.ST[:], T.X1[:], T.Y[:], Op.max, ["X1", "Y"], ["ST"])
+
+    def h_update(part):
+        if part == 0:
+            cp(T.hL[:], T.o3[:, 1, :], ["o3"], ["hL"])
+            tt(T.u3[:], T.PC[:, 0:S], T.nm[:], Op.mult, ["PC", "nm"], ["u3"])
+            tt(T.u2[:], T.PU0[:, 0:S], T.Hc[:], Op.mult, ["U0", "Hc"], ["u2"])
+        else:
+            tt(H[:].indirect(T.hL[:]), T.u2[:], T.u3[:], Op.add, ["hL", "u2", "u3"], ["H"])
+
+    Ar = ["A", "Aown", "Aown2", "Az"] + ["As%d" % o for o in range(N)]
+    Aw = A[:, 0:AW]
+    for t in range(RO):
+        w0 = (L * t) % B
+        c0 = w0 // 16
+        win = slice(w0, w0 + 1056)
+        if t > 0:
+            new_state(t - 1)
+        ts(T.sa[:], T.ST[:], TAG - 1, Op.bitwise_and, ["ST"], ["sa"])
+        ts(T.hl[:, 0:64 - c0], T.sa[:, c0:64], float(ZC), Op.is_ge, ["sa"], ["hl"])
+        if c0:
+            ts(T.hl[:, 64 - c0:64], T.sa[:, 0:c0], float(ZC), Op.is_ge, ["sa"], ["hl2"])
+        scan(T.inc[:], T.hl[:], T.hl[:], 0.0, Op.add, Op.max, ["hl", "hl2"], ["inc"])
+        mm(T.PA[:, 0:64], BLK, T.inc[:], True, True, ["inc", "BLK"], ["PA"])
+        mm(T.PB[:, 0:64], BLK, T.inc[:], True, False, ["inc"], ["PB"])
+        mm(T.PB[:, 0:64], NUP, T.hl[:], False, True, ["hl", "hl2", "NUP"], ["PB"], inc=False)
+        mm(T.PB[:, 64:65], BLK, T.inc[:, 63:64], True, True, ["inc"], ["PB"])
+        mm(T.PD[:, 0:64], BLK, T.inc[:], True, True, ["inc"], ["PD"])
+        for m in range(10):
+            act(T.junk[:, 64 * m:64 * m + 64], T.PA[:, 0:64], ["PA", "JB"], ["acc"] if m in (0, 9) else [], func=AF.Sign, scale=-1.0, bias=T.JB[:, m:m + 1],
+                accum_out=T.acc[:, m:m + 1])
+        cp(T.P[:, 0:65], T.PB[:, 0:65], ["PB"], ["P"])
+        for m in range(10, 16):
+            ts(T.junk[:, 64 * m:64 * m + 64], T.PD[:, 0:64], T.JB[:, m:m + 1], Op.is_lt, ["PD", "JB"], ["junk"] if m in (10, 15) else [])
+        scan(T.cs[:], T.RS64[:], T.junk[:, 640:1024], 0.0, Op.mult, Op.add, ["junk", "RS64"], ["cs"])
+        cp(T.cL[:, 10:16], T.cs[:, 63:384:64], ["cs"], ["cL2"])
+        ts(T.c16[:, 10:16], T.cs[:, 63:384:64], 16.0, Op.mult, ["cs"], ["c162"])
+        if t == 0:
+            late_start(0)
+        ts(T.cL[:, 0:10], T.acc[:, 0:10], 64.0, Op.add, ["acc"], ["cL"], 0.5, Op.mult)
+        ts(T.c16[:, 0:10], T.acc[:, 0:10], 64.0, Op.add, ["acc"], ["c16"], 8.0, Op.mult)
+        tt(T.cmp[:], T.P[:, 0:65].indirect(T.cL[:]), IO[:, 0:256], Op.is_le, ["P", "cL", "cL2", "IO"], ["cmp"])
+        mm(T.PA[:, 0:16], IDN, T.c16[:], True, False, ["c16", "c162", "IDN"], ["PA"])
+        sel16(T.PA[:, 0:16], lambda r: T.cmp[:, r:256:16], ["cmp"], ["PA"], first=False)
+        if t > 0:
+            h_update(0)
+        else:
+            late_start(1)
+        cp(T.bL[:], T.PA[:, 0:16], ["PA"], ["bL"])
+        act(T.ug[:], T.TU[:, win].indirect(T.bL[:]), ["TU", "TU2", "bL"], ["ug"])
+        cp(T.FO[:], T.TX[:, win].indirect(T.bL[:]), ["TX", "TX2", "bL"], ["FO"])
+        ts(T.PD[:, 256:512], T.I256[:], T.P[:, 64:65], Op.is_ge, ["I256", "P"], ["PD"], 197.0, Op.mult)
+        if t == 0:
+            late_start(2)
+            arrive("A", "ag", 4 * NPC * KE)
+        Ek = []
+        for ci, (j0, nj, s0) in enumerate(CHUNKS):
+            n = 16 * nj
+            PU = T.PU0 if s0 < B else T.PU1
+            banks = ["U%d" % (s0 // 512 + i) for i in range(n // 512)]
+            gk = ["G%d" % (s0 + 512 * i) for i in range(n // 512)]
+            mk = ["MX%d" % (s0 + 512 * i) for i in range(n // 512)]
+            act(T.G[:, s0:s0 + n], Aw.indirect(T.FO[:, j0:j0 + nj]), Ar + ["FO"], gk)
+            if ci >= 4:
+                act(T.PB[:, j0 - 128:j0 - 64], T.MX[:, s0 + 15:s0 + B:16], mk, ["PB"])
+            for hb in range(n // 512):
+                u0 = s0 % B + 512 * hb
+                for k in range(16):
+                    mm(PU[:, u0 + k:u0 + 512:16], T.BRD[:, k, :], T.ug[:, j0 + 32 * hb:j0 + 32 * hb + 32], True, True,
+                       ["ug", "BRD"], [banks[hb]], inc=(k == 15))
+            tt(T.E[:, 16 * j0:16 * j0 + n], T.G[:, s0:s0 + n], PU[:, s0 % B:s0 % B + n], Op.mult, gk + banks, ["E%d" % ci])
+            scan(T.MX[:, s0:s0 + n], T.RST[:, 0:n], T.E[:, 16 * j0:16 * j0 + n], 0.0, Op.mult, Op.max, ["E%d" % ci, "RST"], mk)
+            Ek.append("E%d" % ci)
+        if t == 0:
+            late_start(3)
+        act(T.dg[:, 2, :], T.TOW[:, win].indirect(T.bL[:]), ["TOW", "TOW2", "bL"], ["dg2"])
+        act(T.xg[:], T.TX[:, win].indirect(T.bL[:]), ["TX", "TX2", "bL"], ["xg"])
+        act(T.dg[:, 0, :], T.xg[:], ["xg"], ["dg0"])
+        act(T.PC[:, 0:256], T.dg[:, 0, :], ["dg0"], ["PC"])
+        for b0, bn, bs in CHUNKS[-2:]:
+            act(T.PB[:, b0:b0 + bn], T.MX[:, bs + 15:bs + 16 * bn:16], ["MX%d" % bs], ["PB"])
+        if t == 0:
+            late_start(4)
+        act(T.b8[:], IO[:, win].indirect(T.bL[:]), ["IO", "IO2", "bL"], ["b8"], scale=float(TAG))
+        for o in range(N):
+            act(T.W[:, o:512:8], T.DEF[:, CAP * o:CAP * o + CAP], ["DEF"], ["W"] if o in (0, N - 1) else [])
+        act(T.PU1[:, 0:CAP], T.DM[:, 0:CAP], ["DM"], ["U2"])
+        act(T.VAL[:, 0:S], IO[:, 0:S], ["IO"], ["VAL0"], func=AF.Identity, scale=0.0, bias=float(TAG * (t + 1) + ZC))
+        tt(T.ow[:], T.dg[:, 2, :], T.PD[:, 256:512], Op.max, ["dg2", "PD"], ["ow"])
+        for k in range(16):
+            tt(T.TOP[:, k:4096:16], T.E[:, k:4096:16], T.PB[:, 0:256], Op.is_equal, Ek + ["PB"], ["TOP%d" % k])
+            mm(T.PA[:, 0:256], T.SEL[:, k, :], T.TOP[:, k:4096:16], k == 0, k == 15, ["TOP%d" % k], ["PA"])
+        act(T.w[:], T.PA[:, 0:256], ["PA", "eb"], ["w"], func=AF.Exp, scale=16.0 * math.log(2.0), bias=ebias)
+        tt(T.dg[:, 1, :], T.xg[:], T.PC[:, 0:256], Op.subtract, ["xg", "PC"], ["dg1"])
+        if t == 0:
+            late_start(5)
+        mm(T.PC[:, 0:256], D2M, T.w[:], True, True, ["w", "D2M"], ["PC"])
+        oh = T.PC[:, 256:512]
+        ts(oh, T.PC[:, 0:256], 0.0, Op.is_ge, ["PC"], ["PC"])
+        tt(T.Z2[:, 512:768], oh, T.ow[:], Op.mult, ["PC", "ow"], ["Z22"])
+        mm(T.PD[:, 0:256], BLK, T.Z2[:, 512:768], True, True, ["Z22"], ["PD"])
+        tt(T.Z2[:, 0:256], oh, T.dg[:, 0, :], Op.mult, ["PC", "dg0"], ["Z20"])
+        tt(T.Z2[:, 256:512], oh, T.dg[:, 1, :], Op.mult, ["PC", "dg1"], ["Z21"])
+        mm(T.PA[:, 0:256], BLK, T.Z2[:, 0:256], True, False, ["Z20"], ["PA"])
+        mm(T.PA[:, 0:256], BLK, T.Z2[:, 256:512], False, True, ["Z21"], ["PA"])
+        ts(T.ind[:], T.PD[:, 0:256], T.cF[:, 3:4], Op.is_equal, ["PD", "c128"], ["ind"], 8.0, Op.mult)
+        scan(T.PD[:, 256:512], T.ind[:], T.ind[:], rcol, Op.add, Op.max, ["ind"], ["PD"])
+        tt(T.q1[:], T.ind[:], T.PD[:, 256:512], Op.mult, ["ind", "PD"], ["q1"])
+        sel16(T.PB[:, 0:16], lambda r: T.q1[:, r:256:16], ["q1"], ["PB"], mat=T.SELH)
+        tt(T.pay[:], T.PA[:, 0:256], T.b8[:], Op.add, ["PA", "b8"], ["pay"])
+        ts(T.Z2[:, 768:1024], oh, rcol, Op.mult, ["PC"], ["Z23"])
+        sel16(T.PD[:, 256:272], lambda r: T.Z2[:, 768 + r:1024:16], ["Z23"], ["PD"])
+        if t == 0:
+            late_start(7)
+        act(T.PU1[:, 512:512 + S], T.TRIM[:], ["TRIM"], ["U3"])
+        ts(T.slot[:], T.PB[:, 0:16], 0.125, Op.mult, ["PB"], ["slot"], -8.0, Op.add)
+        cp(T.W[:].indirect(T.slot[:]), T.pay[:], ["slot", "pay"], ["W"])
+        for o in range(N):
+            tt(T.G[:, CAP * o:CAP * o + CAP], T.W[:, o:512:8], T.PU1[:, 0:CAP], Op.mult, ["W", "U2"], ["G0"] if o in (0, N - 1) else [])
+        scan(T.G[:, 512:512 + S], T.RST[:, 0:S], T.G[:, 0:S], 0.0, Op.mult, Op.add, ["G0"], ["G512"])
+        lm = T.LM[:, t, me, :]
+        cp(lm, T.G[:, 512 + 15:512 + S:16], ["G512"], ["LMo%d" % t])
+        send(peers, [lm] * 4, [lm] * 4, "ea%d" % t, ["LMo%d" % t])
+        arrive("LM%d" % t, "ea%d" % t, 4 * KE)
+        tt(T.tkf[:], T.PD[:, 256:272], T.J16[:], Op.add, ["PD", "J16"], ["tkf"])
+        cp(T.tk[:], T.tkf[:], ["tkf"], ["tk"])
+        act(T.fc[:], T.TOP[:].indirect(T.tk[:]), ["tk"] + ["TOP%d" % k for k in range(16)], ["fc"], func=AF.Identity, scale=-0.0625, bias=1.0)
+        if t > 0:
+            h_update(1)
+        cp(T.F[:].indirect(T.slot[:]), T.fc[:], ["slot", "fc"], ["F"])
+        for o in range(N):
+            act(T.FL[:, t, me, CAP * o:CAP * o + CAP], T.F[:, o:512:8], ["F"], ["FLo%d" % t] if o == N - 1 else [])
+        fl = T.FL[:, t, me, :]
+        send(peers, [fl] * 4, [fl] * 4, "eb%d" % t, ["FLo%d" % t])
+        arrive("FL%d" % t, "eb%d" % t, 4 * KE)
+        if t == 0:
+            late_start(6)
+        lmk = ["LM%d" % t, "LMo%d" % t]
+        mine = T.LM[:, t, :, 4 * me:4 * me + 4]
+        ts(T.pa[:], mine, TAG - 1, Op.bitwise_and, lmk, ["pa"])
+        ts(T.XO[:], T.pa[:], float(-me * VS), Op.add, ["pa"], ["XO"])
+        ts(T.XOf[:], T.pa[:], float(-me * VS), Op.add, ["pa"], ["XOf"])
+        act(T.Hc[:], H[:].indirect(T.XO[:]), ["H", "Hd", "XO"], ["Hc"])
+        cp(T.x16[:], IO[:, 0:B].indirect(T.XO[:]), ["IO", "XO"], ["x16"])
+        act(T.yhi[:], T.Hc[:], ["Hc"], ["yhi"], func=AF.Identity, scale=-1.0, bias=float(TAG))
+        act(T.PU0[:, 512:512 + S], T.Hc[:], ["Hc"], ["U1"], func=AF.Identity, scale=-1.0, bias=float(TAG))
+        act(T.VAL[:, S:2 * S], IO[:, 0:B].indirect(T.XO[:]), ["IO", "XO"], ["VAL1"], func=AF.Identity, bias=float(TAG * (t + 1) + me * VS))
+        D = T.PA[:, 0:S]
+
+        def pair(m):
+            ts(T.E3[:, m, 0:S - 16 * m], T.x16[:, 16 * m:S], T.XOf[:, m:m + 1], Op.is_equal, ["x16", "XOf"], ["E3%d" % m])
+
+        pair(0)
+        ts(T.EO[:, 0, :], T.Hc[:], 0.0, Op.is_equal, ["Hc"], ["EO0"])
+        mm(D, L1, T.EO[:, 0, :], True, False, ["EO0", "L1"], ["PA"])
+        for m in range(20):
+            if m == 8:
+                ts(T.EO[:, 1, :], T.Hc[:], -0.5, Op.is_lt, ["Hc"], ["EO1"])
+                mm(D, L2, T.EO[:, 1, :], False, False, ["EO1", "L2"], ["PA"])
+            if m:
+                pair(m)
+            if m < 19:
+                mm(T.PA[:, 16 * m + 16:S], B4, T.E3[:, m, 16:S - 16 * m], False, False, ["E3%d" % m, "B4"], ["PA"])
+        tt(T.sgn[:], T.E3[:, :, 0:16], T.PU1[:, 512:512 + S], Op.mult, ["E319", "U3"], ["sgn"])
+        mm(D, B4, T.sgn[:], False, True, ["sgn"], ["PA"])
+        tt(T.ylo[:], T.PU0[:, 512:512 + S], T.yhi[:], Op.subtract, ["U1", "yhi"], ["ylo"])
+        ts(T.pb[:], mine, 13, Op.logical_shift_right, lmk, ["pb"])
+        ts(T.pc[:], T.LM[:, t, :, :], TAG - 1, Op.bitwise_and, lmk, ["pc"])
+        tt(T.cc[:, 20:40], T.pb[:], T.DMP[:, 5, :], Op.subtract, ["pb", "DMP"], ["cc1"])
+        ts(T.PC[:, 0:S], D, 0.0, Op.is_gt, ["PA"], ["PC"])
+        ts(T.Z[:, 2 * S:3 * S], D, 0.0, Op.is_equal, ["PA"], ["Z0"])
+        tt(T.Z[:, 0:S], T.PC[:, 0:S], T.yhi[:], Op.mult, ["PC", "yhi"], ["Z1"])
+        tt(T.Z[:, S:2 * S], T.PC[:, 0:S], T.ylo[:], Op.mult, ["PC", "ylo"], ["Z2"])
+        sel16(T.PD[:, 0:60], lambda r: T.Z[:, r:3 * S:16], ["Z0", "Z1", "Z2"], ["PD"])
+        for o in range(N):
+            cp(T.XA[:, o, :], T.pc[:, :, 4 * o:4 * o + 4], ["pc"], ["XA"] if o in (0, N - 1) else [])
+        cp(T.NO[:], T.pb[:], ["pb"], ["NO"])
+        tt(T.xd[:, 0, :], T.pa[:], T.DMP[:, 2, :], Op.subtract, ["pa"], ["xd0"])
+        tt(T.xd[:, 1, :], T.XOf[:], T.DMP[:, 3, :], Op.subtract, ["XOf"], ["xd1"])
+        for o in range(N):
+            act(T.E[:, 2048 + S * o:2048 + S * o + S], T.FL[:, t, :, CAP * o:CAP * o + CAP], ["FL%d" % t, "FLo%d" % t],
+                ["ff%d" % o] + (Ek if o == 0 else []))
+        for q in range(N):
+            act(T.E[:, S * q:S * q + S], Aw.indirect(T.XA[:, q, :]), Ar + ["XA"], ["old%d" % q])
+        act(T.sgn[:], D, ["PA"], ["sgn"], func=AF.Sign)
+        act(T.sgn[:], T.sgn[:], ["sgn"], ["sgn"], func=AF.Abs, scale=-2.0, bias=0.5)
+        act(T.PU0[:, 0:S], T.sgn[:], ["sgn"], ["U0"], func=AF.Identity, bias=-1.5)
+        for q in range(N):
+            act(T.nm[:, CAP * q:CAP * q + CAP], IO[:, 0:B].indirect(T.NO[:, 4 * q:4 * q + 4]), ["IO", "NO"], ["nm"] if q in (0, N - 1) else [],
+                func=AF.Identity, bias=float(q * B + 1))
+        cp(T.s60[:, 0:60], T.PD[:, 0:60], ["PD"], ["s60"])
+        tt(T.ev[:], T.s60[:, 0:20], T.s60[:, 20:40], Op.add, ["s60"], ["ev"])
+        ts(T.gg[:, 0:20], T.ev[:], TAG + 0.5, Op.is_gt, ["ev"], ["gg0"])
+        ts(T.gg[:, 20:40], T.ev[:], 0.5, Op.is_gt, ["ev"], ["gg1"])
+        tt(T.cc[:, 0:20], T.ev[:], T.DMP[:, 4, :], Op.subtract, ["ev"], ["cc0"])
+        tt(T.s60[:, 60:80], T.ev[:], T.s60[:, 40:60], Op.add, ["ev", "s60"], ["s61"])
+        tt(T.n2[:], T.cc[:], T.gg[:], Op.mult, ["cc0", "cc1", "gg0", "gg1"], ["n2"])
+        ts(T.g2[:], T.s60[:, 40:80], 0.5, Op.is_gt, ["s60", "s61"], ["g2"])
+        tt(T.n3[:], T.n2[:], T.DMP[:, 0:2, :], Op.add, ["n2"], ["n3"])
+        tt(T.o2[:], T.g2[:], T.xd[:], Op.mult, ["g2", "xd0", "xd1"], ["o2"])
+        ts(T.hI[:], T.n3[:], 0.0625, Op.mult, ["n3"], ["hI"])
+        tt(T.o3[:], T.o2[:], T.DMP[:, 2:4, :], Op.add, ["o2"], ["o3"])
+        ts(T.n4[:], T.n3[:], 7.5, Op.add, ["n3"], ["n4"], 360.0, Op.mult)
+        oa = T.OA[:, t, me, 0:20]
+        ts(T.h2[:], T.hI[:], -5759.0, Op.mult, ["hI"], ["h2"])
+        cp(oa, T.o3[:, 0, :], ["o3"], ["OAo%d" % t])
+        send(peers, [oa] * 4, [oa] * 4, "eo%d" % t, ["OAo%d" % t])
+        arrive("OA%d" % t, "eo%d" % t, 4 * KE)
+        tt(T.n5[:], T.n4[:], T.h2[:], Op.add, ["n4", "h2"], ["n5"])
+        cp(T.uL[:], T.n5[:], ["n5"], ["uL"])
+        cp(U[:].indirect(T.uL[:]), T.VAL[:], ["uL", "VAL0", "VAL1"], ["U"])
+        dma("s", T.UX[:, t, :], U[0:128:18, :], "dx%d" % t, ["U"], ["UX%d" % t])
+        send(peers, [T.UX[:, t, 64 * r:64 * r + 64] for r in peers_r],
+             [T.LU[:, t, 64 * ((me - r - 1) % N):64 * ((me - r - 1) % N) + 64] for r in peers_r], "eu%d" % t, ["UX%d" % t])
+        arrive("LU%d" % t, "eu%d" % t, 4 * KE)
+        if t == RO - 1:
+            h_update(0)
+            h_update(1)
+            deps("g", ["H", "yh"], [])
+            g.dma_start(T.yh[:], H[:, 0:V], accum_op=Op.add).then_inc(T.sem["dyh"], 16)
+            total["dyh"] = 16
+        for o in range(N):
+            a_scatter(t, o)
+        tt(T.Y[:], T.ST[:], T.UX[:, t, 64 * me:64 * me + 64], Op.max, ["ST", "UX%d" % t], ["Y"])
+
+    dma("s", T.yal[:], A[:, own], "dout", ["A"], [], final=48)
+    new_state(RO - 1)
+    ts(T.sa[:], T.ST[:], TAG - 1, Op.bitwise_and, ["ST"], ["sa"])
+    cp(T.hold[:], T.sa[:], ["sa"], ["hold"])
+    for c in range(2):
+        tt(T.G[:, 512 * c:512 * c + 512], Aw.indirect(T.hold[:, 32 * c:32 * c + 32]), T.monb[:, 512 * c:512 * c + 512], Op.mult,
+           ["A", "hold", "monb"], ["G%d" % (512 * c)])
+        dma("a" if c == 0 else "s", T.yp[:, 512 * c:512 * c + 512], T.G[:, 512 * c:512 * c + 512], "dout", ["G%d" % (512 * c)], [], final=48)
+    for e in cnt:
+        total["s" + e] = cnt[e]
+    for sem, val in total.items():
+        g.wait_ge(T.sem[sem], val)

@@ -4,17 +4,15 @@ from concourse.mybir import AluOpType, ActivationFunctionType
 
 Op, AF = AluOpType, ActivationFunctionType
 N, V, B, L, CAP, RO = 5, 816, 1024, 256, 64, 5
-VS = V + CAP
-ZC = N * VS
-AW = ZC + 16
-AD = AW
-S = N * CAP
-TW = 768 + 1056
-UW = 16 * 360
+W = N * V
+HO = 4096
+DO = 2 * HO
 TAG = 8192
-NPC = 4
-PW = V // NPC
+MID = W // 2
+TW = 768 + 1056
+PW = 168
 CHUNKS = ((0, 32, 0), (32, 32, 512), (64, 32, 1024), (96, 32, 1536), (128, 64, 0), (192, 64, 1024))
+NA = 9
 
 f32, bf, f16, i32, u16 = "float32", "bfloat16", "float16", "int32", "uint16"
 
@@ -24,40 +22,28 @@ def _sb(shape, d):
 
 
 SCRATCH = {
-    "A": _sb([AD + N * N * CAP], f32), "H": _sb([VS + S], f32), "U": _sb([UW], i32),
-    "W": _sb([2064], f32), "F": _sb([2064], bf), "IOTA": _sb([TW], f32),
-    "TX": _sb([TW], f32), "TU": _sb([TW], bf), "xg": _sb([256], f32), "acc2": _sb([20], f32),
-    "TOW": _sb([TW], bf), "monb": _sb([B], bf),
-    "G": _sb([2048], f32), "E": _sb([4096], f32), "MX": _sb([2048], f32), "TOP": _sb([4096], bf), "E3": _sb([20, S], bf), "TRIM": _sb([S], bf),
-    "RST": _sb([B], bf), "DM": _sb([B], bf),
-    "SEL": _sb([16, 128], bf), "SELH": _sb([16, 128], f16), "BRD": _sb([16, 128], bf), "MAT": _sb([10, 128], bf),
-    "cI": _sb([8], i32), "cF": _sb([8], f32), "cB": _sb([8], bf), "EQ": _sb([32], f32), "J16": _sb([16], f32),
-    "JB": _sb([16], f32), "I256": _sb([256], bf), "C16": _sb([B], bf), "DEF": _sb([S], f32),
-    "DMP": _sb([6, 20], f32), "RS64": _sb([384], bf), "cs": _sb([384], bf),
-    "ST": _sb([64], i32), "Y": _sb([64], i32), "X2": _sb([128], i32), "X1": _sb([64], i32), "sa": _sb([64], i32),
-    "hl": _sb([64], bf), "inc": _sb([64], bf), "P": _sb([72], f32), "junk": _sb([1024], bf), "acc": _sb([16], f32),
-    "cL": _sb([16], u16), "c16": _sb([16], bf), "cmp": _sb([256], bf), "bL": _sb([16], u16),
-    "FO": _sb([256], u16), "ug": _sb([256], bf), "dg": _sb([3, 256], bf), "ow": _sb([256], bf),
-    "b8": _sb([256], f32), "w": _sb([256], bf), "Z2": _sb([1024], bf), "x16": _sb([S], u16),
-    "ind": _sb([256], bf), "q1": _sb([256], f16),
-    "pay": _sb([256], f32), "slot": _sb([16], u16),
-    "pa": _sb([20], i32), "pb": _sb([20], i32), "pc": _sb([N, 20], i32), "tkf": _sb([16], f32), "tk": _sb([16], u16),
-    "fc": _sb([256], bf),
-    "LM": _sb([RO, N, 20], i32), "FL": _sb([RO, N, S], bf), "LU": _sb([RO, 256], i32), "OA": _sb([RO, N, 24], u16),
-    "UX": _sb([RO, 360], i32), "XA": _sb([N, 20], u16), "sgn": _sb([S], bf),
-    "XO": _sb([20], u16), "XOf": _sb([20], f32), "NO": _sb([20], u16), "xd": _sb([2, 20], f32), "Hc": _sb([S], f32), "EO": _sb([2, S], bf),
-    "Z": _sb([3 * S], bf), "yhi": _sb([S], bf), "ylo": _sb([S], bf), "s60": _sb([80], f32),
-    "ev": _sb([20], f32), "gg": _sb([40], f32), "cc": _sb([40], f32), "n2": _sb([40], f32), "n3": _sb([40], f32),
-    "hI": _sb([40], i32), "h2": _sb([40], f32), "n4": _sb([40], f32), "n5": _sb([40], f32), "uL": _sb([40], u16),
-    "VAL": _sb([2 * S], f32), "g2": _sb([2, 20], f32), "o2": _sb([2, 20], f32), "o3": _sb([2, 20], f32),
-    "hL": _sb([20], u16), "nm": _sb([S], f32), "u2": _sb([S], f32), "u3": _sb([S], f32),
-    "hold": _sb([64], u16),
+    "C": _sb([DO + L], f32), "PL": _sb([RO, N, L + 16], f32), "OL": _sb([N, 16], u16),
+    "XR": _sb([B + L], f32), "NV": _sb([B + L], f32), "HL": _sb([64], u16), "EQ": _sb([B], bf),
+    "XI": _sb([B], i32), "hnI": _sb([V], i32), "IOTA": _sb([TW], f32), "TX": _sb([TW], i32), "TU": _sb([TW], bf), "monb": _sb([B], bf),
+    "G": _sb([2048], f32), "E": _sb([4096], f32), "MX": _sb([2048], f32), "TOP": _sb([4096], bf), "E3": _sb([16, L], bf),
+    "RST": _sb([B], bf), "ONE": _sb([512], bf), "TRIM": _sb([L], bf), "C16": _sb([L], bf),
+    "TMP": _sb([144], bf), "SEL": _sb([144], bf), "SELH": _sb([144], f16), "SELK": _sb([144], bf), "SELF": _sb([144], f32),
+    "BRD": _sb([16, 128], bf), "MAT": _sb([16, 128], bf), "MATH": _sb([2, 128], f16),
+    "cI": _sb([8], i32), "cF": _sb([12], f32), "cB": _sb([8], bf), "EK": _sb([16], f32), "SG": _sb([2, 8], f32),
+    "JT": _sb([4, 16], f32), "JH": _sb([16], f16),
+    "RS64": _sb([448], bf), "cs": _sb([448], bf), "hz": _sb([64], bf), "hl": _sb([64], bf), "inc": _sb([64], bf), "P": _sb([72], f32),
+    "junk": _sb([1024], bf), "acc": _sb([16], f32), "cL": _sb([16], u16), "c16": _sb([16], bf), "cmp": _sb([L], bf), "bL": _sb([16], u16),
+    "FO": _sb([L], u16), "ug": _sb([L], bf), "xc": _sb([L], f16), "nv": _sb([L], f32), "w": _sb([L], bf), "sg": _sb([L], bf),
+    "Z": _sb([L], f16), "XL": _sb([16], u16), "XLf": _sb([16], f32), "xr": _sb([L], u16), "tk": _sb([16], u16),
+    "SA": _sb([L], bf), "Hc": _sb([L], f32), "EM": _sb([L], bf), "AA": _sb([L], f32), "fc": _sb([L], bf), "own": _sb([L], bf),
+    "ind": _sb([L], bf), "cn": _sb([L], bf), "q1": _sb([L], bf), "AV": _sb([L], bf), "dg": _sb([L], bf), "Rb": _sb([L], bf), "X": _sb([L], f32),
+    "li": _sb([2, 16], i32), "lf": _sb([8, 16], f32), "pos": _sb([16], u16),
     "PU0": ("psum", [128, 1024], f32), "PU1": ("psum", [128, 1024], f32),
     "PA": ("psum", [128, 512], f32), "PB": ("psum", [128, 512], f32), "PC": ("psum", [128, 512], f32),
     "PD": ("psum", [128, 512], f32),
 }
-SEMAPHORES = (["sv", "sa", "sp", "sg", "sent", "feed", "ag", "dal", "dft", "dut", "dhb", "dhn", "dmon", "dz", "dout", "dc", "dyh"]
-              + ["%s%d" % (k, t) for k in ("ea", "eb", "eu", "eo", "dx") for t in range(RO)])
+SEMAPHORES = (["sv", "sa", "sp", "sg", "sent", "feed0", "feed1", "ag0", "ag1", "dal", "dft", "dut", "dhb", "dhn", "dmon", "dout"]
+              + ["ea%d" % t for t in range(RO)])
 PSUM = ("U0", "U1", "U2", "U3", "PA", "PB", "PC", "PD")
 
 
@@ -67,7 +53,12 @@ def _senders(core, topo):
         if topo.addr(c)[2] not in seen:
             seen.add(topo.addr(c)[2])
             out.append(c)
-    return out[:NPC]
+    return out
+
+
+def _piece(T, part, q, i, n):
+    c0 = part * HO + q * V
+    return T.C[:, c0 + (n - 1) * PW:c0 + V] if i == 0 else T.C[:, c0 + (i - 1) * PW:c0 + i * PW]
 
 
 def _mask(engs):
@@ -89,12 +80,14 @@ def _spread(g, T, topo, core, dsts, srcs, outs, sem):
     return k
 
 
-def helper_program(g, core, T, topo, q, piece):
+def helper_program(g, core, T, topo, q, piece, n):
     peers = [T.cores[(q + 1 + i) % N] for i in range(N - 1)]
-    g.wait_ge(T.sem["feed"], len(topo.engines(T.cores[q], core)) // 4)
-    ap = T.A[:, q * VS + piece * PW:q * VS + (piece + 1) * PW]
-    k = _spread(g, T, topo, core, peers, [ap] * 4, [ap] * 4, T.sem["ag"])
-    g.wait_ge(T.sem["sent"], 4 * k)
+    sent = 0
+    for part in range(2):
+        g.wait_ge(T.sem["feed%d" % part], len(topo.engines(T.cores[q], core)) // 4)
+        ap = _piece(T, part, q, piece, n)
+        sent += 4 * _spread(g, T, topo, core, peers, [ap] * 4, [ap] * 4, T.sem["ag%d" % part])
+    g.wait_ge(T.sem["sent"], sent)
 
 
 def rank_program(g, core, T, topo):
@@ -103,10 +96,9 @@ def rank_program(g, core, T, topo):
         for q in range(N):
             s = _senders(T.cores[q], topo)
             if core in s:
-                helper_program(g, core, T, topo, q, s.index(core))
+                helper_program(g, core, T, topo, q, s.index(core), len(s))
         return
-    peers_r = [(me + 1 + i) % N for i in range(N - 1)]
-    peers = [T.cores[r] for r in peers_r]
+    peers = [T.cores[(me + 1 + i) % N] for i in range(N - 1)]
     KE = len(topo.engines(core, peers[0])) // 4
     Q = {"v": g.vector, "a": g.scalar, "p": g.tensor, "g": g, "s": g.sync}
     cnt = {"v": 0, "a": 0, "p": 0, "g": 0}
@@ -196,7 +188,7 @@ def rank_program(g, core, T, topo):
 
     def sel16(out, rhs_of, R, Wr, first=True, mat=T.SEL):
         for r in range(16):
-            mm(out, mat[:, r, :], rhs_of(r), first and r == 0, r == 15, R + ["SEL", "SELH"], Wr)
+            mm(out, mat[:, 16 - r:144 - r], rhs_of(r), first and r == 0, r == 15, R + ["SEL"], Wr)
 
     def iota(out, pat, base, cm, Wr, small=True):
         if small:
@@ -204,172 +196,165 @@ def rank_program(g, core, T, topo):
         else:
             op("g", lambda: g.iota(out, pat, base, cm), [], Wr)
 
-    A, H, U, IO = T.A, T.H, T.U, T.IOTA
-    own = slice(me * VS, me * VS + V)
-    REL, BLK, IDN, D2M, NUP, L1, L2, B4, TM2, TMP = [T.MAT[:, i, :] for i in range(10)]
-    rcol, g16, ebias, pw4 = T.cF[:, 0:1], T.cF[:, 1:2], T.cF[:, 2:3], T.cB[:, 0:1]
-    ftI, hbI, hnI, owI = U[:, 0:B], U[:, B:2 * B], U[:, 2 * B:2 * B + V], U[:, 3 * B:4 * B]
+    C, IO, TMP = T.C, T.IOTA, T.TMP
+    Aw, Hw = C[:, 0:HO], C[:, HO:DO]
+    REL, BLK, IDN, D2M, NUP, NL1, NL2, B4K, B9, BN24, BN8, B05, I8K, BNC, TM2 = [T.MAT[:, i, :] for i in range(15)]
+    BLKH, IDNH = T.MATH[:, 0, :], T.MATH[:, 1, :]
+    rcol, g16, ebias, c192, pw4f, r0, rh = [T.cF[:, i:i + 1] for i in range(7)]
+    pw4 = T.cB[:, 0:1]
+    J16, JB, DUM, JD = [T.JT[:, i, :] for i in range(4)]
+    invL, xI, fl, xo, lm, la, lb = [T.lf[:, i, :] for i in range(7)]
+    ao, ho = me * V, HO + me * V
+    name0 = me * B + 1
+    Ar, Hr = ["A", "Aown", "Aown2", "Az", "C"], ["H", "Hown", "Hz", "C"]
+
+    def holdings():
+        sel16(T.PC[:, 0:64], lambda r: T.XR[:, r:B:16], ["XR", "SELF"], ["PC"], mat=T.SELF)
+        cp(T.HL[:], T.PC[:, 0:64], ["PC"], ["HL"])
+
+    def check(w0):
+        h = w0 or B // 2
+        e0 = B - h if w0 else 0
+        tt(T.EQ[:, (h - w0) % B:(h - w0) % B + B - h], Hw.indirect(T.HL[:, h // 16:64]), T.NV[:, h:B], Op.is_equal, Hr + ["HL", "NV"], ["EQ0"])
+        tt(T.EQ[:, e0:e0 + h], Hw.indirect(T.HL[:, 0:h // 16]), T.NV[:, 0:h], Op.is_equal, Hr + ["HL", "NV"], ["EQ1"])
 
     h = V // 2
-    dma("s", A[:, me * VS:me * VS + h], T.al[:, 0:h], "dal", [], ["Aown"], final=32)
-    dma("a", A[:, me * VS + h:me * VS + V], T.al[:, h:V], "dal", [], ["Aown2"], final=32)
-    dma("s", ftI, T.ft[:], "dft", [], ["ftI"])
-    for r in range(16):
-        dma("s" if r % 2 else "a", U[r:128:16, B:2 * B], T.hb[:], "dhb", [], ["hbI%d" % r], final=256)
-    dma("a", T.TU[:, 0:B], T.ut[:], "dut", [], ["TU"], final=32)
+    dma("s", C[:, ao:ao + h], T.al[:, 0:h], "dal", [], ["Aown"], final=32)
+    dma("a", C[:, ao + h:ao + V], T.al[:, h:V], "dal", [], ["Aown2"], final=32)
+    dma("s", T.hnI[:], T.hn[:], "dhn", [], ["hnI"])
+    ms(T.XI[:], 0, ["XI"])
+    dma("s", T.XI[0:128:16, :], T.hb[:], "dhb", [], ["XI"])
+    dma("s", T.TX[:, 0:B], T.ft[:], "dft", [], ["TX"], final=32)
+    dma("s", T.TX[:, B:TW], T.ft[:, 0:TW - B], "dft", [], ["TX2"], final=32)
+    dma("s", T.TU[:, 0:B], T.ut[:], "dut", [], ["TU"], final=32)
     dma("s", T.TU[:, B:TW], T.ut[:, 0:TW - B], "dut", [], ["TU2"], final=32)
-    dma("s", hnI, T.hn[:], "dhn", [], ["hnI"])
     dma("s", T.monb[:], T.mon[:], "dmon", [], ["monb"])
 
     iota(T.cI[:, 0:1], [[0, 1]], 0, 1, ["cI"], small=False)
-    iota(TMP, [[1, 128]], 0, 0, ["TMP"])
-    iota(T.C16[:], [[0, 64], [1, 16]], 0, 0, ["C16"])
+    iota(TMP[:], [[1, 144]], 0, 0, ["TMP"])
+    iota(T.C16[:], [[0, 16], [1, 16]], 0, 0, ["C16"])
     snd = _senders(core, topo)
-    pc = [A[:, me * VS + i * PW:me * VS + (i + 1) * PW] for i in range(NPC)]
-    send(snd[1:], pc[1:], pc[1:], "feed", ["Aown", "Aown2"])
-    send(peers, [pc[0]] * 4, [pc[0]] * 4, "ag", [])
+
+    def gather_all(part, R):
+        pc = [_piece(T, part, me, i, len(snd)) for i in range(len(snd))]
+        send(snd[1:], pc[1:], pc[1:], "feed%d" % part, R)
+        send(peers, [pc[0]] * 4, [pc[0]] * 4, "ag%d" % part, [])
+
+    gather_all(0, ["Aown", "Aown2"])
     iota(IO[:, 0:B], [[1, B]], 0, 0, ["IO"])
-    iota(IO[:, B:TW], [[1, TW - B]], 0, 0, ["IO2"])
 
     ts(T.cI[:, 1:2], T.cI[:, 0:1], 15, Op.bitwise_and, ["cI"], ["cI1"])
     ts(T.cI[:, 2:3], T.cI[:, 0:1], 112, Op.bitwise_and, ["cI"], ["cI2"])
+    ms(T.ONE[:], 1.0, ["ONE"])
     cp(T.cF[:, 0:2], T.cI[:, 1:3], ["cI1", "cI2"], ["cF"])
+    ms(C[:, W:HO], 0.0, ["Az"])
+    ms(C[:, HO + W:DO], 1.0, ["Hz"])
+    ts(REL, TMP[:, 0:128], g16, Op.subtract, ["TMP", "cF"], ["REL"])
     ts(ebias, rcol, 136.0, Op.add, ["cF"], ["eb"], -math.log(2.0), Op.mult)
-    ts(T.cF[:, 3:4], rcol, 192.0, Op.add, ["cF"], ["c128"])
-    act(pw4, rcol, ["cF"], ["pw4"], func=AF.Exp, scale=-math.log(4.0))
-    act(T.cF[:, 4:5], pw4, ["pw4"], ["pw4f"])
-    ts(REL, TMP, g16, Op.subtract, ["TMP", "cF"], ["REL"])
     ts(IDN, REL, rcol, Op.is_equal, ["REL"], ["IDN"])
     ts(TM2, REL, 0.0, Op.is_ge, ["REL"], ["TM2"])
     ts(BLK, REL, 16.0, Op.is_lt, ["REL"], ["BLK"])
+    ts(T.EK[:], TMP[:, 0:16], rcol, Op.is_equal, ["TMP", "cF"], ["EK"])
     tt(BLK, BLK, TM2, Op.mult, ["TM2", "BLK"], ["BLK"])
-    ts(NUP, REL, rcol, Op.is_lt, ["REL"], ["NUP"], -1.0, Op.mult)
-    tt(NUP, NUP, BLK, Op.mult, ["NUP", "BLK"], ["NUP"])
-    ts(T.EQ[:, 0:16], TMP[:, 0:16], rcol, Op.is_equal, ["TMP", "cF"], ["EQ"])
-    ms(T.RS64[:], 1.0, ["RS64"])
-    ms(T.RS64[:, 0:384:64], 0.0, ["RS64"])
-    ts(T.DM[:], T.C16[:], rcol, Op.is_equal, ["C16", "cF"], ["DM"])
-    act(T.PU1[:], T.DM[:], ["DM"], ["U2", "U3"])
+    act(pw4, rcol, ["cF"], ["pw4"], func=AF.Exp, scale=-math.log(4.0))
+    hf, ab, c1, c2 = T.G[:, 0:V], T.MX[:, 0:V], T.TOP[:, 0:V], T.TOP[:, B:B + V]
+    cp(hf, T.hnI[:], ["hnI"], ["G0", "G512"])
+    ts(c1, T.hnI[:], 0.5, Op.is_gt, ["hnI"], ["TOP0"], -float(TAG), Op.mult)
+    ts(c2, T.hnI[:], N * B + 0.5, Op.is_gt, ["hnI"], ["TOP1"], -6.0 * TAG, Op.mult)
+    act(ab, hf, ["G0", "G512"], ["MX0", "MX512"], func=AF.Abs)
+    for c0, c9, k in ((0, 512, "U2"), (512, V, "U3")):
+        mm(T.PU1[:, c0:c9], IDN, T.TOP[:, c0:c9], True, False, ["TOP0", "IDN"], [k])
+        mm(T.PU1[:, c0:c9], IDN, T.TOP[:, B + c0:B + c9], False, True, ["TOP1"], [k])
+    ts(T.SEL[:], TMP[:], -16.0, Op.add, ["TMP", "cF"], ["SEL"], g16, Op.is_equal)
+    ts(r0, rcol, 0.0, Op.is_equal, ["cF"], ["r0"])
+    ts(rh, rcol, 0.5, Op.mult, ["cF"], ["rh"])
+    cp(T.XR[:, 0:B], T.XI[:], ["XI"], ["XR"])
+    ts(T.SELF[:], T.SEL[:], r0, Op.mult, ["SEL", "r0"], ["SELF"])
+    tt(C[:, ho:ho + V], T.PU1[:, 0:V], ab, Op.subtract, ["U2", "U3", "MX0", "MX512"], ["Hown"])
+    gather_all(1, ["Hown"])
+    iota(IO[:, B:TW], [[1, TW - B]], 0, 0, ["IO2"])
     for k in range(16):
-        act(T.BRD[:, k, :], BLK, ["BLK", "EQ"], ["BRD"] if k == 15 else [], scale=T.EQ[:, k:k + 1])
-    ts(T.RST[:], T.C16[:], 0.0, Op.is_gt, ["C16"], ["RST"])
-    for r in range(16):
-        ts(T.SEL[:, r, :], REL, float(r), Op.is_equal, ["REL"], ["SEL"] if r == 15 else [])
-    ts(T.TOW[:, 0:B], ftI, 1.0 / V, Op.mult, ["ftI"], ["TOW"], 0.5 / V + 191.5, Op.add)
-    act(T.PU0[:], T.TOW[:, 0:B], ["TOW"], ["U0", "U1"], func=AF.Identity, scale=float(CAP), bias=-192.0 * CAP)
-    t0, t1 = T.G[:, 0:B], T.G[:, B:2 * B]
-    tt(t0, hbI, T.PU1[:], Op.mult, ["hbI%d" % r for r in range(16)] + ["U2", "U3"], ["G0", "G512"])
-    scan(t1, T.RST[:], t0, 0.0, Op.mult, Op.add, ["G0", "RST"], ["G1024", "G1536"])
-    ts(T.inc[:], T.G[:, B + 15:2 * B:16], 1.0 / V, Op.mult, ["G1024"], ["inc"], 0.5 / V + 191.5, Op.add)
-    ts(T.J16[:], TMP[:, 0:16], 16.0, Op.mult, ["TMP", "cF"], ["J16a"], rcol, Op.add)
-    ts(T.sa[:], T.inc[:], -192.0, Op.add, ["inc"], ["sa"], float(CAP), Op.mult)
-    ts(T.JB[:], T.J16[:], 0.5, Op.add, ["J16a"], ["JB"])
-    tt(T.ST[:], T.sa[:], T.G[:, B + 15:2 * B:16], Op.add, ["sa", "G1024"], ["ST"])
+        act(T.BRD[:, k, :], BLK, ["BLK", "EK"], ["BRD"] if k == 15 else [], scale=T.EK[:, k:k + 1])
+    ts(NUP, REL, rcol, Op.is_lt, ["REL"], ["NUP"], -1.0, Op.mult)
+    ms(T.RS64[:], 1.0, ["RS64"])
+    ms(T.RST[:], 1.0, ["RST"])
+    tt(NUP, NUP, BLK, Op.mult, ["NUP", "BLK"], ["NUP"])
+    ms(T.RS64[:, 0:448:64], 0.0, ["RS64"])
+    ms(T.RST[:, 0:B:16], 0.0, ["RST"])
+    ts(J16, TMP[:, 0:16], 16.0, Op.mult, ["TMP", "cF"], ["J16"], rcol, Op.add)
+    holdings()
+    ts(JB, J16, 0.5, Op.add, ["J16"], ["JB"])
+    ts(T.hz[:], T.PC[:, 0:64], W - 0.5, Op.is_lt, ["PC"], ["hz"])
 
     def late_start(part):
         if part == 0:
-            tt(T.TX[:, 0:B], ftI, T.PU0[:], Op.add, ["U0", "U1", "ftI"], ["TX"])
-            act(T.TX[:, B:TW], T.TX[:, 0:TW - B], ["TX"], ["TX2"])
-        if part == 1:
-            cp(T.I256[:], IO[:, 0:256], ["IO"], ["I256"])
-            ms(A[:, ZC:AW], 0.0, ["Az"])
-            for o in range(N):
-                ms(A[:, o * VS + V:(o + 1) * VS], 1.0, ["As%d" % o])
-        if part == 2:
             ts(D2M, IDN, 2.0, Op.mult, ["IDN"], ["D2M"])
+            ts(c192, rcol, 192.0, Op.add, ["cF"], ["c192"])
             tt(D2M, D2M, BLK, Op.subtract, ["D2M", "BLK"], ["D2M"])
-        if part == 3:
-            act(T.TOW[:, B:TW], T.TOW[:, 0:TW - B], ["TOW"], ["TOW2"])
-        if part == 5:
+            ts(DUM, J16, float(DO), Op.add, ["J16"], ["DUM"])
+            ts(JD, J16, float(B), Op.add, ["J16"], ["JD"])
+            ts(T.JH[:], J16, 16.0, Op.mult, ["J16"], ["JH"], 60.0, Op.add)
             cp(T.SELH[:], T.SEL[:], ["SEL"], ["SELH"])
-        if part == 7:
-            ms(T.F[:, 0:512], 1.0, ["F"])
-            ts(T.TRIM[:], T.C16[:, 0:S], rcol, Op.is_gt, ["C16", "cF"], ["TRIM"])
-        if part == 4:
-            act(T.J16[:], T.J16[:], ["J16a"], ["J16a", "J16"], scale=16.0)
-            act(B4, BLK, ["BLK"], ["B4"], scale=-4.0)
-            act(L1, D2M, ["D2M", "pw4f"], ["L1"], scale=T.cF[:, 4:5])
-            act(L2, L1, ["L1"], ["L2"], scale=2.0 ** -32)
-            base = T.acc2[:]
-            act(base, IO[:, 0:20], ["IO", "cF"], ["DMP0"], func=AF.Identity, scale=16.0, bias=rcol)
-            for i, c in enumerate((N * B - 7.5, N * B + S - 7.5, AD + me * S, VS, N * B + TAG + 1)):
-                act(T.DMP[:, i, :], base, ["DMP0"], [], func=AF.Identity, bias=float(c))
-            for q in range(N):
-                act(T.DMP[:, 5, 4 * q:4 * q + 4], T.acc2[:, 4 * q:4 * q + 4], ["DMP0"], ["DMP"] if q == N - 1 else [], func=AF.Identity,
-                    bias=float(N * B + S - q * B))
-            for o in range(N):
-                act(T.DEF[:, o * CAP:(o + 1) * CAP], IO[:, 0:CAP], ["IO"], ["DEF"] if o == N - 1 else [], func=AF.Identity, bias=float(o * VS + V))
-        if part == 6:
-            ts(T.PU0[:, 0:V], hnI, 5120.5, Op.is_lt, ["hnI"], ["U0", "U1"], 2.0 ** -32, Op.max)
-            tt(H[:, 0:V], hnI, T.PU0[:, 0:V], Op.mult, ["hnI", "U0", "U1"], ["H"])
-            ms(H[:, V:VS + S], 2.0 ** -20, ["Hd"])
-            act(T.MX[:, 0:V], T.PU0[:, 0:V], ["U0", "U1"], ["MX0", "MX512"], func=AF.Identity, scale=-5121.0, bias=5121.0)
-            dma("s", T.yh[:], T.MX[:, 0:V], "dc", ["MX0", "MX512"], ["yh"])
-            ms(T.UX[:, RO - 1, :], 0, ["UX%d" % (RO - 1)])
-            dma("s", U[0:128:18, :], T.UX[:, RO - 1, :], "dz", ["UX%d" % (RO - 1)], ["U", "ftI", "hnI"] + ["hbI%d" % r for r in range(16)])
+            ts(T.SELK[:], T.SEL[:], rh, Op.mult, ["SEL", "rh"], ["SELK"])
+            cp(BLKH, BLK, ["BLK"], ["BLKH"])
+            cp(IDNH, IDN, ["IDN"], ["IDNH"])
+            ts(T.TRIM[:], T.C16[:], rcol, Op.is_gt, ["C16", "cF"], ["TRIM"])
+            ts(T.SG[:, 0, :], TMP[:, 0:8], rcol, Op.is_lt, ["TMP", "cF"], ["SG0"], 2.0, Op.mult)
+            ts(T.SG[:, 0, :], T.SG[:, 0, :], -1.0, Op.add, ["SG0"], ["SG0"])
+            ts(T.SG[:, 1, :], T.SG[:, 0, :], -0.0625, Op.mult, ["SG0"], ["SG1"])
+        if part == 1:
+            act(pw4f, pw4, ["pw4"], ["pw4f"], scale=-(2.0 ** 80))
+            act(NL1, D2M, ["D2M", "pw4f"], ["NL1"], scale=pw4f)
+            act(NL2, NL1, ["NL1"], ["NL2"], scale=2.0 ** -32)
+            for m, c in ((B4K, TAG / 2), (B9, -9.0 * TAG / 16), (BN24, -(2.0 ** 24)), (BN8, -float(TAG)), (B05, 0.5), (BNC, -12.0 * TAG)):
+                act(m, BLK, ["BLK"], ["BX"], scale=c)
+            act(I8K, IDN, ["IDN"], ["BX"], scale=float(TAG))
+            act(T.NV[:, 0:B], IO[:, 0:B], ["IO"], ["NV"], func=AF.Identity, scale=-1.0, bias=-float(TAG + name0))
 
-    def a_scatter(t, o):
-        tt(A[:].indirect(T.OA[:, t, o, 0:20]), T.E[:, S * o:S * o + S], T.E[:, 2048 + S * o:2048 + S * o + S], Op.mult,
-           ["OA%d" % t, "OAo%d" % t, "old%d" % o, "ff%d" % o, "E0", "E1", "E2", "E3", "E4", "E5"], ["A"])
-
-    def new_state(t):
-        tt(T.X2[:], T.LU[:, t, 0:128], T.LU[:, t, 128:256], Op.max, ["LU%d" % t], ["X2"])
-        tt(T.X1[:], T.X2[:, 0:64], T.X2[:, 64:128], Op.max, ["X2"], ["X1"])
-        tt(T.ST[:], T.X1[:], T.Y[:], Op.max, ["X1", "Y"], ["ST"])
-
-    def h_update(part):
-        if part == 0:
-            cp(T.hL[:], T.o3[:, 1, :], ["o3"], ["hL"])
-            tt(T.u3[:], T.PC[:, 0:S], T.nm[:], Op.mult, ["PC", "nm"], ["u3"])
-            tt(T.u2[:], T.PU0[:, 0:S], T.Hc[:], Op.mult, ["U0", "Hc"], ["u2"])
-        else:
-            tt(H[:].indirect(T.hL[:]), T.u2[:], T.u3[:], Op.add, ["hL", "u2", "u3"], ["H"])
-
-    Ar = ["A", "Aown", "Aown2", "Az"] + ["As%d" % o for o in range(N)]
-    Aw = A[:, 0:AW]
     for t in range(RO):
         w0 = (L * t) % B
-        c0 = w0 // 16
         win = slice(w0, w0 + 1056)
         if t > 0:
-            new_state(t - 1)
-        ts(T.sa[:], T.ST[:], TAG - 1, Op.bitwise_and, ["ST"], ["sa"])
-        ts(T.hl[:, 0:64 - c0], T.sa[:, c0:64], float(ZC), Op.is_ge, ["sa"], ["hl"])
-        if c0:
-            ts(T.hl[:, 64 - c0:64], T.sa[:, 0:c0], float(ZC), Op.is_ge, ["sa"], ["hl2"])
-        scan(T.inc[:], T.hl[:], T.hl[:], 0.0, Op.add, Op.max, ["hl", "hl2"], ["inc"])
-        mm(T.PA[:, 0:64], BLK, T.inc[:], True, True, ["inc", "BLK"], ["PA"])
-        mm(T.PB[:, 0:64], BLK, T.inc[:], True, False, ["inc"], ["PB"])
-        mm(T.PB[:, 0:64], NUP, T.hl[:], False, True, ["hl", "hl2", "NUP"], ["PB"], inc=False)
-        mm(T.PB[:, 64:65], BLK, T.inc[:, 63:64], True, True, ["inc"], ["PB"])
-        mm(T.PD[:, 0:64], BLK, T.inc[:], True, True, ["inc"], ["PD"])
-        for m in range(10):
-            act(T.junk[:, 64 * m:64 * m + 64], T.PA[:, 0:64], ["PA", "JB"], ["acc"] if m in (0, 9) else [], func=AF.Sign, scale=-1.0, bias=T.JB[:, m:m + 1],
-                accum_out=T.acc[:, m:m + 1])
-        cp(T.P[:, 0:65], T.PB[:, 0:65], ["PB"], ["P"])
-        for m in range(10, 16):
-            ts(T.junk[:, 64 * m:64 * m + 64], T.PD[:, 0:64], T.JB[:, m:m + 1], Op.is_lt, ["PD", "JB"], ["junk"] if m in (10, 15) else [])
-        scan(T.cs[:], T.RS64[:], T.junk[:, 640:1024], 0.0, Op.mult, Op.add, ["junk", "RS64"], ["cs"])
-        cp(T.cL[:, 10:16], T.cs[:, 63:384:64], ["cs"], ["cL2"])
-        ts(T.c16[:, 10:16], T.cs[:, 63:384:64], 16.0, Op.mult, ["cs"], ["c162"])
-        if t == 0:
-            late_start(0)
-        ts(T.cL[:, 0:10], T.acc[:, 0:10], 64.0, Op.add, ["acc"], ["cL"], 0.5, Op.mult)
-        ts(T.c16[:, 0:10], T.acc[:, 0:10], 64.0, Op.add, ["acc"], ["c16"], 8.0, Op.mult)
-        tt(T.cmp[:], T.P[:, 0:65].indirect(T.cL[:]), IO[:, 0:256], Op.is_le, ["P", "cL", "cL2", "IO"], ["cmp"])
-        mm(T.PA[:, 0:16], IDN, T.c16[:], True, False, ["c16", "c162", "IDN"], ["PA"])
-        sel16(T.PA[:, 0:16], lambda r: T.cmp[:, r:256:16], ["cmp"], ["PA"], first=False)
-        if t > 0:
-            h_update(0)
+            check(w0)
+            sel16(T.PC[:, 0:64], lambda r: T.EQ[:, r:B:16], ["EQ0", "EQ1"], ["PC"])
+            hz, hk = T.PC[:, 0:64], "PC"
         else:
-            late_start(1)
+            hz, hk = T.hz[:], "hz"
+        scan(T.inc[:], T.ONE[:, 0:64], hz, 0.0, Op.add, Op.subtract, [hk, "ONE"], ["inc"])
+        ts(T.hl[:], hz, 0.5, Op.is_lt, [hk], ["hl"])
+        mm(T.PA[:, 0:64], BLK, T.inc[:], True, True, ["inc", "BLK"], ["PA"])
+        mm(T.PD[:, 0:64], BLK, T.inc[:], True, True, ["inc"], ["PD"])
+        mm(T.PB[:, 0:64], BLK, T.inc[:], True, False, ["inc"], ["PB"])
+        mm(T.PB[:, 0:64], NUP, T.hl[:], False, True, ["hl", "NUP"], ["PB"], inc=False)
+        mm(T.PB[:, 64:65], BLK, T.inc[:, 63:64], True, True, ["inc"], ["PB"])
+        for m in range(NA):
+            act(T.junk[:, 64 * m:64 * m + 64], T.PA[:, 0:64], ["PA", "JB"], ["acc"] if m in (0, NA - 1) else [], func=AF.Sign, scale=-1.0, bias=JB[:, m:m + 1],
+                accum_out=T.acc[:, m:m + 1])
+        for m in range(NA, 16):
+            ts(T.junk[:, 64 * m:64 * m + 64], T.PD[:, 0:64], JB[:, m:m + 1], Op.is_lt, ["PD", "JB"], ["junk"] if m in (NA, 15) else [])
+        cp(T.P[:, 0:65], T.PB[:, 0:65], ["PB"], ["P"])
+        nb = 64 * (16 - NA)
+        scan(T.cs[:, 0:nb], T.RS64[:, 0:nb], T.junk[:, 64 * NA:1024], 0.0, Op.mult, Op.add, ["junk", "RS64"], ["cs"])
+        ts(invL, J16, T.P[:, 64:65], Op.is_ge, ["J16", "P"], ["invL"], 2.0 * TAG, Op.mult)
+        cp(T.cL[:, NA:16], T.cs[:, 63:nb:64], ["cs"], ["cL2"])
+        ts(T.c16[:, NA:16], T.cs[:, 63:nb:64], 16.0, Op.mult, ["cs"], ["c162"])
+        ts(T.cL[:, 0:NA], T.acc[:, 0:NA], 64.0, Op.add, ["acc"], ["cL"], 0.5, Op.mult)
+        ts(T.c16[:, 0:NA], T.acc[:, 0:NA], 64.0, Op.add, ["acc"], ["c16"], 8.0, Op.mult)
+        tt(T.cmp[:], T.P[:, 0:65].indirect(T.cL[:]), IO[:, 0:L], Op.is_le, ["P", "cL", "cL2", "IO"], ["cmp"])
+        mm(T.PA[:, 0:16], IDN, T.c16[:], True, False, ["c16", "c162", "IDN"], ["PA"])
+        sel16(T.PA[:, 0:16], lambda r: T.cmp[:, r:L:16], ["cmp"], ["PA"], first=False)
         cp(T.bL[:], T.PA[:, 0:16], ["PA"], ["bL"])
         act(T.ug[:], T.TU[:, win].indirect(T.bL[:]), ["TU", "TU2", "bL"], ["ug"])
         cp(T.FO[:], T.TX[:, win].indirect(T.bL[:]), ["TX", "TX2", "bL"], ["FO"])
-        ts(T.PD[:, 256:512], T.I256[:], T.P[:, 64:65], Op.is_ge, ["I256", "P"], ["PD"], 197.0, Op.mult)
+        ts(T.li[:, 0, :], T.bL[:], float(w0), Op.add, ["bL"], ["li0"])
+        ts(T.xc[:], T.FO[:], -float(MID), Op.add, ["FO"], ["xc"])
+        ts(T.li[:, 1, :], T.li[:, 0, :], B - 1, Op.bitwise_and, ["li0"], ["li1"])
         if t == 0:
-            late_start(2)
-            arrive("A", "ag", 4 * NPC * KE)
+            late_start(0)
+            arrive("A", "ag0", 4 * len(snd) * KE)
+        tt(la, T.li[:, 1, :], invL, Op.add, ["li1", "invL"], ["la"])
+        tt(lb, la, JD, Op.min, ["la", "JD"], ["lb"])
+        cp(T.pos[:], lb, ["lb"], ["pos"])
         Ek = []
         for ci, (j0, nj, s0) in enumerate(CHUNKS):
             n = 16 * nj
@@ -377,7 +362,7 @@ def rank_program(g, core, T, topo):
             banks = ["U%d" % (s0 // 512 + i) for i in range(n // 512)]
             gk = ["G%d" % (s0 + 512 * i) for i in range(n // 512)]
             mk = ["MX%d" % (s0 + 512 * i) for i in range(n // 512)]
-            act(T.G[:, s0:s0 + n], Aw.indirect(T.FO[:, j0:j0 + nj]), Ar + ["FO"], gk)
+            act(T.G[:, s0:s0 + n], Aw.indirect(T.FO[:, j0:j0 + nj]), Ar + ["FO"], gk, func=AF.Abs)
             if ci >= 4:
                 act(T.PB[:, j0 - 128:j0 - 64], T.MX[:, s0 + 15:s0 + B:16], mk, ["PB"])
             for hb in range(n // 512):
@@ -388,166 +373,122 @@ def rank_program(g, core, T, topo):
             tt(T.E[:, 16 * j0:16 * j0 + n], T.G[:, s0:s0 + n], PU[:, s0 % B:s0 % B + n], Op.mult, gk + banks, ["E%d" % ci])
             scan(T.MX[:, s0:s0 + n], T.RST[:, 0:n], T.E[:, 16 * j0:16 * j0 + n], 0.0, Op.mult, Op.max, ["E%d" % ci, "RST"], mk)
             Ek.append("E%d" % ci)
-        if t == 0:
-            late_start(3)
-        act(T.dg[:, 2, :], T.TOW[:, win].indirect(T.bL[:]), ["TOW", "TOW2", "bL"], ["dg2"])
-        act(T.xg[:], T.TX[:, win].indirect(T.bL[:]), ["TX", "TX2", "bL"], ["xg"])
-        act(T.dg[:, 0, :], T.xg[:], ["xg"], ["dg0"])
-        act(T.PC[:, 0:256], T.dg[:, 0, :], ["dg0"], ["PC"])
         for b0, bn, bs in CHUNKS[-2:]:
             act(T.PB[:, b0:b0 + bn], T.MX[:, bs + 15:bs + 16 * bn:16], ["MX%d" % bs], ["PB"])
         if t == 0:
-            late_start(4)
-        act(T.b8[:], IO[:, win].indirect(T.bL[:]), ["IO", "IO2", "bL"], ["b8"], scale=float(TAG))
-        for o in range(N):
-            act(T.W[:, o:512:8], T.DEF[:, CAP * o:CAP * o + CAP], ["DEF"], ["W"] if o in (0, N - 1) else [])
-        act(T.PU1[:, 0:CAP], T.DM[:, 0:CAP], ["DM"], ["U2"])
-        act(T.VAL[:, 0:S], IO[:, 0:S], ["IO"], ["VAL0"], func=AF.Identity, scale=0.0, bias=float(TAG * (t + 1) + ZC))
-        tt(T.ow[:], T.dg[:, 2, :], T.PD[:, 256:512], Op.max, ["dg2", "PD"], ["ow"])
+            late_start(1)
+            arrive("H", "ag1", 4 * len(snd) * KE)
+        act(T.nv[:], IO[:, win].indirect(T.bL[:]), ["IO", "IO2", "bL"], ["nv"], func=AF.Identity, scale=-1.0, bias=-float(TAG * (t + 2) + name0))
+        act(T.PU0[:, 768:B], T.TRIM[:], ["TRIM"], ["U1"])
+        TH, DN, FA, RR = T.PU1[:, 0:L], T.PU1[:, 512:512 + L], T.PC[:, 0:L], T.PA[:, 0:L]
+        mm(TH, B9, T.ONE[:, 0:L], True, False, ["BX", "ONE"], ["U2"])
+        mm(DN, BLK, T.ONE[:, 0:L], True, False, ["ONE"], ["U3"])
         for k in range(16):
-            tt(T.TOP[:, k:4096:16], T.E[:, k:4096:16], T.PB[:, 0:256], Op.is_equal, Ek + ["PB"], ["TOP%d" % k])
-            mm(T.PA[:, 0:256], T.SEL[:, k, :], T.TOP[:, k:4096:16], k == 0, k == 15, ["TOP%d" % k], ["PA"])
-        act(T.w[:], T.PA[:, 0:256], ["PA", "eb"], ["w"], func=AF.Exp, scale=16.0 * math.log(2.0), bias=ebias)
-        tt(T.dg[:, 1, :], T.xg[:], T.PC[:, 0:256], Op.subtract, ["xg", "PC"], ["dg1"])
-        if t == 0:
-            late_start(5)
-        mm(T.PC[:, 0:256], D2M, T.w[:], True, True, ["w", "D2M"], ["PC"])
-        oh = T.PC[:, 256:512]
-        ts(oh, T.PC[:, 0:256], 0.0, Op.is_ge, ["PC"], ["PC"])
-        tt(T.Z2[:, 512:768], oh, T.ow[:], Op.mult, ["PC", "ow"], ["Z22"])
-        mm(T.PD[:, 0:256], BLK, T.Z2[:, 512:768], True, True, ["Z22"], ["PD"])
-        tt(T.Z2[:, 0:256], oh, T.dg[:, 0, :], Op.mult, ["PC", "dg0"], ["Z20"])
-        tt(T.Z2[:, 256:512], oh, T.dg[:, 1, :], Op.mult, ["PC", "dg1"], ["Z21"])
-        mm(T.PA[:, 0:256], BLK, T.Z2[:, 0:256], True, False, ["Z20"], ["PA"])
-        mm(T.PA[:, 0:256], BLK, T.Z2[:, 256:512], False, True, ["Z21"], ["PA"])
-        ts(T.ind[:], T.PD[:, 0:256], T.cF[:, 3:4], Op.is_equal, ["PD", "c128"], ["ind"], 8.0, Op.mult)
-        scan(T.PD[:, 256:512], T.ind[:], T.ind[:], rcol, Op.add, Op.max, ["ind"], ["PD"])
-        tt(T.q1[:], T.ind[:], T.PD[:, 256:512], Op.mult, ["ind", "PD"], ["q1"])
-        sel16(T.PB[:, 0:16], lambda r: T.q1[:, r:256:16], ["q1"], ["PB"], mat=T.SELH)
-        tt(T.pay[:], T.PA[:, 0:256], T.b8[:], Op.add, ["PA", "b8"], ["pay"])
-        ts(T.Z2[:, 768:1024], oh, rcol, Op.mult, ["PC"], ["Z23"])
-        sel16(T.PD[:, 256:272], lambda r: T.Z2[:, 768 + r:1024:16], ["Z23"], ["PD"])
-        if t == 0:
-            late_start(7)
-        act(T.PU1[:, 512:512 + S], T.TRIM[:], ["TRIM"], ["U3"])
-        ts(T.slot[:], T.PB[:, 0:16], 0.125, Op.mult, ["PB"], ["slot"], -8.0, Op.add)
-        cp(T.W[:].indirect(T.slot[:]), T.pay[:], ["slot", "pay"], ["W"])
-        for o in range(N):
-            tt(T.G[:, CAP * o:CAP * o + CAP], T.W[:, o:512:8], T.PU1[:, 0:CAP], Op.mult, ["W", "U2"], ["G0"] if o in (0, N - 1) else [])
-        scan(T.G[:, 512:512 + S], T.RST[:, 0:S], T.G[:, 0:S], 0.0, Op.mult, Op.add, ["G0"], ["G512"])
-        lm = T.LM[:, t, me, :]
-        cp(lm, T.G[:, 512 + 15:512 + S:16], ["G512"], ["LMo%d" % t])
-        send(peers, [lm] * 4, [lm] * 4, "ea%d" % t, ["LMo%d" % t])
-        arrive("LM%d" % t, "ea%d" % t, 4 * KE)
-        tt(T.tkf[:], T.PD[:, 256:272], T.J16[:], Op.add, ["PD", "J16"], ["tkf"])
-        cp(T.tk[:], T.tkf[:], ["tkf"], ["tk"])
-        act(T.fc[:], T.TOP[:].indirect(T.tk[:]), ["tk"] + ["TOP%d" % k for k in range(16)], ["fc"], func=AF.Identity, scale=-0.0625, bias=1.0)
-        if t > 0:
-            h_update(1)
-        cp(T.F[:].indirect(T.slot[:]), T.fc[:], ["slot", "fc"], ["F"])
-        for o in range(N):
-            act(T.FL[:, t, me, CAP * o:CAP * o + CAP], T.F[:, o:512:8], ["F"], ["FLo%d" % t] if o == N - 1 else [])
-        fl = T.FL[:, t, me, :]
-        send(peers, [fl] * 4, [fl] * 4, "eb%d" % t, ["FLo%d" % t])
-        arrive("FL%d" % t, "eb%d" % t, 4 * KE)
-        if t == 0:
-            late_start(6)
-        lmk = ["LM%d" % t, "LMo%d" % t]
-        mine = T.LM[:, t, :, 4 * me:4 * me + 4]
-        ts(T.pa[:], mine, TAG - 1, Op.bitwise_and, lmk, ["pa"])
-        ts(T.XO[:], T.pa[:], float(-me * VS), Op.add, ["pa"], ["XO"])
-        ts(T.XOf[:], T.pa[:], float(-me * VS), Op.add, ["pa"], ["XOf"])
-        act(T.Hc[:], H[:].indirect(T.XO[:]), ["H", "Hd", "XO"], ["Hc"])
-        cp(T.x16[:], IO[:, 0:B].indirect(T.XO[:]), ["IO", "XO"], ["x16"])
-        act(T.yhi[:], T.Hc[:], ["Hc"], ["yhi"], func=AF.Identity, scale=-1.0, bias=float(TAG))
-        act(T.PU0[:, 512:512 + S], T.Hc[:], ["Hc"], ["U1"], func=AF.Identity, scale=-1.0, bias=float(TAG))
-        act(T.VAL[:, S:2 * S], IO[:, 0:B].indirect(T.XO[:]), ["IO", "XO"], ["VAL1"], func=AF.Identity, bias=float(TAG * (t + 1) + me * VS))
-        D = T.PA[:, 0:S]
+            tt(T.TOP[:, k:4096:16], T.E[:, k:4096:16], T.PB[:, 0:L], Op.is_equal, Ek + ["PB"], ["TOP%d" % k])
+            mm(T.PA[:, 0:L], T.SEL[:, 16 - k:144 - k], T.TOP[:, k:4096:16], k == 0, k == 15, ["TOP%d" % k], ["PA"])
+        act(T.w[:], T.PA[:, 0:L], ["PA", "eb"], ["w"], func=AF.Exp, scale=16.0 * math.log(2.0), bias=ebias)
+        mm(T.PC[:, 0:L], D2M, T.w[:], True, True, ["w", "D2M"], ["PC"])
+        mm(T.PD[:, 0:L], D2M, T.w[:], True, True, ["w"], ["PD"])
+        oh = T.PC[:, L:2 * L]
+        ts(oh, T.PC[:, 0:L], 0.0, Op.is_ge, ["PC"], ["PC"])
+        act(T.sg[:], T.PD[:, 0:L], ["PD"], ["sg"], func=AF.Sign)
+        tt(T.Z[:], oh, T.xc[:], Op.mult, ["PC", "xc"], ["Z"])
+        sel16(T.PB[:, 0:16], lambda r: T.Z[:, r:L:16], ["Z", "SELH"], ["PB"], mat=T.SELH)
+        mm(T.PU0[:, 0:L], BLKH, T.Z[:], True, True, ["Z", "BLKH"], ["U0"])
+        mm(T.PU0[:, 512:512 + L], BLKH, T.Z[:], True, True, ["Z"], ["U1"])
+        mm(T.PD[:, L:L + 16], IDNH, T.JH[:], True, False, ["IDNH", "JH", "sg"], ["PD"])
+        sel16(T.PD[:, L:L + 16], lambda r: T.sg[:, r:L:16], ["sg", "SELK"], ["PD"], first=False, mat=T.SELK)
+        ts(T.XL[:], T.PB[:, 0:16], float(MID), Op.add, ["PB"], ["XL"])
+        ts(T.xr[:], T.PU0[:, 0:L], float(MID), Op.add, ["U0"], ["xr"])
+        ts(T.XLf[:], T.PB[:, 0:16], float(MID), Op.add, ["PB"], ["XLf"])
+        ts(T.E3[:, 0, :], T.xr[:], T.XLf[:, 0:1], Op.is_equal, ["xr", "XLf"], ["E30"], 256.0, Op.mult)
+        cp(T.tk[:], T.PD[:, L:L + 16], ["PD"], ["tk"])
+        act(T.own[:], T.PU0[:, 512:512 + L], ["U1"], ["own"], func=AF.Identity, scale=1.0 / V, bias=(MID + 0.5) / V + 191.5)
+        act(T.SA[:], Aw.indirect(T.XL[:]), Ar + ["XL"], ["SA"], func=AF.Sign)
+        act(T.Hc[:], Hw.indirect(T.XL[:]), Hr + ["XL"], ["Hc"])
+        mm(TH, B4K, T.SA[:], False, True, ["SA"], ["U2"])
+        act(T.EM[:], T.Hc[:], ["Hc"], ["EM"], func=AF.Relu, bias=1.0)
+        act(T.fc[:], T.TOP[:].indirect(T.tk[:]), ["tk", "SG0", "SG1"] + ["TOP%d" % k for k in range(16)], ["fc"], func=AF.Identity,
+            scale=T.SG[:, 1, t:t + 1], bias=T.SG[:, 0, t:t + 1])
+        act(T.AA[:], Aw.indirect(T.XL[:]), Ar + ["XL"], ["AA"], func=AF.Abs)
 
         def pair(m):
-            ts(T.E3[:, m, 0:S - 16 * m], T.x16[:, 16 * m:S], T.XOf[:, m:m + 1], Op.is_equal, ["x16", "XOf"], ["E3%d" % m])
+            ts(T.E3[:, m, 0:L - 16 * m], T.xr[:, 16 * m:L], T.XLf[:, m:m + 1], Op.is_equal, ["xr", "XLf"], ["E3%d" % m], 256.0, Op.mult)
+            if m < 15:
+                mm(T.PA[:, 16 * m + 16:L], BLK, T.E3[:, m, 16:L - 16 * m], False, False, ["E3%d" % m], ["PA"])
 
-        pair(0)
-        ts(T.EO[:, 0, :], T.Hc[:], 0.0, Op.is_equal, ["Hc"], ["EO0"])
-        mm(D, L1, T.EO[:, 0, :], True, False, ["EO0", "L1"], ["PA"])
-        for m in range(20):
-            if m == 8:
-                ts(T.EO[:, 1, :], T.Hc[:], -0.5, Op.is_lt, ["Hc"], ["EO1"])
-                mm(D, L2, T.EO[:, 1, :], False, False, ["EO1", "L2"], ["PA"])
-            if m:
-                pair(m)
-            if m < 19:
-                mm(T.PA[:, 16 * m + 16:S], B4, T.E3[:, m, 16:S - 16 * m], False, False, ["E3%d" % m, "B4"], ["PA"])
-        tt(T.sgn[:], T.E3[:, :, 0:16], T.PU1[:, 512:512 + S], Op.mult, ["E319", "U3"], ["sgn"])
-        mm(D, B4, T.sgn[:], False, True, ["sgn"], ["PA"])
-        tt(T.ylo[:], T.PU0[:, 512:512 + S], T.yhi[:], Op.subtract, ["U1", "yhi"], ["ylo"])
-        ts(T.pb[:], mine, 13, Op.logical_shift_right, lmk, ["pb"])
-        ts(T.pc[:], T.LM[:, t, :, :], TAG - 1, Op.bitwise_and, lmk, ["pc"])
-        tt(T.cc[:, 20:40], T.pb[:], T.DMP[:, 5, :], Op.subtract, ["pb", "DMP"], ["cc1"])
-        ts(T.PC[:, 0:S], D, 0.0, Op.is_gt, ["PA"], ["PC"])
-        ts(T.Z[:, 2 * S:3 * S], D, 0.0, Op.is_equal, ["PA"], ["Z0"])
-        tt(T.Z[:, 0:S], T.PC[:, 0:S], T.yhi[:], Op.mult, ["PC", "yhi"], ["Z1"])
-        tt(T.Z[:, S:2 * S], T.PC[:, 0:S], T.ylo[:], Op.mult, ["PC", "ylo"], ["Z2"])
-        sel16(T.PD[:, 0:60], lambda r: T.Z[:, r:3 * S:16], ["Z0", "Z1", "Z2"], ["PD"])
-        for o in range(N):
-            cp(T.XA[:, o, :], T.pc[:, :, 4 * o:4 * o + 4], ["pc"], ["XA"] if o in (0, N - 1) else [])
-        cp(T.NO[:], T.pb[:], ["pb"], ["NO"])
-        tt(T.xd[:, 0, :], T.pa[:], T.DMP[:, 2, :], Op.subtract, ["pa"], ["xd0"])
-        tt(T.xd[:, 1, :], T.XOf[:], T.DMP[:, 3, :], Op.subtract, ["XOf"], ["xd1"])
-        for o in range(N):
-            act(T.E[:, 2048 + S * o:2048 + S * o + S], T.FL[:, t, :, CAP * o:CAP * o + CAP], ["FL%d" % t, "FLo%d" % t],
-                ["ff%d" % o] + (Ek if o == 0 else []))
-        for q in range(N):
-            act(T.E[:, S * q:S * q + S], Aw.indirect(T.XA[:, q, :]), Ar + ["XA"], ["old%d" % q])
-        act(T.sgn[:], D, ["PA"], ["sgn"], func=AF.Sign)
-        act(T.sgn[:], T.sgn[:], ["sgn"], ["sgn"], func=AF.Abs, scale=-2.0, bias=0.5)
-        act(T.PU0[:, 0:S], T.sgn[:], ["sgn"], ["U0"], func=AF.Identity, bias=-1.5)
-        for q in range(N):
-            act(T.nm[:, CAP * q:CAP * q + CAP], IO[:, 0:B].indirect(T.NO[:, 4 * q:4 * q + 4]), ["IO", "NO"], ["nm"] if q in (0, N - 1) else [],
-                func=AF.Identity, bias=float(q * B + 1))
-        cp(T.s60[:, 0:60], T.PD[:, 0:60], ["PD"], ["s60"])
-        tt(T.ev[:], T.s60[:, 0:20], T.s60[:, 20:40], Op.add, ["s60"], ["ev"])
-        ts(T.gg[:, 0:20], T.ev[:], TAG + 0.5, Op.is_gt, ["ev"], ["gg0"])
-        ts(T.gg[:, 20:40], T.ev[:], 0.5, Op.is_gt, ["ev"], ["gg1"])
-        tt(T.cc[:, 0:20], T.ev[:], T.DMP[:, 4, :], Op.subtract, ["ev"], ["cc0"])
-        tt(T.s60[:, 60:80], T.ev[:], T.s60[:, 40:60], Op.add, ["ev", "s60"], ["s61"])
-        tt(T.n2[:], T.cc[:], T.gg[:], Op.mult, ["cc0", "cc1", "gg0", "gg1"], ["n2"])
-        ts(T.g2[:], T.s60[:, 40:80], 0.5, Op.is_gt, ["s60", "s61"], ["g2"])
-        tt(T.n3[:], T.n2[:], T.DMP[:, 0:2, :], Op.add, ["n2"], ["n3"])
-        tt(T.o2[:], T.g2[:], T.xd[:], Op.mult, ["g2", "xd0", "xd1"], ["o2"])
-        ts(T.hI[:], T.n3[:], 0.0625, Op.mult, ["n3"], ["hI"])
-        tt(T.o3[:], T.o2[:], T.DMP[:, 2:4, :], Op.add, ["o2"], ["o3"])
-        ts(T.n4[:], T.n3[:], 7.5, Op.add, ["n3"], ["n4"], 360.0, Op.mult)
-        oa = T.OA[:, t, me, 0:20]
-        ts(T.h2[:], T.hI[:], -5759.0, Op.mult, ["hI"], ["h2"])
-        cp(oa, T.o3[:, 0, :], ["o3"], ["OAo%d" % t])
-        send(peers, [oa] * 4, [oa] * 4, "eo%d" % t, ["OAo%d" % t])
-        arrive("OA%d" % t, "eo%d" % t, 4 * KE)
-        tt(T.n5[:], T.n4[:], T.h2[:], Op.add, ["n4", "h2"], ["n5"])
-        cp(T.uL[:], T.n5[:], ["n5"], ["uL"])
-        cp(U[:].indirect(T.uL[:]), T.VAL[:], ["uL", "VAL0", "VAL1"], ["U"])
-        dma("s", T.UX[:, t, :], U[0:128:18, :], "dx%d" % t, ["U"], ["UX%d" % t])
-        send(peers, [T.UX[:, t, 64 * r:64 * r + 64] for r in peers_r],
-             [T.LU[:, t, 64 * ((me - r - 1) % N):64 * ((me - r - 1) % N) + 64] for r in peers_r], "eu%d" % t, ["UX%d" % t])
-        arrive("LU%d" % t, "eu%d" % t, 4 * KE)
-        if t == RO - 1:
-            h_update(0)
-            h_update(1)
-            deps("g", ["H", "yh"], [])
-            g.dma_start(T.yh[:], H[:, 0:V], accum_op=Op.add).then_inc(T.sem["dyh"], 16)
-            total["dyh"] = 16
-        for o in range(N):
-            a_scatter(t, o)
-        tt(T.Y[:], T.ST[:], T.UX[:, t, 64 * me:64 * me + 64], Op.max, ["ST", "UX%d" % t], ["Y"])
+        ts(T.ind[:], T.own[:], c192, Op.is_equal, ["own", "c192"], ["ind"])
+        tt(xI, T.XLf[:], invL, Op.add, ["XLf", "invL"], ["xI"])
+        scan(T.cn[:], T.ind[:], T.ind[:], 0.0, Op.add, Op.max, ["ind"], ["cn"])
+        tt(T.q1[:], T.ind[:], T.cn[:], Op.mult, ["ind", "cn"], ["q1"])
+        mm(RR, BLK, T.q1[:], True, False, ["q1"], ["PA"])
+        mm(T.PA[:, 16:L], BLK, T.E3[:, 0, 16:L], False, False, ["E30"], ["PA"])
+        for m in range(1, 4):
+            pair(m)
+        tt(T.AV[:], T.Hc[:], TH, Op.is_gt, ["Hc", "U2"], ["AV"])
+        mm(DN, NL1, T.EM[:], False, False, ["EM", "NL1"], ["U3"])
+        mm(DN, NL2, T.AV[:], False, True, ["AV", "NL2"], ["U3"])
+        sel16(T.PB[:, 16:32], lambda r: T.AV[:, r:L:16], ["AV"], ["PB"])
+        for m in range(4, 16):
+            pair(m)
+        mm(FA, BN24, T.AV[:], True, False, ["AV"], ["PC"])
+        mm(FA, IDN, T.fc[:], False, True, ["fc"], ["PC"])
+        tt(T.dg[:], T.E3[:, :, 0:16], T.PU0[:, 768:B], Op.mult, ["E3%d" % m for m in range(16)] + ["U1"], ["dg"])
+        mm(RR, BLK, T.dg[:], False, True, ["dg"], ["PA"])
+        act(T.Rb[:], RR, ["PA"], ["Rb"], func=AF.Identity, scale=2048.0, bias=-2048.0 * (CAP + 0.5))
+        sel16(T.PD[:, 0:16], lambda r: T.Rb[:, r:L:16], ["Rb"], ["PD"])
+        pl = T.PL[:, t, me, :]
+        ts(fl, T.PB[:, 16:32], 1.0, Op.min, ["PB"], ["fl"], float(HO), Op.mult)
+        tt(DN, DN, T.nv[:], Op.max, ["U3", "nv"], ["U3"])
+        tt(FA, FA, T.AA[:], Op.mult, ["PC", "AA"], ["PC"])
+        tt(xo, fl, xI, Op.add, ["fl", "xI"], ["xo"])
+        tt(T.X[:], DN, T.Hc[:], Op.min, ["U3", "Hc"], ["X"])
+        tt(pl[:, 0:L], FA, T.X[:], Op.max, ["PC", "X"], ["PLa%d" % t])
+        tt(lm, T.PD[:, 0:16], xo, Op.max, ["PD", "xo"], ["lm"])
+        tt(pl[:, L:L + 16], lm, DUM, Op.min, ["lm", "DUM"], ["PLb%d" % t])
+        send(peers, [pl] * 4, [pl] * 4, "ea%d" % t, ["PLa%d" % t, "PLb%d" % t])
+        arrive("PL%d" % t, "ea%d" % t, 4 * KE)
+        if t == 0:
+            check(0)
+            act(T.G[:, 0:B], IO[:, 0:B], ["IO"], ["G0", "G512"], func=AF.Identity, scale=-1.0, bias=-float(name0))
+            for c in range(2):
+                mm(T.PU1[:, 512 * c:512 * c + 512], BN8, T.EQ[:, 512 * c:512 * c + 512], True, True, ["EQ0", "EQ1"], ["U%d" % (2 + c)])
+        cp(T.XR[:].indirect(T.pos[:]), T.xr[:], ["pos", "xr"], ["XR"])
+        if t == 0:
+            tt(T.NV[:, 0:B], T.PU1[:], T.G[:, 0:B], Op.add, ["U2", "U3", "G0", "G512"], ["NV"])
+        cp(T.NV[:].indirect(T.pos[:]), T.nv[:], ["pos", "nv"], ["NV"])
+        holdings()
+        pk = ["PL%d" % t, "PLa%d" % t, "PLb%d" % t]
+        cp(T.OL[:], T.PL[:, t, :, L:L + 16], pk, ["OL"])
+        for q in range(N - 1, -1, -1):
+            cp(C[:].indirect(T.OL[:, q, :]), T.PL[:, t, q, 0:L], pk + ["OL"] + Ar + Hr, ["C"])
 
-    dma("s", T.yal[:], A[:, own], "dout", ["A"], [], final=48)
-    new_state(RO - 1)
-    ts(T.sa[:], T.ST[:], TAG - 1, Op.bitwise_and, ["ST"], ["sa"])
-    cp(T.hold[:], T.sa[:], ["sa"], ["hold"])
+    check(0)
+    tg, sa = T.TOP[:, 0:V], T.TOP[:, B:B + V]
+    act(T.MX[:, 0:V], C[:, ao:ao + V], ["C"], ["MX0", "MX512"], func=AF.Abs)
+    dma("s", T.yal[:], T.MX[:, 0:V], "dout", ["MX0", "MX512"], [], final=80)
+    act(tg, C[:, ho:ho + V], ["C"], ["TOP0"], func=AF.Identity, scale=-1.0 / TAG, bias=192.0 - 0.3125)
+    act(sa, C[:, ao:ao + V], ["C"], ["TOP1"], func=AF.Sign)
     for c in range(2):
-        tt(T.G[:, 512 * c:512 * c + 512], Aw.indirect(T.hold[:, 32 * c:32 * c + 32]), T.monb[:, 512 * c:512 * c + 512], Op.mult,
-           ["A", "hold", "monb"], ["G%d" % (512 * c)])
-        dma("a" if c == 0 else "s", T.yp[:, 512 * c:512 * c + 512], T.G[:, 512 * c:512 * c + 512], "dout", ["G%d" % (512 * c)], [], final=48)
+        cs = slice(512 * c, 512 * c + 512)
+        mm(T.PU0[:, cs], BLK, T.EQ[:, cs], True, True, ["EQ0", "EQ1"], ["U%d" % c])
+        tt(T.PU0[:, cs], T.PU0[:, cs], T.monb[:, cs], Op.mult, ["U%d" % c, "monb"], ["U%d" % c])
+    halves = ((0, h, T.PA, "PA", "U2"), (h, V, T.PB, "PB", "U3"))
+    for c, (c0, c9, ps, k, u) in enumerate(halves):
+        t8 = T.PU1[:, 512 * c:512 * c + h]
+        mm(t8, BNC, T.ONE[:, 0:h], True, False, ["ONE"], [u])
+        mm(t8, I8K, T.TOP[:, c0:c9], False, True, ["TOP0"], [u])
+        mm(ps[:, 0:h], IDN, T.TOP[:, c0:c9], True, False, ["TOP0"], [k])
+        mm(ps[:, 0:h], B05, T.TOP[:, B + c0:B + c9], False, True, ["TOP1"], [k])
+        tt(T.E[:, c0:c9], t8, C[:, ho + c0:ho + c9], Op.add, [u, "C"], ["E%d" % c])
+    for c, (c0, c9, ps, k, u) in enumerate(halves):
+        cs = slice(512 * c, 512 * c + 512)
+        act(ps[:, 0:h], ps[:, 0:h], [k], [k], func=AF.Sign, scale=-1.0, bias=200.5)
+        act(T.G[:, cs], Aw.indirect(T.HL[:, 32 * c:32 * c + 32]), ["C", "HL"], ["G%d" % (512 * c)], func=AF.Abs)
+        tt(T.E[:, B + c0:B + c9], ps[:, 0:h], T.E[:, c0:c9], Op.mult, [k, "E%d" % c], ["Y%d" % c])
+        dma("s", T.yh[:, c0:c9], T.E[:, B + c0:B + c9], "dout", ["Y%d" % c], [], final=80)
+        tt(T.E[:, 2 * B + 512 * c:2 * B + 512 * c + 512], T.PU0[:, cs], T.G[:, cs], Op.mult, ["U%d" % c, "G%d" % (512 * c)], ["Yp%d" % c])
+        dma("s", T.yp[:, cs], T.E[:, 2 * B + 512 * c:2 * B + 512 * c + 512], "dout", ["Yp%d" % c], [], final=80)
     for e in cnt:
         total["s" + e] = cnt[e]
     for sem, val in total.items():

@@ -10,9 +10,11 @@ DO = 2 * HO
 TAG = 8192
 MID = W // 2
 TW = 768 + 1056
-PW = 168
-CHUNKS = ((0, 32, 0), (32, 32, 512), (64, 32, 1024), (96, 32, 1536), (128, 64, 0), (192, 64, 1024))
-NA = 9
+PW = (128, 272)
+CHUNKS = ((0, 16, 0), (16, 16, 1), (32, 32, 2), (64, 32, 3), (96, 32, 0), (128, 64, 2), (192, 64, 0))
+M0, NA = 4, 8
+CYC, FIX, HOP, SELF = 0.00083, 0.05, 0.1, 0.06
+WAIT, LEAD, FAST = 0.5, 0.3, 3.0
 
 f32, bf, f16, i32, u16 = "float32", "bfloat16", "float16", "int32", "uint16"
 
@@ -22,43 +24,44 @@ def _sb(shape, d):
 
 
 SCRATCH = {
-    "C": _sb([DO + L], f32), "PL": _sb([RO, N, L + 16], f32), "OL": _sb([N, 16], u16),
-    "XR": _sb([B + L], f32), "NV": _sb([B + L], f32), "HL": _sb([64], u16), "EQ": _sb([B], bf),
+    "C": _sb([DO + L], f32), "PL": _sb([RO, N, L], f32), "OL": _sb([RO, N, 16], u16),
+    "XR": _sb([B + L], f32), "NV": _sb([B + L], f32), "NV1": _sb([B], f32), "HL": _sb([64], u16), "EQ": _sb([B], bf),
     "XI": _sb([B], i32), "hnI": _sb([V], i32), "IOTA": _sb([TW], f32), "TX": _sb([TW], i32), "TU": _sb([TW], bf), "monb": _sb([B], bf),
-    "G": _sb([2048], f32), "E": _sb([4096], f32), "MX": _sb([2048], f32), "TOP": _sb([4096], bf), "E3": _sb([16, L], bf),
-    "RST": _sb([B], bf), "ONE": _sb([512], bf), "TRIM": _sb([L], bf), "C16": _sb([L], bf),
-    "TMP": _sb([144], bf), "SEL": _sb([144], bf), "SELH": _sb([144], f16), "SELK": _sb([144], bf), "SELF": _sb([144], f32),
-    "BRD": _sb([16, 128], bf), "MAT": _sb([16, 128], bf), "MATH": _sb([2, 128], f16),
+    "G": _sb([4096], f32), "E": _sb([4096], f32), "MX": _sb([4096], f32), "TOP": _sb([4096], bf), "E3": _sb([16, L], bf),
+    "RST": _sb([B], bf), "ONE": _sb([512], bf), "C16": _sb([L], bf),
+    "TMP": _sb([144], bf), "SEL": _sb([3, 144], bf), "SELH": _sb([144], f16), "SELF": _sb([144], f32), "IDNF": _sb([128], f32),
+    "BRD": _sb([16, 128], bf), "MAT": _sb([17, 128], bf), "MATH": _sb([2, 128], f16),
     "cI": _sb([8], i32), "cF": _sb([12], f32), "cB": _sb([8], bf), "EK": _sb([16], f32), "SG": _sb([2, 8], f32),
     "JT": _sb([4, 16], f32), "JH": _sb([16], f16),
-    "RS64": _sb([448], bf), "cs": _sb([448], bf), "hz": _sb([64], bf), "hl": _sb([64], bf), "inc": _sb([64], bf), "P": _sb([72], f32),
-    "junk": _sb([1024], bf), "acc": _sb([16], f32), "cL": _sb([16], u16), "c16": _sb([16], bf), "cmp": _sb([L], bf), "bL": _sb([16], u16),
+    "RS64": _sb([B], bf), "cs": _sb([B], bf), "hz": _sb([64], bf), "hl": _sb([64], bf), "inc": _sb([64], bf), "P": _sb([72], f32),
+    "junk": _sb([B], bf), "acc": _sb([16], f32), "cL": _sb([16], u16), "cmp": _sb([L], bf), "bL": _sb([16], u16),
     "FO": _sb([L], u16), "ug": _sb([L], bf), "xc": _sb([L], f16), "nv": _sb([L], f32), "w": _sb([L], bf), "sg": _sb([L], bf),
-    "Z": _sb([L], f16), "XL": _sb([16], u16), "XLf": _sb([16], f32), "xr": _sb([L], u16), "tk": _sb([16], u16),
+    "Z": _sb([L], f16), "XL": _sb([16], u16), "tk": _sb([16], u16), "XLf": _sb([16], f32), "xr": _sb([L], u16),
     "SA": _sb([L], bf), "Hc": _sb([L], f32), "EM": _sb([L], bf), "AA": _sb([L], f32), "fc": _sb([L], bf), "own": _sb([L], bf),
-    "ind": _sb([L], bf), "cn": _sb([L], bf), "q1": _sb([L], bf), "AV": _sb([L], bf), "dg": _sb([L], bf), "Rb": _sb([L], bf), "X": _sb([L], f32),
-    "li": _sb([2, 16], i32), "lf": _sb([8, 16], f32), "pos": _sb([16], u16),
+    "ind": _sb([L], bf), "cn": _sb([L], bf), "q1": _sb([L], bf), "dg": _sb([L], bf), "X": _sb([L], f32),
+    "AV": _sb([L], bf), "sF": _sb([L], bf), "Rb": _sb([L], bf),
+    "li": _sb([2, 16], i32), "lf": _sb([4, 16], f32), "pos": _sb([16], u16),
     "PU0": ("psum", [128, 1024], f32), "PU1": ("psum", [128, 1024], f32),
     "PA": ("psum", [128, 512], f32), "PB": ("psum", [128, 512], f32), "PC": ("psum", [128, 512], f32),
     "PD": ("psum", [128, 512], f32),
 }
 SEMAPHORES = (["sv", "sa", "sp", "sg", "sent", "feed0", "feed1", "ag0", "ag1", "dal", "dft", "dut", "dhb", "dhn", "dmon", "dout"]
-              + ["ea%d" % t for t in range(RO)])
+              + ["%s%d" % (k, t) for k in ("ea", "eb") for t in range(RO)])
 PSUM = ("U0", "U1", "U2", "U3", "PA", "PB", "PC", "PD")
 
 
 def _senders(core, topo):
-    out, seen = [core], {topo.addr(core)[2]}
+    out, seen = [core], set()
     for c in topo.cores_of(core):
-        if topo.addr(c)[2] not in seen:
+        if topo.die(c) != topo.die(core) and topo.addr(c)[2] not in seen:
             seen.add(topo.addr(c)[2])
             out.append(c)
     return out
 
 
 def _piece(T, part, q, i, n):
-    c0 = part * HO + q * V
-    return T.C[:, c0 + (n - 1) * PW:c0 + V] if i == 0 else T.C[:, c0 + (i - 1) * PW:c0 + i * PW]
+    c0, w = part * HO + q * V, PW[part]
+    return T.C[:, c0 + (n - 1) * w:c0 + V] if i == 0 else T.C[:, c0 + (i - 1) * w:c0 + i * w]
 
 
 def _mask(engs):
@@ -68,26 +71,64 @@ def _mask(engs):
     return m
 
 
+def _engines(T, topo, core, dst):
+    eng = topo.engines(core, dst)
+    if topo.chip(core) == topo.chip(dst):
+        far = topo.engines(core, [c for c in T.cores if topo.chip(c) != topo.chip(core)][0])
+        eng = [e for e in eng if e not in far]
+        return eng, len(eng) // 2
+    return eng, len(eng) // 4
+
+
 def _spread(g, T, topo, core, dsts, srcs, outs, sem):
-    eng = topo.engines(core, dsts[0])
-    k = len(eng) // 4
+    eng, k = _engines(T, topo, core, dsts[0])
     tr = []
     for i, d in enumerate(dsts):
         rid, pid, _ = topo.addr(d)
         tr.append(RemoteDMATransfer(dst_ids=[DstId(rid=rid, pnc=pid)], dma_engine_mask=_mask(eng[len(eng) - k * (i + 1):len(eng) - k * i]),
                                     remote_sem=sem, src=srcs[i], dst=outs[i]))
     g.remote_dma_fused(tr, local_sem=T.sem["sent"])
-    return k
 
 
 def helper_program(g, core, T, topo, q, piece, n):
     peers = [T.cores[(q + 1 + i) % N] for i in range(N - 1)]
-    sent = 0
     for part in range(2):
-        g.wait_ge(T.sem["feed%d" % part], len(topo.engines(T.cores[q], core)) // 4)
+        g.wait_ge(T.sem["feed%d" % part], _engines(T, topo, T.cores[q], core)[1])
         ap = _piece(T, part, q, piece, n)
-        sent += 4 * _spread(g, T, topo, core, peers, [ap] * 4, [ap] * 4, T.sem["ag%d" % part])
-    g.wait_ge(T.sem["sent"], sent)
+        _spread(g, T, topo, core, peers, [ap] * 4, [ap] * 4, T.sem["ag%d" % part])
+    g.wait_ge(T.sem["sent"], 2 * 4 * (len(topo.engines(core, peers[0])) // 4))
+
+
+def _order(nodes):
+    n = len(nodes)
+    eng, cost, lat = [[x[k] for x in nodes] for k in ("e", "cost", "lat")]
+    nxt = [[] for _ in nodes]
+    for i in range(n):
+        for j in nodes[i]["pre"]:
+            nxt[j].append(i)
+
+    def gap(i, j):
+        return HOP if eng[i] != eng[j] else SELF if i in nodes[j]["wait"] and eng[i] != "p" else 0.0
+
+    left, start = [len(x["pre"]) for x in nodes], [0.0] * n
+    ready, free, out = {}, {}, []
+    for i in range(n):
+        if not left[i]:
+            ready.setdefault(eng[i], []).append(i)
+    for _ in range(n):
+        t0, e = min((max(free.get(e, 0.0), min(start[i] for i in r)), e) for e, r in ready.items() if r)
+        i = min(i for i in ready[e] if start[i] <= t0)
+        j = min(j for j in ready[e] if start[j] <= t0 + WAIT * cost[i])
+        i, t0 = j, max(t0, start[j])
+        ready[e].remove(i)
+        out.append(i)
+        free[e] = t0 + cost[i]
+        for j in nxt[i]:
+            start[j] = max(start[j], t0 + cost[i] + lat[i] + gap(i, j))
+            left[j] -= 1
+            if not left[j]:
+                ready.setdefault(eng[j], []).append(j)
+    return out
 
 
 def rank_program(g, core, T, topo):
@@ -101,122 +142,119 @@ def rank_program(g, core, T, topo):
     peers = [T.cores[(me + 1 + i) % N] for i in range(N - 1)]
     KE = len(topo.engines(core, peers[0])) // 4
     Q = {"v": g.vector, "a": g.scalar, "p": g.tensor, "g": g, "s": g.sync}
-    cnt = {"v": 0, "a": 0, "p": 0, "g": 0}
-    seen = {k: {} for k in Q}
-    wr, rd, total = {}, {}, {}
+    v, a, p = g.vector, g.scalar, g.tensor
+    nodes, wr, rd, total, group, first = [], {}, {}, {}, [], [0.0]
 
-    def need(e, dep):
-        sem, val, src = dep
-        if src == "p" and e == "p":
+    def node(e, fn, cost, R, Wr, lat=0.0, sem=None):
+        if group:
+            n = group[0]
+            n["e"], n["cost"] = e, n["cost"] + cost
+            n["calls"].append(fn)
             return
-        if seen[e].get(sem, 0) < val:
-            Q[e].wait_ge(T.sem[sem], val)
-            seen[e][sem] = val
-
-    def deps(e, R, Wr):
-        ds = []
+        pre = set()
+        after = [i for k in Wr if k[0] == "~" for i in wr.get(k, [])]
         for k in R:
-            ds += wr.get(k, [])
+            pre.update(wr.get(k, []))
             if k in PSUM:
-                ds += [d for d in rd.get(k, []) if d[2] != e]
+                pre.update(i for i in rd.get(k, []) if nodes[i]["e"] != e)
         for k in Wr:
-            ds += wr.get(k, []) + rd.get(k, [])
-        best = {}
-        for d in ds:
-            if d[0] not in best or best[d[0]][1] < d[1]:
-                best[d[0]] = d
-        for d in best.values():
-            need(e, d)
-
-    def note(me_dep, R, Wr):
+            if k[0] != "~":
+                pre.update(wr.get(k, []) + rd.get(k, []))
         for k in R:
-            rd.setdefault(k, []).append(me_dep)
+            rd.setdefault(k, []).append(len(nodes))
         for k in Wr:
-            wr[k] = [me_dep]
-            rd[k] = []
+            wr[k], rd[k] = [len(nodes)], []
+        nodes.append({"e": e, "calls": fn if isinstance(fn, list) else [fn], "cost": cost, "lat": lat, "pre": sorted(pre.union(after)),
+                      "wait": pre, "sem": sem, "first": first[0]})
 
-    def op(e, fn, R, Wr, inc=True):
-        deps(e, R, Wr)
-        ins = fn()
-        if inc:
-            cnt[e] += 1
-            ins.then_inc(T.sem["s" + e], 1)
-            note(("s" + e, cnt[e], e), R, Wr)
-        else:
-            note(("s" + e, cnt[e] + 1, e), R, Wr)
+    def block(body, R, Wr):
+        group.append({"cost": 0.0, "calls": []})
+        body()
+        n = group.pop()
+        node(n["e"], n["calls"], n["cost"], R, Wr)
 
-    def dma(e, out, in_, sem, R, Wr, final=None):
-        deps(e, R, Wr)
-        Q[e].dma_start(out, in_).then_inc(T.sem[sem], 16)
-        total[sem] = total.get(sem, 0) + 16
-        note((sem, final or total[sem], "dma"), R, Wr)
+    def size(ap):
+        return math.prod(ap.shape[1:])
+
+    def vcost(ap, c):
+        return FIX + CYC * c * size(ap)
+
+    def dma(e, out, in_, sem, R, Wr, final=16):
+        total[sem] = final
+        node(e, lambda: Q[e].dma_start(out, in_).then_inc(T.sem[sem], 16), 0.1, R, Wr, lat=2.2, sem=(sem, final))
 
     def send(dsts, srcs, outs, sem, R):
-        deps("g", R, [])
-        k = _spread(g, T, topo, core, dsts, srcs, outs, T.sem[sem])
-        total["sent"] = total.get("sent", 0) + k * len(dsts)
+        total["sent"] = total.get("sent", 0) + _engines(T, topo, core, dsts[0])[1] * len(dsts)
+        node("g", lambda: _spread(g, T, topo, core, dsts, srcs, outs, T.sem[sem]), 0.9, R, ["sent"], sem=())
 
-    def arrive(key, sem, val):
-        wr.setdefault(key, []).append((sem, val, "net"))
+    def arrive(key, sem, val, cost):
         total[sem] = val
+        node("link", [], cost, ["sent"], [key], lat=1.5, sem=(sem, val))
+        rd["sent"] = []
 
-    v, a, p = g.vector, g.scalar, g.tensor
-
-    def ts(out, in0, s1, o0, R, Wr, s2=None, o1=None):
+    def ts(out, in0, s1, o0, R, Wr, s2=None, o1=None, c=1.0):
         if o1 is None:
-            op("v", lambda: v.tensor_scalar(out, in0, s1, None, o0), R, Wr)
+            node("v", lambda: v.tensor_scalar(out, in0, s1, None, o0), vcost(out, c), R, Wr)
         else:
-            op("v", lambda: v.tensor_scalar(out, in0, s1, s2, o0, o1), R, Wr)
+            node("v", lambda: v.tensor_scalar(out, in0, s1, s2, o0, o1), vcost(out, c), R, Wr)
 
-    def tt(out, in0, in1, o, R, Wr):
-        op("v", lambda: v.tensor_tensor(out, in0, in1, o), R, Wr)
+    def tt(out, in0, in1, o, R, Wr, c=1.0):
+        node("v", lambda: v.tensor_tensor(out, in0, in1, o), vcost(out, c), R, Wr)
 
-    def cp(out, in_, R, Wr):
-        op("v", lambda: v.tensor_copy(out, in_), R, Wr)
+    def cp(out, in_, R, Wr, c=1.0):
+        node("v", lambda: v.tensor_copy(out, in_), vcost(out, c), R, Wr)
+
+    def scatter(win, off, in_, R, Wr):
+        node("v", lambda: v.tensor_copy(win.indirect(off), in_), vcost(in_, 3.8), R, Wr)
 
     def ms(out, c, Wr):
-        op("v", lambda: v.memset(out, c), [], Wr)
+        node("v", lambda: v.memset(out, c), vcost(out, 0.5), [], Wr)
 
-    def scan(out, d0, d1, init, o0, o1, R, Wr):
-        op("v", lambda: v.tensor_tensor_scan(out, d0, d1, init, o0, o1), R, Wr)
+    def scan(out, d0, d1, init, o0, o1, R, Wr, c=1.0):
+        node("v", lambda: v.tensor_tensor_scan(out, d0, d1, init, o0, o1), vcost(out, c), R, Wr)
 
-    def act(out, in_, R, Wr, func=AF.Copy, **kw):
-        op("a", lambda: a.activation(out, in_, func, **kw), R, Wr)
+    def act(out, in_, R, Wr, func=AF.Copy, c=1.0, **kw):
+        node("a", lambda: a.activation(out, in_, func, **kw), 0.065 + CYC * c * size(out), R, Wr)
 
-    def mm(out, lhsT, rhs, st, sp, R, Wr, inc=None):
-        op("p", lambda: p.matmul(out, lhsT, rhs, st, sp), R, Wr, inc=sp if inc is None else inc)
+    def mm(out, lhsT, rhs, st, sp, R, Wr, c=1.0):
+        node("p", lambda: p.matmul(out, lhsT, rhs, st, sp), 0.55 * CYC * c * max(64, size(out)), R, Wr)
 
-    def sel16(out, rhs_of, R, Wr, first=True, mat=T.SEL):
-        for r in range(16):
-            mm(out, mat[:, 16 - r:144 - r], rhs_of(r), first and r == 0, r == 15, R + ["SEL"], Wr)
+    def sel16(out, rhs_of, R, Wr, st=True, sp=True, mat=T.SEL[:, 0, :], c=1.0):
+        block(lambda: [mm(out, mat[:, 16 - r:144 - r], rhs_of(r), st and r == 0, sp and r == 15, [], [], c=c) for r in range(16)], R + ["SEL"], Wr)
 
     def iota(out, pat, base, cm, Wr, small=True):
         if small:
-            op("g", lambda: g.iota(out, pat, base, cm, allow_small_or_imprecise_dtypes=True), [], Wr)
+            node("g", lambda: g.iota(out, pat, base, cm, allow_small_or_imprecise_dtypes=True), 0.13 + 2 * CYC * size(out), [], Wr)
         else:
-            op("g", lambda: g.iota(out, pat, base, cm), [], Wr)
+            node("g", lambda: g.iota(out, pat, base, cm), 0.13 + 2 * CYC * size(out), [], Wr)
 
+    GA = 1.56
     C, IO, TMP = T.C, T.IOTA, T.TMP
     Aw, Hw = C[:, 0:HO], C[:, HO:DO]
-    REL, BLK, IDN, D2M, NUP, NL1, NL2, B4K, B9, BN24, BN8, B05, I8K, BNC, TM2 = [T.MAT[:, i, :] for i in range(15)]
+    REL, BLK, IDN, D2M, NUP, NL1, NL2, B4K, B9, BN24, BN8, B05, I8K, BNC, TM2, BCP, B2K = [T.MAT[:, i, :] for i in range(17)]
+    SEL, SELK, SELN = [T.SEL[:, i, :] for i in range(3)]
     BLKH, IDNH = T.MATH[:, 0, :], T.MATH[:, 1, :]
     rcol, g16, ebias, c192, pw4f, r0, rh = [T.cF[:, i:i + 1] for i in range(7)]
     pw4 = T.cB[:, 0:1]
     J16, JB, DUM, JD = [T.JT[:, i, :] for i in range(4)]
-    invL, xI, fl, xo, lm, la, lb = [T.lf[:, i, :] for i in range(7)]
+    invL, la, lb, lc = [T.lf[:, i, :] for i in range(4)]
     ao, ho = me * V, HO + me * V
     name0 = me * B + 1
     Ar, Hr = ["A", "Aown", "Aown2", "Az", "C"], ["H", "Hown", "Hz", "C"]
+    Gk, Ek, Mk = [["%s%d" % (s, c) for c in range(len(CHUNKS))] for s in ("G", "E", "MX")]
+    Tk = ["TOP%d" % k for k in range(16)]
+    jk = ["junk%d" % m for m in range(NA, 16, 2)]
+    TRIM = T.PD[:, L:2 * L]
 
     def holdings():
-        sel16(T.PC[:, 0:64], lambda r: T.XR[:, r:B:16], ["XR", "SELF"], ["PC"], mat=T.SELF)
+        sel16(T.PC[:, 0:64], lambda r: T.XR[:, r:B:16], ["XR", "SELF"], ["PC"], mat=T.SELF, c=4.0)
         cp(T.HL[:], T.PC[:, 0:64], ["PC"], ["HL"])
 
-    def check(w0):
+    def check(w0, nv=T.NV, k="NV"):
         h = w0 or B // 2
         e0 = B - h if w0 else 0
-        tt(T.EQ[:, (h - w0) % B:(h - w0) % B + B - h], Hw.indirect(T.HL[:, h // 16:64]), T.NV[:, h:B], Op.is_equal, Hr + ["HL", "NV"], ["EQ0"])
-        tt(T.EQ[:, e0:e0 + h], Hw.indirect(T.HL[:, 0:h // 16]), T.NV[:, 0:h], Op.is_equal, Hr + ["HL", "NV"], ["EQ1"])
+        tt(T.EQ[:, (h - w0) % B:(h - w0) % B + B - h], Hw.indirect(T.HL[:, h // 16:64]), nv[:, h:B], Op.is_equal, Hr + ["HL", k], ["EQ0"], c=GA)
+        tt(T.EQ[:, e0:e0 + h], Hw.indirect(T.HL[:, 0:h // 16]), nv[:, 0:h], Op.is_equal, Hr + ["HL", k], ["EQ1"], c=GA)
 
     h = V // 2
     dma("s", C[:, ao:ao + h], T.al[:, 0:h], "dal", [], ["Aown"], final=32)
@@ -228,25 +266,23 @@ def rank_program(g, core, T, topo):
     dma("s", T.TX[:, B:TW], T.ft[:, 0:TW - B], "dft", [], ["TX2"], final=32)
     dma("s", T.TU[:, 0:B], T.ut[:], "dut", [], ["TU"], final=32)
     dma("s", T.TU[:, B:TW], T.ut[:, 0:TW - B], "dut", [], ["TU2"], final=32)
-    dma("s", T.monb[:], T.mon[:], "dmon", [], ["monb"])
+    dma("s", T.monb[:], T.mon[:], "dmon", ["hnI"], ["monb"])
 
     iota(T.cI[:, 0:1], [[0, 1]], 0, 1, ["cI"], small=False)
     iota(TMP[:], [[1, 144]], 0, 0, ["TMP"])
     iota(T.C16[:], [[0, 16], [1, 16]], 0, 0, ["C16"])
     snd = _senders(core, topo)
-
-    def gather_all(part, R):
-        pc = [_piece(T, part, me, i, len(snd)) for i in range(len(snd))]
-        send(snd[1:], pc[1:], pc[1:], "feed%d" % part, R)
-        send(peers, [pc[0]] * 4, [pc[0]] * 4, "ag%d" % part, [])
-
-    gather_all(0, ["Aown", "Aown2"])
+    pcs = [[_piece(T, part, me, i, len(snd)) for i in range(len(snd))] for part in range(2)]
+    send(snd[1:], pcs[0][1:], pcs[0][1:], "feed0", ["Aown", "Aown2"])
+    send(peers, [pcs[0][0]] * 4, [pcs[0][0]] * 4, "ag0", [])
+    arrive("A", "ag0", 4 * len(snd) * KE, 12.0)
     iota(IO[:, 0:B], [[1, B]], 0, 0, ["IO"])
+    iota(IO[:, B:TW], [[1, TW - B]], 0, 0, ["IO2"])
 
     ts(T.cI[:, 1:2], T.cI[:, 0:1], 15, Op.bitwise_and, ["cI"], ["cI1"])
     ts(T.cI[:, 2:3], T.cI[:, 0:1], 112, Op.bitwise_and, ["cI"], ["cI2"])
-    ms(T.ONE[:], 1.0, ["ONE"])
     cp(T.cF[:, 0:2], T.cI[:, 1:3], ["cI1", "cI2"], ["cF"])
+    ms(T.ONE[:], 1.0, ["ONE"])
     ms(C[:, W:HO], 0.0, ["Az"])
     ms(C[:, HO + W:DO], 1.0, ["Hz"])
     ts(REL, TMP[:, 0:128], g16, Op.subtract, ["TMP", "cF"], ["REL"])
@@ -256,60 +292,60 @@ def rank_program(g, core, T, topo):
     ts(BLK, REL, 16.0, Op.is_lt, ["REL"], ["BLK"])
     ts(T.EK[:], TMP[:, 0:16], rcol, Op.is_equal, ["TMP", "cF"], ["EK"])
     tt(BLK, BLK, TM2, Op.mult, ["TM2", "BLK"], ["BLK"])
-    act(pw4, rcol, ["cF"], ["pw4"], func=AF.Exp, scale=-math.log(4.0))
+    act(pw4, rcol, ["cF"], ["pw4"], func=AF.Exp, scale=-math.log(4.0), c=1500.0)
     hf, ab, c1, c2 = T.G[:, 0:V], T.MX[:, 0:V], T.TOP[:, 0:V], T.TOP[:, B:B + V]
-    cp(hf, T.hnI[:], ["hnI"], ["G0", "G512"])
+    cp(hf, T.hnI[:], ["hnI"], Gk)
     ts(c1, T.hnI[:], 0.5, Op.is_gt, ["hnI"], ["TOP0"], -float(TAG), Op.mult)
     ts(c2, T.hnI[:], N * B + 0.5, Op.is_gt, ["hnI"], ["TOP1"], -6.0 * TAG, Op.mult)
-    act(ab, hf, ["G0", "G512"], ["MX0", "MX512"], func=AF.Abs)
+    act(ab, hf, Gk, Mk, func=AF.Abs)
     for c0, c9, k in ((0, 512, "U2"), (512, V, "U3")):
         mm(T.PU1[:, c0:c9], IDN, T.TOP[:, c0:c9], True, False, ["TOP0", "IDN"], [k])
         mm(T.PU1[:, c0:c9], IDN, T.TOP[:, B + c0:B + c9], False, True, ["TOP1"], [k])
-    ts(T.SEL[:], TMP[:], -16.0, Op.add, ["TMP", "cF"], ["SEL"], g16, Op.is_equal)
+    tt(C[:, ho:ho + V], T.PU1[:, 0:V], ab, Op.subtract, ["U2", "U3"] + Mk, ["Hown"])
+    send(snd[1:], pcs[1][1:], pcs[1][1:], "feed1", ["Hown"])
+    send(peers, [pcs[1][0]] * 4, [pcs[1][0]] * 4, "ag1", ["A"])
+    arrive("H", "ag1", 4 * len(snd) * KE, 7.0)
+    ts(SEL, TMP[:], -16.0, Op.add, ["TMP", "cF"], ["SEL"], g16, Op.is_equal)
     ts(r0, rcol, 0.0, Op.is_equal, ["cF"], ["r0"])
     ts(rh, rcol, 0.5, Op.mult, ["cF"], ["rh"])
     cp(T.XR[:, 0:B], T.XI[:], ["XI"], ["XR"])
-    ts(T.SELF[:], T.SEL[:], r0, Op.mult, ["SEL", "r0"], ["SELF"])
-    tt(C[:, ho:ho + V], T.PU1[:, 0:V], ab, Op.subtract, ["U2", "U3", "MX0", "MX512"], ["Hown"])
-    gather_all(1, ["Hown"])
-    iota(IO[:, B:TW], [[1, TW - B]], 0, 0, ["IO2"])
-    for k in range(16):
-        act(T.BRD[:, k, :], BLK, ["BLK", "EK"], ["BRD"] if k == 15 else [], scale=T.EK[:, k:k + 1])
+    ts(T.SELF[:], SEL, r0, Op.mult, ["SEL", "r0"], ["SELF"])
+    block(lambda: [act(T.BRD[:, k, :], BLK, [], [], scale=T.EK[:, k:k + 1]) for k in range(16)], ["BLK", "EK"], ["BRD"])
     ts(NUP, REL, rcol, Op.is_lt, ["REL"], ["NUP"], -1.0, Op.mult)
-    ms(T.RS64[:], 1.0, ["RS64"])
-    ms(T.RST[:], 1.0, ["RST"])
     tt(NUP, NUP, BLK, Op.mult, ["NUP", "BLK"], ["NUP"])
-    ms(T.RS64[:, 0:448:64], 0.0, ["RS64"])
+    ms(T.RS64[:], 1.0, ["RS64"])
+    ms(T.RS64[:, 0:B:64], 0.0, ["RS64"])
+    ms(T.RST[:], 1.0, ["RST"])
     ms(T.RST[:, 0:B:16], 0.0, ["RST"])
     ts(J16, TMP[:, 0:16], 16.0, Op.mult, ["TMP", "cF"], ["J16"], rcol, Op.add)
-    holdings()
     ts(JB, J16, 0.5, Op.add, ["J16"], ["JB"])
+    holdings()
     ts(T.hz[:], T.PC[:, 0:64], W - 0.5, Op.is_lt, ["PC"], ["hz"])
-
-    def late_start(part):
-        if part == 0:
-            ts(D2M, IDN, 2.0, Op.mult, ["IDN"], ["D2M"])
-            ts(c192, rcol, 192.0, Op.add, ["cF"], ["c192"])
-            tt(D2M, D2M, BLK, Op.subtract, ["D2M", "BLK"], ["D2M"])
-            ts(DUM, J16, float(DO), Op.add, ["J16"], ["DUM"])
-            ts(JD, J16, float(B), Op.add, ["J16"], ["JD"])
-            ts(T.JH[:], J16, 16.0, Op.mult, ["J16"], ["JH"], 60.0, Op.add)
-            cp(T.SELH[:], T.SEL[:], ["SEL"], ["SELH"])
-            ts(T.SELK[:], T.SEL[:], rh, Op.mult, ["SEL", "rh"], ["SELK"])
-            cp(BLKH, BLK, ["BLK"], ["BLKH"])
-            cp(IDNH, IDN, ["IDN"], ["IDNH"])
-            ts(T.TRIM[:], T.C16[:], rcol, Op.is_gt, ["C16", "cF"], ["TRIM"])
-            ts(T.SG[:, 0, :], TMP[:, 0:8], rcol, Op.is_lt, ["TMP", "cF"], ["SG0"], 2.0, Op.mult)
-            ts(T.SG[:, 0, :], T.SG[:, 0, :], -1.0, Op.add, ["SG0"], ["SG0"])
-            ts(T.SG[:, 1, :], T.SG[:, 0, :], -0.0625, Op.mult, ["SG0"], ["SG1"])
-        if part == 1:
-            act(pw4f, pw4, ["pw4"], ["pw4f"], scale=-(2.0 ** 80))
-            act(NL1, D2M, ["D2M", "pw4f"], ["NL1"], scale=pw4f)
-            act(NL2, NL1, ["NL1"], ["NL2"], scale=2.0 ** -32)
-            for m, c in ((B4K, TAG / 2), (B9, -9.0 * TAG / 16), (BN24, -(2.0 ** 24)), (BN8, -float(TAG)), (B05, 0.5), (BNC, -12.0 * TAG)):
-                act(m, BLK, ["BLK"], ["BX"], scale=c)
-            act(I8K, IDN, ["IDN"], ["BX"], scale=float(TAG))
-            act(T.NV[:, 0:B], IO[:, 0:B], ["IO"], ["NV"], func=AF.Identity, scale=-1.0, bias=-float(TAG + name0))
+    ts(D2M, IDN, 2.0, Op.mult, ["IDN"], ["D2M"])
+    ts(c192, rcol, 192.0, Op.add, ["cF"], ["c192"])
+    tt(D2M, D2M, BLK, Op.subtract, ["D2M", "BLK"], ["D2M"])
+    ts(DUM, J16, float(DO), Op.add, ["J16"], ["DUM"])
+    ts(JD, J16, float(B), Op.add, ["J16"], ["JD"])
+    ts(T.JH[:], J16, 16.0, Op.mult, ["J16"], ["JH"], 60.0, Op.add)
+    cp(T.SELH[:], SEL, ["SEL"], ["SELH"])
+    ts(SELK, SEL, rh, Op.mult, ["SEL", "rh"], ["SELK"])
+    ts(SELN, SEL, -HO / 2, Op.mult, ["SEL"], ["SELN"])
+    cp(BLKH, BLK, ["BLK"], ["BLKH"])
+    cp(IDNH, IDN, ["IDN"], ["IDNH"])
+    cp(T.IDNF[:], IDN, ["IDN"], ["IDNF"])
+    ts(TRIM, T.C16[:], rcol, Op.is_gt, ["C16", "cF"], ["PD"])
+    ts(T.SG[:, 0, :], TMP[:, 0:8], rcol, Op.is_lt, ["TMP", "cF"], ["SG0"], 2.0, Op.mult)
+    ts(T.SG[:, 0, :], T.SG[:, 0, :], -1.0, Op.add, ["SG0"], ["SG0"])
+    ts(T.SG[:, 1, :], T.SG[:, 0, :], -0.0625, Op.mult, ["SG0"], ["SG1"])
+    act(pw4f, pw4, ["pw4"], ["pw4f"], scale=-(2.0 ** 80))
+    act(NL1, D2M, ["D2M", "pw4f"], ["NL1"], scale=pw4f)
+    act(NL2, NL1, ["NL1"], ["NL2"], scale=2.0 ** -32)
+    block(lambda: [act(m, BLK, [], [], scale=c) for m, c in (
+        (B4K, TAG / 2), (B9, -9.0 * TAG / 16), (BN24, -(2.0 ** 24)), (BN8, -float(TAG)), (B05, 0.5), (BNC, -12.0 * TAG), (BCP, -(CAP + 0.5) / 16),
+        (B2K, HO / 2))], ["BLK"], ["BX"])
+    act(I8K, IDN, ["IDN"], ["I8K"], scale=float(TAG))
+    act(T.NV[:, 0:B], IO[:, 0:B], ["IO"], ["NV"], func=AF.Identity, scale=-1.0, bias=-float(name0))
+    act(T.NV1[:], IO[:, 0:B], ["IO"], ["NV1"], func=AF.Identity, scale=-1.0, bias=-float(TAG + name0))
 
     for t in range(RO):
         w0 = (L * t) % B
@@ -323,173 +359,179 @@ def rank_program(g, core, T, topo):
         scan(T.inc[:], T.ONE[:, 0:64], hz, 0.0, Op.add, Op.subtract, [hk, "ONE"], ["inc"])
         ts(T.hl[:], hz, 0.5, Op.is_lt, [hk], ["hl"])
         mm(T.PA[:, 0:64], BLK, T.inc[:], True, True, ["inc", "BLK"], ["PA"])
-        mm(T.PD[:, 0:64], BLK, T.inc[:], True, True, ["inc"], ["PD"])
+        mm(T.PD[:, 0:64], BLK, T.inc[:], True, True, ["inc", "BLK"], ["PD"])
+        mm(T.PB[:, 64:65], BLK, T.inc[:, 63:64], True, True, ["inc", "BLK"], ["PB"])
         mm(T.PB[:, 0:64], BLK, T.inc[:], True, False, ["inc"], ["PB"])
-        mm(T.PB[:, 0:64], NUP, T.hl[:], False, True, ["hl", "NUP"], ["PB"], inc=False)
-        mm(T.PB[:, 64:65], BLK, T.inc[:, 63:64], True, True, ["inc"], ["PB"])
-        for m in range(NA):
-            act(T.junk[:, 64 * m:64 * m + 64], T.PA[:, 0:64], ["PA", "JB"], ["acc"] if m in (0, NA - 1) else [], func=AF.Sign, scale=-1.0, bias=JB[:, m:m + 1],
-                accum_out=T.acc[:, m:m + 1])
-        for m in range(NA, 16):
-            ts(T.junk[:, 64 * m:64 * m + 64], T.PD[:, 0:64], JB[:, m:m + 1], Op.is_lt, ["PD", "JB"], ["junk"] if m in (NA, 15) else [])
+        mm(T.PB[:, 0:64], NUP, T.hl[:], False, True, ["hl", "NUP"], ["PB"])
         cp(T.P[:, 0:65], T.PB[:, 0:65], ["PB"], ["P"])
-        nb = 64 * (16 - NA)
-        scan(T.cs[:, 0:nb], T.RS64[:, 0:nb], T.junk[:, 64 * NA:1024], 0.0, Op.mult, Op.add, ["junk", "RS64"], ["cs"])
+        for m0, m1, s, ps, k in ((0, M0, "0", T.PC[:, 64:80], "PC"), (M0, 16, "1", T.PB[:, 80:96], "PB")):
+            c, ma = slice(16 * m0, 16 * m1), min(m1, NA)
+            block(lambda: [act(T.junk[:, 64 * m:64 * m + 64], T.PA[:, 0:64], [], [], func=AF.Sign, scale=-1.0, bias=JB[:, m:m + 1], c=1.4,
+                               accum_out=T.acc[:, m:m + 1]) for m in range(m0, ma)], ["PA", "JB"], ["acc" + s])
+            if m0:
+                for m in range(NA, 16, 2):
+                    block(lambda: [ts(T.junk[:, 64 * x:64 * x + 64], T.PD[:, 0:64], JB[:, x:x + 1], Op.is_lt, [], [], 16.0, Op.mult) for x in (m, m + 1)],
+                          ["PD", "JB"], ["junk%d" % m])
+                scan(T.cs[:, 64 * NA:B], T.RS64[:, 64 * NA:B], T.junk[:, 64 * NA:B], 0.0, Op.mult, Op.add, jk + ["RS64"], ["cs"], c=0.5)
+                ts(T.cL[:, NA:16], T.cs[:, 64 * NA + 63:B:64], 0.0625, Op.mult, ["cs"], ["cL2"])
+            ts(T.cL[:, m0:ma], T.acc[:, m0:ma], 64.0, Op.add, ["acc" + s], ["cL" + s], 0.5, Op.mult)
+            tt(T.cmp[:, c], T.P[:, 0:65].indirect(T.cL[:, m0:m1]), IO[:, c], Op.is_le, ["P", "IO", "cL" + s] + ["cL2"] * m0, ["cmp" + s], c=GA)
+            ts(T.cs[:, 64 * m0 + 63:64 * ma:64], T.acc[:, m0:ma], 64.0, Op.add, ["acc" + s], ["cs" + s], 8.0, Op.mult)
+            sel16(ps[:, m0:m1], lambda r: T.cmp[:, 16 * m0 + r:16 * m1:16], ["cmp" + s], [k], sp=False)
+            mm(ps[:, m0:m1], IDN, T.cs[:, 64 * m0 + 63:64 * m1:64], False, True, ["cs" + s, "IDN"] + ["cs"] * m0, [k])
+            cp(T.bL[:, m0:m1], ps[:, m0:m1], [k], ["bL" + s])
+            cp(T.FO[:, c], T.TX[:, win].indirect(T.bL[:, m0:m1]), ["TX", "TX2", "bL" + s], ["FO" + s], c=GA)
+            act(T.ug[:, c], T.TU[:, win].indirect(T.bL[:, m0:m1]), ["TU", "TU2", "bL" + s], ["ug" + s], c=GA)
+        def largest(ci):
+            c = slice(16 * CHUNKS[ci][0], 16 * (CHUNKS[ci][0] + CHUNKS[ci][1]))
+            scan(T.MX[:, c], T.RST[:, 0:16 * CHUNKS[ci][1]], T.E[:, c], 0.0, Op.mult, Op.max, [Ek[ci], "RST"], [Mk[ci]])
+
+        for ci, (j0, nj, b0) in enumerate(CHUNKS):
+            c = slice(16 * j0, 16 * (j0 + nj))
+            pu = (T.PU0, T.PU1)[b0 // 2][:, 512 * (b0 % 2):512 * (b0 % 2) + 16 * nj]
+            banks = ["U%d" % (b0 + i) for i in range((nj + 31) // 32)]
+            s = "0" if j0 < 16 * M0 else "1"
+            act(T.G[:, c], Aw.indirect(T.FO[:, j0:j0 + nj]), Ar + ["FO" + s], [Gk[ci], "~G"], func=AF.Abs, c=GA)
+            for i, k0 in enumerate(banks):
+                n1 = min(32, nj - 32 * i)
+                block(lambda: [mm(pu[:, 512 * i + k:512 * i + 16 * n1:16], T.BRD[:, k, :], T.ug[:, j0 + 32 * i:j0 + 32 * i + n1], True, True, [], [])
+                               for k in range(16)], ["ug" + s, "BRD"], [k0])
+            tt(T.E[:, c], T.G[:, c], pu, Op.mult, [Gk[ci]] + banks, [Ek[ci]])
+            if ci:
+                largest(ci - 1)
+        largest(len(CHUNKS) - 1)
+        jl = CHUNKS[-1][0]
+        act(T.PB[:, 0:jl], T.MX[:, 15:16 * jl:16], Mk[:-1], ["PB"])
+        cp(T.PB[:, jl:L], T.MX[:, 16 * jl + 15:16 * L:16], Mk[-1:], ["PB"])
+        ts(T.xc[:], T.FO[:], -float(MID), Op.add, ["FO0", "FO1"], ["xc"], c=0.5)
         ts(invL, J16, T.P[:, 64:65], Op.is_ge, ["J16", "P"], ["invL"], 2.0 * TAG, Op.mult)
-        cp(T.cL[:, NA:16], T.cs[:, 63:nb:64], ["cs"], ["cL2"])
-        ts(T.c16[:, NA:16], T.cs[:, 63:nb:64], 16.0, Op.mult, ["cs"], ["c162"])
-        ts(T.cL[:, 0:NA], T.acc[:, 0:NA], 64.0, Op.add, ["acc"], ["cL"], 0.5, Op.mult)
-        ts(T.c16[:, 0:NA], T.acc[:, 0:NA], 64.0, Op.add, ["acc"], ["c16"], 8.0, Op.mult)
-        tt(T.cmp[:], T.P[:, 0:65].indirect(T.cL[:]), IO[:, 0:L], Op.is_le, ["P", "cL", "cL2", "IO"], ["cmp"])
-        mm(T.PA[:, 0:16], IDN, T.c16[:], True, False, ["c16", "c162", "IDN"], ["PA"])
-        sel16(T.PA[:, 0:16], lambda r: T.cmp[:, r:L:16], ["cmp"], ["PA"], first=False)
-        cp(T.bL[:], T.PA[:, 0:16], ["PA"], ["bL"])
-        act(T.ug[:], T.TU[:, win].indirect(T.bL[:]), ["TU", "TU2", "bL"], ["ug"])
-        cp(T.FO[:], T.TX[:, win].indirect(T.bL[:]), ["TX", "TX2", "bL"], ["FO"])
-        ts(T.li[:, 0, :], T.bL[:], float(w0), Op.add, ["bL"], ["li0"])
-        ts(T.xc[:], T.FO[:], -float(MID), Op.add, ["FO"], ["xc"])
+        act(T.nv[:], IO[:, win].indirect(T.bL[:]), ["IO", "IO2", "bL0", "bL1"], ["nv"], func=AF.Identity, scale=-1.0, bias=-float(TAG * (t + 2) + name0), c=GA)
+        for k in range(16):
+            tt(T.TOP[:, k:4096:16], T.E[:, k:4096:16], T.PB[:, 0:L], Op.is_equal, Ek + ["PB"], [Tk[k]])
+            mm(T.PA[:, 0:L], SEL[:, 16 - k:144 - k], T.TOP[:, k:4096:16], k == 0, k == 15, [Tk[k], "SEL"], ["PA"])
+        D1, OH, D2, TK = T.PC[:, 0:L], T.PC[:, L:2 * L], T.PD[:, 0:L], T.PD[:, 0:16]
+        XV, XS, XP, TH = T.PU0[:, 0:L], T.PU0[:, 512:512 + L], T.PU1[:, 0:16], T.PU1[:, 512:512 + L]
+        FA, DN, RR, Y = XV, OH, T.PA[:, L:2 * L], T.PB[:, L:L + 16]
+        act(T.w[:], T.PA[:, 0:L], ["PA", "eb"], ["w"], func=AF.Exp, scale=16.0 * math.log(2.0), bias=ebias)
+        mm(D1, D2M, T.w[:], True, True, ["w", "D2M"], ["PC"])
+        mm(D2, D2M, T.w[:], True, True, ["w", "D2M"], ["PD"])
+        ts(OH, D1, 0.0, Op.is_ge, ["PC"], ["PC"])
+        act(T.sg[:], D2, ["PD"], ["sg"], func=AF.Sign)
+        tt(T.Z[:], OH, T.xc[:], Op.mult, ["PC", "xc"], ["Z"])
+        sel16(XP, lambda c: T.Z[:, c:L:16], ["Z", "SELH"], ["U2", "~x"], mat=T.SELH)
+        mm(XV, BLKH, T.Z[:], True, True, ["Z", "BLKH"], ["U0"])
+        mm(XS, BLKH, T.Z[:], True, True, ["Z", "BLKH"], ["U1"])
+        ts(T.XL[:], XP, float(MID), Op.add, ["U2"], ["XL"])
+        cp(T.Hc[:], Hw.indirect(T.XL[:]), Hr + ["XL"], ["Hc"], c=GA)
+        ts(T.xr[:], XV, float(MID), Op.add, ["U0"], ["xr"])
+        ts(T.XLf[:], XP, float(MID), Op.add, ["U2"], ["XLf"])
+        mm(TK, IDNH, T.JH[:], True, False, ["IDNH", "JH"], ["PD"])
+        sel16(TK, lambda c: T.sg[:, c:L:16], ["sg", "SELK"], ["PD", "~x"], st=False, mat=SELK)
+        cp(T.tk[:], TK, ["PD"], ["tk"])
+        act(T.SA[:], Aw.indirect(T.XL[:]), Ar + ["XL"], ["SA"], func=AF.Sign, c=GA)
+        act(T.EM[:], Hw.indirect(T.XL[:]), Hr + ["XL"], ["EM"], func=AF.Relu, bias=1.0, c=GA)
+        mm(TH, B9, T.ONE[:, 0:L], True, False, ["BX", "ONE"], ["U3"])
+        mm(TH, B4K, T.SA[:], False, True, ["SA"], ["U3"])
+        tt(T.AV[:], T.Hc[:], TH, Op.is_gt, ["Hc", "U3"], ["AV"])
+        mm(DN, BLK, T.ONE[:, 0:L], True, False, ["ONE"], ["PC"])
+        mm(DN, NL1, T.EM[:], False, False, ["EM", "NL1"], ["PC"])
+        mm(DN, NL2, T.AV[:], False, True, ["AV", "NL2"], ["PC"])
+        act(T.fc[:], T.TOP[:].indirect(T.tk[:]), ["tk", "SG0", "SG1"] + Tk, ["fc"], func=AF.Identity, scale=T.SG[:, 1, t:t + 1], bias=T.SG[:, 0, t:t + 1], c=GA)
+        act(T.AA[:], Aw.indirect(T.XL[:]), Ar + ["XL"], ["AA"], func=AF.Abs, c=GA)
+        block(lambda: [mm(FA, IDN, T.fc[:], True, False, [], []), mm(FA, BN24, T.AV[:], False, True, [], [])], ["AV", "fc"], ["U0"])
+        pl, ol = T.PL[:, t, me, :], T.OL[:, t, me, :]
+        tt(D1, DN, T.nv[:], Op.max, ["PC", "nv"], ["PC"])
+        tt(T.X[:], D1, T.Hc[:], Op.min, ["PC", "Hc"], ["X"])
+        tt(FA, FA, T.AA[:], Op.mult, ["U0", "AA"], ["U0"])
+        tt(pl, FA, T.X[:], Op.max, ["U0", "X"], ["PLo"])
+        send(peers, [pl] * 4, [pl] * 4, "ea%d" % t, ["PLo"])
+        arrive("PL", "ea%d" % t, 4 * KE, 4.0)
+        act(T.own[:], XS, ["U1"], ["own"], func=AF.Identity, scale=1.0 / V, bias=(MID + 0.5) / V + 191.5)
+        act(T.sF[:], DN, ["PC"], ["sF"], func=AF.Sign)
+        ts(T.ind[:], T.own[:], c192, Op.is_equal, ["own", "c192"], ["ind"], c=0.5)
+        mm(RR, BCP, T.ONE[:, 0:L], True, False, ["BX", "ONE"], ["PA"])
+        for m in range(16):
+            if m == 5:
+                scan(T.cn[:], T.ind[:], T.ind[:], 0.0, Op.add, Op.max, ["ind"], ["cn"], c=0.5)
+            if m == 8:
+                tt(T.q1[:], T.ind[:], T.cn[:], Op.mult, ["ind", "cn"], ["q1"])
+            ts(T.E3[:, m, 0:L - 16 * m], T.xr[:, 16 * m:L], T.XLf[:, m:m + 1], Op.is_equal, ["xr", "XLf"], ["E3%d" % m], 256.0, Op.mult, c=0.5)
+            if m < 15:
+                mm(RR[:, 16 * m + 16:L], BLK, T.E3[:, m, 16:L - 16 * m], False, False, ["E3%d" % m], ["PA"])
+        mm(RR, BLK, T.q1[:], False, False, ["q1"], ["PA"])
+        tt(T.dg[:], T.E3[:, :, 0:16], TRIM, Op.mult, ["E3%d" % m for m in range(16)] + ["PD"], ["dg"])
+        mm(RR, BLK, T.dg[:], False, True, ["dg"], ["PA"])
+        act(T.Rb[:], RR, ["PA"], ["Rb"], func=AF.Relu, scale=2048.0)
+        mm(Y, B2K, T.ONE[:, 0:16], True, False, ["BX", "ONE"], ["PB"])
+        mm(Y, T.IDNF[:], invL, False, False, ["IDNF", "invL"], ["PB"], c=4.0)
+        mm(Y, T.IDNF[:], T.XLf[:], False, False, ["XLf"], ["PB"], c=4.0)
+        sel16(Y, lambda c: T.sF[:, c:L:16], ["sF", "SELN"], ["PB"], st=False, sp=False, mat=SELN)
+        sel16(Y, lambda c: T.Rb[:, c:L:16], ["Rb"], ["PB"], st=False)
+        tt(lc, Y, DUM, Op.min, ["PB", "DUM"], ["lc"])
+        cp(ol, lc, ["lc"], ["OLo"])
+        send(peers, [ol] * 4, [ol] * 4, "eb%d" % t, ["OLo"])
+        arrive("OL", "eb%d" % t, 4 * KE, 0.5)
+        ts(T.li[:, 0, :], T.bL[:], float(w0), Op.add, ["bL0", "bL1"], ["li0"])
         ts(T.li[:, 1, :], T.li[:, 0, :], B - 1, Op.bitwise_and, ["li0"], ["li1"])
-        if t == 0:
-            late_start(0)
-            arrive("A", "ag0", 4 * len(snd) * KE)
         tt(la, T.li[:, 1, :], invL, Op.add, ["li1", "invL"], ["la"])
         tt(lb, la, JD, Op.min, ["la", "JD"], ["lb"])
         cp(T.pos[:], lb, ["lb"], ["pos"])
-        Ek = []
-        for ci, (j0, nj, s0) in enumerate(CHUNKS):
-            n = 16 * nj
-            PU = T.PU0 if s0 < B else T.PU1
-            banks = ["U%d" % (s0 // 512 + i) for i in range(n // 512)]
-            gk = ["G%d" % (s0 + 512 * i) for i in range(n // 512)]
-            mk = ["MX%d" % (s0 + 512 * i) for i in range(n // 512)]
-            act(T.G[:, s0:s0 + n], Aw.indirect(T.FO[:, j0:j0 + nj]), Ar + ["FO"], gk, func=AF.Abs)
-            if ci >= 4:
-                act(T.PB[:, j0 - 128:j0 - 64], T.MX[:, s0 + 15:s0 + B:16], mk, ["PB"])
-            for hb in range(n // 512):
-                u0 = s0 % B + 512 * hb
-                for k in range(16):
-                    mm(PU[:, u0 + k:u0 + 512:16], T.BRD[:, k, :], T.ug[:, j0 + 32 * hb:j0 + 32 * hb + 32], True, True,
-                       ["ug", "BRD"], [banks[hb]], inc=(k == 15))
-            tt(T.E[:, 16 * j0:16 * j0 + n], T.G[:, s0:s0 + n], PU[:, s0 % B:s0 % B + n], Op.mult, gk + banks, ["E%d" % ci])
-            scan(T.MX[:, s0:s0 + n], T.RST[:, 0:n], T.E[:, 16 * j0:16 * j0 + n], 0.0, Op.mult, Op.max, ["E%d" % ci, "RST"], mk)
-            Ek.append("E%d" % ci)
-        for b0, bn, bs in CHUNKS[-2:]:
-            act(T.PB[:, b0:b0 + bn], T.MX[:, bs + 15:bs + 16 * bn:16], ["MX%d" % bs], ["PB"])
         if t == 0:
-            late_start(1)
-            arrive("H", "ag1", 4 * len(snd) * KE)
-        act(T.nv[:], IO[:, win].indirect(T.bL[:]), ["IO", "IO2", "bL"], ["nv"], func=AF.Identity, scale=-1.0, bias=-float(TAG * (t + 2) + name0))
-        act(T.PU0[:, 768:B], T.TRIM[:], ["TRIM"], ["U1"])
-        TH, DN, FA, RR = T.PU1[:, 0:L], T.PU1[:, 512:512 + L], T.PC[:, 0:L], T.PA[:, 0:L]
-        mm(TH, B9, T.ONE[:, 0:L], True, False, ["BX", "ONE"], ["U2"])
-        mm(DN, BLK, T.ONE[:, 0:L], True, False, ["ONE"], ["U3"])
-        for k in range(16):
-            tt(T.TOP[:, k:4096:16], T.E[:, k:4096:16], T.PB[:, 0:L], Op.is_equal, Ek + ["PB"], ["TOP%d" % k])
-            mm(T.PA[:, 0:L], T.SEL[:, 16 - k:144 - k], T.TOP[:, k:4096:16], k == 0, k == 15, ["TOP%d" % k], ["PA"])
-        act(T.w[:], T.PA[:, 0:L], ["PA", "eb"], ["w"], func=AF.Exp, scale=16.0 * math.log(2.0), bias=ebias)
-        mm(T.PC[:, 0:L], D2M, T.w[:], True, True, ["w", "D2M"], ["PC"])
-        mm(T.PD[:, 0:L], D2M, T.w[:], True, True, ["w"], ["PD"])
-        oh = T.PC[:, L:2 * L]
-        ts(oh, T.PC[:, 0:L], 0.0, Op.is_ge, ["PC"], ["PC"])
-        act(T.sg[:], T.PD[:, 0:L], ["PD"], ["sg"], func=AF.Sign)
-        tt(T.Z[:], oh, T.xc[:], Op.mult, ["PC", "xc"], ["Z"])
-        sel16(T.PB[:, 0:16], lambda r: T.Z[:, r:L:16], ["Z", "SELH"], ["PB"], mat=T.SELH)
-        mm(T.PU0[:, 0:L], BLKH, T.Z[:], True, True, ["Z", "BLKH"], ["U0"])
-        mm(T.PU0[:, 512:512 + L], BLKH, T.Z[:], True, True, ["Z"], ["U1"])
-        mm(T.PD[:, L:L + 16], IDNH, T.JH[:], True, False, ["IDNH", "JH", "sg"], ["PD"])
-        sel16(T.PD[:, L:L + 16], lambda r: T.sg[:, r:L:16], ["sg", "SELK"], ["PD"], first=False, mat=T.SELK)
-        ts(T.XL[:], T.PB[:, 0:16], float(MID), Op.add, ["PB"], ["XL"])
-        ts(T.xr[:], T.PU0[:, 0:L], float(MID), Op.add, ["U0"], ["xr"])
-        ts(T.XLf[:], T.PB[:, 0:16], float(MID), Op.add, ["PB"], ["XLf"])
-        ts(T.E3[:, 0, :], T.xr[:], T.XLf[:, 0:1], Op.is_equal, ["xr", "XLf"], ["E30"], 256.0, Op.mult)
-        cp(T.tk[:], T.PD[:, L:L + 16], ["PD"], ["tk"])
-        act(T.own[:], T.PU0[:, 512:512 + L], ["U1"], ["own"], func=AF.Identity, scale=1.0 / V, bias=(MID + 0.5) / V + 191.5)
-        act(T.SA[:], Aw.indirect(T.XL[:]), Ar + ["XL"], ["SA"], func=AF.Sign)
-        act(T.Hc[:], Hw.indirect(T.XL[:]), Hr + ["XL"], ["Hc"])
-        mm(TH, B4K, T.SA[:], False, True, ["SA"], ["U2"])
-        act(T.EM[:], T.Hc[:], ["Hc"], ["EM"], func=AF.Relu, bias=1.0)
-        act(T.fc[:], T.TOP[:].indirect(T.tk[:]), ["tk", "SG0", "SG1"] + ["TOP%d" % k for k in range(16)], ["fc"], func=AF.Identity,
-            scale=T.SG[:, 1, t:t + 1], bias=T.SG[:, 0, t:t + 1])
-        act(T.AA[:], Aw.indirect(T.XL[:]), Ar + ["XL"], ["AA"], func=AF.Abs)
-
-        def pair(m):
-            ts(T.E3[:, m, 0:L - 16 * m], T.xr[:, 16 * m:L], T.XLf[:, m:m + 1], Op.is_equal, ["xr", "XLf"], ["E3%d" % m], 256.0, Op.mult)
-            if m < 15:
-                mm(T.PA[:, 16 * m + 16:L], BLK, T.E3[:, m, 16:L - 16 * m], False, False, ["E3%d" % m], ["PA"])
-
-        ts(T.ind[:], T.own[:], c192, Op.is_equal, ["own", "c192"], ["ind"])
-        tt(xI, T.XLf[:], invL, Op.add, ["XLf", "invL"], ["xI"])
-        scan(T.cn[:], T.ind[:], T.ind[:], 0.0, Op.add, Op.max, ["ind"], ["cn"])
-        tt(T.q1[:], T.ind[:], T.cn[:], Op.mult, ["ind", "cn"], ["q1"])
-        mm(RR, BLK, T.q1[:], True, False, ["q1"], ["PA"])
-        mm(T.PA[:, 16:L], BLK, T.E3[:, 0, 16:L], False, False, ["E30"], ["PA"])
-        for m in range(1, 4):
-            pair(m)
-        tt(T.AV[:], T.Hc[:], TH, Op.is_gt, ["Hc", "U2"], ["AV"])
-        mm(DN, NL1, T.EM[:], False, False, ["EM", "NL1"], ["U3"])
-        mm(DN, NL2, T.AV[:], False, True, ["AV", "NL2"], ["U3"])
-        sel16(T.PB[:, 16:32], lambda r: T.AV[:, r:L:16], ["AV"], ["PB"])
-        for m in range(4, 16):
-            pair(m)
-        mm(FA, BN24, T.AV[:], True, False, ["AV"], ["PC"])
-        mm(FA, IDN, T.fc[:], False, True, ["fc"], ["PC"])
-        tt(T.dg[:], T.E3[:, :, 0:16], T.PU0[:, 768:B], Op.mult, ["E3%d" % m for m in range(16)] + ["U1"], ["dg"])
-        mm(RR, BLK, T.dg[:], False, True, ["dg"], ["PA"])
-        act(T.Rb[:], RR, ["PA"], ["Rb"], func=AF.Identity, scale=2048.0, bias=-2048.0 * (CAP + 0.5))
-        sel16(T.PD[:, 0:16], lambda r: T.Rb[:, r:L:16], ["Rb"], ["PD"])
-        pl = T.PL[:, t, me, :]
-        ts(fl, T.PB[:, 16:32], 1.0, Op.min, ["PB"], ["fl"], float(HO), Op.mult)
-        tt(DN, DN, T.nv[:], Op.max, ["U3", "nv"], ["U3"])
-        tt(FA, FA, T.AA[:], Op.mult, ["PC", "AA"], ["PC"])
-        tt(xo, fl, xI, Op.add, ["fl", "xI"], ["xo"])
-        tt(T.X[:], DN, T.Hc[:], Op.min, ["U3", "Hc"], ["X"])
-        tt(pl[:, 0:L], FA, T.X[:], Op.max, ["PC", "X"], ["PLa%d" % t])
-        tt(lm, T.PD[:, 0:16], xo, Op.max, ["PD", "xo"], ["lm"])
-        tt(pl[:, L:L + 16], lm, DUM, Op.min, ["lm", "DUM"], ["PLb%d" % t])
-        send(peers, [pl] * 4, [pl] * 4, "ea%d" % t, ["PLa%d" % t, "PLb%d" % t])
-        arrive("PL%d" % t, "ea%d" % t, 4 * KE)
-        if t == 0:
-            check(0)
-            act(T.G[:, 0:B], IO[:, 0:B], ["IO"], ["G0", "G512"], func=AF.Identity, scale=-1.0, bias=-float(name0))
+            wr["NV1"] = wr["NV1"] + wr["dg"]
+            check(0, T.NV1, "NV1")
             for c in range(2):
-                mm(T.PU1[:, 512 * c:512 * c + 512], BN8, T.EQ[:, 512 * c:512 * c + 512], True, True, ["EQ0", "EQ1"], ["U%d" % (2 + c)])
-        cp(T.XR[:].indirect(T.pos[:]), T.xr[:], ["pos", "xr"], ["XR"])
+                mm(T.PU0[:, 512 * c:512 * c + 512], BN8, T.EQ[:, 512 * c:512 * c + 512], True, True, ["EQ%d" % (1 - c), "BX"], ["U%d" % c])
+        scatter(T.XR[:], T.pos[:], T.xr[:], ["pos", "xr", "dg"], ["XR"])
+        scatter(T.NV[:], T.pos[:], T.nv[:], ["pos", "nv", "OLo" if t else "dg"], ["NV"])
         if t == 0:
-            tt(T.NV[:, 0:B], T.PU1[:], T.G[:, 0:B], Op.add, ["U2", "U3", "G0", "G512"], ["NV"])
-        cp(T.NV[:].indirect(T.pos[:]), T.nv[:], ["pos", "nv"], ["NV"])
+            tt(T.NV[:, 0:B], T.PU0[:], T.NV[:, 0:B], Op.add, ["U0", "U1"], ["NV"])
         holdings()
-        pk = ["PL%d" % t, "PLa%d" % t, "PLb%d" % t]
-        cp(T.OL[:], T.PL[:, t, :, L:L + 16], pk, ["OL"])
         for q in range(N - 1, -1, -1):
-            cp(C[:].indirect(T.OL[:, q, :]), T.PL[:, t, q, 0:L], pk + ["OL"] + Ar + Hr, ["C"])
+            scatter(C[:], T.OL[:, t, q, :], T.PL[:, t, q, :], ["PL", "PLo", "OL", "OLo", "NV", "HL"] + Ar + Hr, ["C"])
 
     check(0)
-    tg, sa = T.TOP[:, 0:V], T.TOP[:, B:B + V]
-    act(T.MX[:, 0:V], C[:, ao:ao + V], ["C"], ["MX0", "MX512"], func=AF.Abs)
-    dma("s", T.yal[:], T.MX[:, 0:V], "dout", ["MX0", "MX512"], [], final=80)
-    act(tg, C[:, ho:ho + V], ["C"], ["TOP0"], func=AF.Identity, scale=-1.0 / TAG, bias=192.0 - 0.3125)
-    act(sa, C[:, ao:ao + V], ["C"], ["TOP1"], func=AF.Sign)
-    for c in range(2):
+    tg, sa = T.junk[:, 0:V], T.TU[:, 0:V]
+    act(tg, C[:, ho:ho + V], ["C"], ["junk", "acc0", "acc1"] + jk, func=AF.Identity, scale=-1.0 / TAG, bias=192.0 - 0.3125)
+    act(sa, C[:, ao:ao + V], ["C"], ["TU"], func=AF.Sign)
+    act(T.MX[:, 0:V], C[:, ao:ao + V], ["C"], Mk, func=AF.Abs)
+    dma("s", T.yal[:], T.MX[:, 0:V], "dout", Mk, [], final=80)
+    for c, (c0, c9, ps, k, u) in enumerate(((0, h, T.PA, "PA", "U2"), (h, V, T.PB, "PB", "U3"))):
         cs = slice(512 * c, 512 * c + 512)
-        mm(T.PU0[:, cs], BLK, T.EQ[:, cs], True, True, ["EQ0", "EQ1"], ["U%d" % c])
-        tt(T.PU0[:, cs], T.PU0[:, cs], T.monb[:, cs], Op.mult, ["U%d" % c, "monb"], ["U%d" % c])
-    halves = ((0, h, T.PA, "PA", "U2"), (h, V, T.PB, "PB", "U3"))
-    for c, (c0, c9, ps, k, u) in enumerate(halves):
         t8 = T.PU1[:, 512 * c:512 * c + h]
-        mm(t8, BNC, T.ONE[:, 0:h], True, False, ["ONE"], [u])
-        mm(t8, I8K, T.TOP[:, c0:c9], False, True, ["TOP0"], [u])
-        mm(ps[:, 0:h], IDN, T.TOP[:, c0:c9], True, False, ["TOP0"], [k])
-        mm(ps[:, 0:h], B05, T.TOP[:, B + c0:B + c9], False, True, ["TOP1"], [k])
-        tt(T.E[:, c0:c9], t8, C[:, ho + c0:ho + c9], Op.add, [u, "C"], ["E%d" % c])
-    for c, (c0, c9, ps, k, u) in enumerate(halves):
-        cs = slice(512 * c, 512 * c + 512)
+        mm(T.PU0[:, cs], BLK, T.EQ[:, cs], True, True, ["EQ%d" % (1 - c)], ["U%d" % c])
+        mm(t8, BNC, T.ONE[:, 0:h], True, False, ["ONE", "BX"], [u])
+        mm(t8, I8K, tg[:, c0:c9], False, True, ["junk", "I8K"], [u])
+        mm(ps[:, 0:h], IDN, tg[:, c0:c9], True, False, ["junk"], [k])
+        mm(ps[:, 0:h], B05, sa[:, c0:c9], False, True, ["TU"], [k])
+        tt(T.PU0[:, cs], T.PU0[:, cs], T.monb[:, cs], Op.mult, ["U%d" % c, "monb"], ["U%d" % c])
+        tt(T.E[:, c0:c9], t8, C[:, ho + c0:ho + c9], Op.add, [u, "C"] + Ek, ["Y0%d" % c])
+        act(T.G[:, cs], Aw.indirect(T.HL[:, 32 * c:32 * c + 32]), ["C", "HL"] + Gk, ["Ga%d" % c], func=AF.Abs, c=GA)
         act(ps[:, 0:h], ps[:, 0:h], [k], [k], func=AF.Sign, scale=-1.0, bias=200.5)
-        act(T.G[:, cs], Aw.indirect(T.HL[:, 32 * c:32 * c + 32]), ["C", "HL"], ["G%d" % (512 * c)], func=AF.Abs)
-        tt(T.E[:, B + c0:B + c9], ps[:, 0:h], T.E[:, c0:c9], Op.mult, [k, "E%d" % c], ["Y%d" % c])
-        dma("s", T.yh[:, c0:c9], T.E[:, B + c0:B + c9], "dout", ["Y%d" % c], [], final=80)
-        tt(T.E[:, 2 * B + 512 * c:2 * B + 512 * c + 512], T.PU0[:, cs], T.G[:, cs], Op.mult, ["U%d" % c, "G%d" % (512 * c)], ["Yp%d" % c])
+        tt(T.E[:, 2 * B + 512 * c:2 * B + 512 * c + 512], T.PU0[:, cs], T.G[:, cs], Op.mult, ["U%d" % c, "Ga%d" % c], ["Yp%d" % c])
         dma("s", T.yp[:, cs], T.E[:, 2 * B + 512 * c:2 * B + 512 * c + 512], "dout", ["Yp%d" % c], [], final=80)
-    for e in cnt:
-        total["s" + e] = cnt[e]
+        tt(T.E[:, B + c0:B + c9], ps[:, 0:h], T.E[:, c0:c9], Op.mult, [k, "Y0%d" % c], ["Y%d" % c])
+        dma("s", T.yh[:, c0:c9], T.E[:, B + c0:B + c9], "dout", ["Y%d" % c], [], final=80)
+
+    seen = {}
+    for i in _order(nodes):
+        n = nodes[i]
+        e = n["e"]
+        if e == "link":
+            continue
+        need = {}
+        for j in n["wait"]:
+            if nodes[j]["sem"] and not (e == "p" and nodes[j]["e"] == "p"):
+                sem, val = nodes[j]["sem"]
+                need[sem] = max(need.get(sem, 0), val)
+        for sem, val in need.items():
+            if seen.get((e, sem), 0) < val:
+                Q[e].wait_ge(T.sem[sem], val)
+                seen[(e, sem)] = val
+        for fn in n["calls"]:
+            ins = fn()
+        if n["sem"] is None:
+            total["s" + e] = total.get("s" + e, 0) + 1
+            n["sem"] = ("s" + e, total["s" + e])
+            ins.then_inc(T.sem["s" + e], 1)
     for sem, val in total.items():
         g.wait_ge(T.sem[sem], val)

@@ -11,10 +11,14 @@ TAG = 8192
 MID = W // 2
 TW = 768 + 1056
 PW = (128, 272)
-CHUNKS = ((0, 16, 0), (16, 16, 1), (32, 32, 2), (64, 32, 3), (96, 32, 0), (128, 64, 2), (192, 64, 0))
+CH, NCH = 64, 4
+PARTS = (2, 1, 1, 1)
+KEEP, REP = (0, 0, 0, 1), (4, 4, 4, 4)
 M0, NA = 4, 8
-CYC, FIX, HOP, SELF = 0.00083, 0.05, 0.1, 0.06
-WAIT, LEAD, FAST = 0.5, 0.3, 3.0
+CYC, PEC, FIX, VFIX, HOP, SELF = 0.00083, 0.52, 0.05, 0.015, 0.15, 0.2
+WAIT, TURNS = 0.5, 2
+OHS, HCS, NVQ, XRQ = 1, 0, 4, 1
+LA, LINK = 192, (2.9, 0.95)
 
 f32, bf, f16, i32, u16 = "float32", "bfloat16", "float16", "int32", "uint16"
 
@@ -27,16 +31,17 @@ SCRATCH = {
     "C": _sb([DO + L], f32), "PL": _sb([RO, N, L], f32), "OL": _sb([RO, N, 16], u16),
     "XR": _sb([B + L], f32), "NV": _sb([B + L], f32), "NV1": _sb([B], f32), "HL": _sb([64], u16), "EQ": _sb([B], bf),
     "XI": _sb([B], i32), "hnI": _sb([V], i32), "IOTA": _sb([TW], f32), "TX": _sb([TW], i32), "TU": _sb([TW], bf), "monb": _sb([B], bf),
-    "G": _sb([4096], f32), "E": _sb([4096], f32), "MX": _sb([4096], f32), "TOP": _sb([4096], bf), "E3": _sb([16, L], bf),
-    "RST": _sb([B], bf), "ONE": _sb([512], bf), "C16": _sb([L], bf),
+    "G": _sb([4096], f32), "E": _sb([4096], f32), "MX": _sb([2048], f32), "TOP": _sb([4096], bf), "E3": _sb([16, L], bf),
+    "SCL": _sb([L], bf), "ONE": _sb([512], bf), "C16": _sb([L], bf),
     "TMP": _sb([144], bf), "SEL": _sb([3, 144], bf), "SELH": _sb([144], f16), "SELF": _sb([144], f32), "IDNF": _sb([128], f32),
-    "BRD": _sb([16, 128], bf), "MAT": _sb([17, 128], bf), "MATH": _sb([2, 128], f16),
+    "BRD": _sb([16, 128], bf), "MAT": _sb([18, 128], bf), "MATH": _sb([2, 128], f16),
     "cI": _sb([8], i32), "cF": _sb([12], f32), "cB": _sb([8], bf), "EK": _sb([16], f32), "SG": _sb([2, 8], f32),
     "JT": _sb([4, 16], f32), "JH": _sb([16], f16),
-    "RS64": _sb([B], bf), "cs": _sb([B], bf), "hz": _sb([64], bf), "hl": _sb([64], bf), "inc": _sb([64], bf), "P": _sb([72], f32),
+    "RS64": _sb([B], bf), "cs": _sb([B], bf), "hl": _sb([64], bf), "inc": _sb([64], bf), "P": _sb([72], f32),
     "junk": _sb([B], bf), "acc": _sb([16], f32), "cL": _sb([16], u16), "cmp": _sb([L], bf), "bL": _sb([16], u16),
     "FO": _sb([L], u16), "ug": _sb([L], bf), "xc": _sb([L], f16), "nv": _sb([L], f32), "w": _sb([L], bf), "sg": _sb([L], bf),
-    "Z": _sb([L], f16), "XL": _sb([16], u16), "tk": _sb([16], u16), "XLf": _sb([16], f32), "xr": _sb([L], u16),
+    "Z": _sb([L], f16), "XL": _sb([16], u16), "tk": _sb([16], u16), "XLf": _sb([16], f32), "xr": _sb([L], f16), "XLh": _sb([16], f16),
+    "TRI": _sb([L], bf), "NEM": _sb([L], f16), "RSY": _sb([L], f32), "YO": _sb([L], f32), "inv": _sb([L], bf), "C256": _sb([L], bf),
     "SA": _sb([L], bf), "Hc": _sb([L], f32), "EM": _sb([L], bf), "AA": _sb([L], f32), "fc": _sb([L], bf), "own": _sb([L], bf),
     "ind": _sb([L], bf), "cn": _sb([L], bf), "q1": _sb([L], bf), "dg": _sb([L], bf), "X": _sb([L], f32),
     "AV": _sb([L], bf), "sF": _sb([L], bf), "Rb": _sb([L], bf),
@@ -99,36 +104,49 @@ def helper_program(g, core, T, topo, q, piece, n):
     g.wait_ge(T.sem["sent"], 2 * 4 * (len(topo.engines(core, peers[0])) // 4))
 
 
-def _order(nodes):
-    n = len(nodes)
-    eng, cost, lat = [[x[k] for x in nodes] for k in ("e", "cost", "lat")]
-    nxt = [[] for _ in nodes]
-    for i in range(n):
-        for j in nodes[i]["pre"]:
-            nxt[j].append(i)
-
-    def gap(i, j):
-        return HOP if eng[i] != eng[j] else SELF if i in nodes[j]["wait"] and eng[i] != "p" else 0.0
-
-    left, start = [len(x["pre"]) for x in nodes], [0.0] * n
+def _pass(eng, cost, pre, key):
+    n = len(eng)
+    nxt = [[] for _ in eng]
+    for j in range(n):
+        for i, d in pre[j]:
+            nxt[i].append((j, d))
+    left, start = [len(x) for x in pre], [0.0] * n
     ready, free, out = {}, {}, []
     for i in range(n):
         if not left[i]:
             ready.setdefault(eng[i], []).append(i)
     for _ in range(n):
         t0, e = min((max(free.get(e, 0.0), min(start[i] for i in r)), e) for e, r in ready.items() if r)
-        i = min(i for i in ready[e] if start[i] <= t0)
-        j = min(j for j in ready[e] if start[j] <= t0 + WAIT * cost[i])
-        i, t0 = j, max(t0, start[j])
+        i = min((i for i in ready[e] if start[i] <= t0), key=lambda x: key[x])
+        i = min((j for j in ready[e] if start[j] <= t0 + WAIT * cost[i]), key=lambda x: key[x])
+        start[i] = max(t0, start[i])
         ready[e].remove(i)
         out.append(i)
-        free[e] = t0 + cost[i]
-        for j in nxt[i]:
-            start[j] = max(start[j], t0 + cost[i] + lat[i] + gap(i, j))
+        free[e] = start[i] + cost[i]
+        for j, d in nxt[i]:
+            start[j] = max(start[j], free[e] + d)
             left[j] -= 1
             if not left[j]:
                 ready.setdefault(eng[j], []).append(j)
-    return out
+    return out, [start[i] + cost[i] for i in range(n)]
+
+
+def _order(nodes):
+    eng, cost = [x["e"] for x in nodes], [x["cost"] for x in nodes]
+    pre, post = [[] for _ in nodes], [[] for _ in nodes]
+    for j, x in enumerate(nodes):
+        for i in x["pre"]:
+            d = nodes[i]["lat"] + (HOP if eng[i] != eng[j] else SELF if eng[i] != "p" else 0.0) if i in x["wait"] else 0.0
+            pre[j].append((i, d))
+            post[i].append((j, d))
+    key, best = list(range(len(nodes))), None
+    for _ in range(TURNS + 1):
+        out, end = _pass(eng, cost, pre, key)
+        t = max(end[i] + x["lat"] for i, x in enumerate(nodes))
+        if best is None or t < best[0]:
+            best = (t, out)
+        key = [-x for x in _pass(eng, cost, post, [-x for x in end])[1]]
+    return best[1]
 
 
 def rank_program(g, core, T, topo):
@@ -143,7 +161,7 @@ def rank_program(g, core, T, topo):
     KE = len(topo.engines(core, peers[0])) // 4
     Q = {"v": g.vector, "a": g.scalar, "p": g.tensor, "g": g, "s": g.sync}
     v, a, p = g.vector, g.scalar, g.tensor
-    nodes, wr, rd, total, group, first = [], {}, {}, {}, [], [0.0]
+    nodes, wr, rd, total, group = [], {}, {}, {}, []
 
     def node(e, fn, cost, R, Wr, lat=0.0, sem=None):
         if group:
@@ -165,7 +183,7 @@ def rank_program(g, core, T, topo):
         for k in Wr:
             wr[k], rd[k] = [len(nodes)], []
         nodes.append({"e": e, "calls": fn if isinstance(fn, list) else [fn], "cost": cost, "lat": lat, "pre": sorted(pre.union(after)),
-                      "wait": pre, "sem": sem, "first": first[0]})
+                      "wait": pre, "sem": sem})
 
     def block(body, R, Wr):
         group.append({"cost": 0.0, "calls": []})
@@ -177,19 +195,19 @@ def rank_program(g, core, T, topo):
         return math.prod(ap.shape[1:])
 
     def vcost(ap, c):
-        return FIX + CYC * c * size(ap)
+        return FIX + CYC * c * size(ap) if c > 1.2 and c != 2 else VFIX + CYC * max(64, c * size(ap))
 
     def dma(e, out, in_, sem, R, Wr, final=16):
         total[sem] = final
         node(e, lambda: Q[e].dma_start(out, in_).then_inc(T.sem[sem], 16), 0.1, R, Wr, lat=2.2, sem=(sem, final))
 
-    def send(dsts, srcs, outs, sem, R):
+    def send(dsts, srcs, outs, sem, R, cost=0.75):
         total["sent"] = total.get("sent", 0) + _engines(T, topo, core, dsts[0])[1] * len(dsts)
-        node("g", lambda: _spread(g, T, topo, core, dsts, srcs, outs, T.sem[sem]), 0.9, R, ["sent"], sem=())
+        node("g", lambda: _spread(g, T, topo, core, dsts, srcs, outs, T.sem[sem]), cost, R, ["sent", "~sent"], sem=())
 
     def arrive(key, sem, val, cost):
         total[sem] = val
-        node("link", [], cost, ["sent"], [key], lat=1.5, sem=(sem, val))
+        node("link", [], cost, ["sent"], [key, "~link"], lat=0.6, sem=(sem, val))
         rd["sent"] = []
 
     def ts(out, in0, s1, o0, R, Wr, s2=None, o1=None, c=1.0):
@@ -205,7 +223,7 @@ def rank_program(g, core, T, topo):
         node("v", lambda: v.tensor_copy(out, in_), vcost(out, c), R, Wr)
 
     def scatter(win, off, in_, R, Wr):
-        node("v", lambda: v.tensor_copy(win.indirect(off), in_), vcost(in_, 3.8), R, Wr)
+        node("v", lambda: v.tensor_copy(win.indirect(off), in_), vcost(in_, 3.5), R, Wr)
 
     def ms(out, c, Wr):
         node("v", lambda: v.memset(out, c), vcost(out, 0.5), [], Wr)
@@ -217,7 +235,7 @@ def rank_program(g, core, T, topo):
         node("a", lambda: a.activation(out, in_, func, **kw), 0.065 + CYC * c * size(out), R, Wr)
 
     def mm(out, lhsT, rhs, st, sp, R, Wr, c=1.0):
-        node("p", lambda: p.matmul(out, lhsT, rhs, st, sp), 0.55 * CYC * c * max(64, size(out)), R, Wr)
+        node("p", lambda: p.matmul(out, lhsT, rhs, st, sp), PEC * CYC * c * max(64, size(out)), R, Wr)
 
     def sel16(out, rhs_of, R, Wr, st=True, sp=True, mat=T.SEL[:, 0, :], c=1.0):
         block(lambda: [mm(out, mat[:, 16 - r:144 - r], rhs_of(r), st and r == 0, sp and r == 15, [], [], c=c) for r in range(16)], R + ["SEL"], Wr)
@@ -231,8 +249,8 @@ def rank_program(g, core, T, topo):
     GA = 1.56
     C, IO, TMP = T.C, T.IOTA, T.TMP
     Aw, Hw = C[:, 0:HO], C[:, HO:DO]
-    REL, BLK, IDN, D2M, NUP, NL1, NL2, B4K, B9, BN24, BN8, B05, I8K, BNC, TM2, BCP, B2K = [T.MAT[:, i, :] for i in range(17)]
-    SEL, SELK, SELN = [T.SEL[:, i, :] for i in range(3)]
+    REL, BLK, IDN, D2M, NUP, NL1, NL2, B4K, B9, BN24, BN8, B05, I8K, BNC, TM2, BBG, BN2K = [T.MAT[:, i, :] for i in range(17)]
+    SEL, SELK = [T.SEL[:, i, :] for i in range(2)]
     BLKH, IDNH = T.MATH[:, 0, :], T.MATH[:, 1, :]
     rcol, g16, ebias, c192, pw4f, r0, rh = [T.cF[:, i:i + 1] for i in range(7)]
     pw4 = T.cB[:, 0:1]
@@ -241,14 +259,13 @@ def rank_program(g, core, T, topo):
     ao, ho = me * V, HO + me * V
     name0 = me * B + 1
     Ar, Hr = ["A", "Aown", "Aown2", "Az", "C"], ["H", "Hown", "Hz", "C"]
-    Gk, Ek, Mk = [["%s%d" % (s, c) for c in range(len(CHUNKS))] for s in ("G", "E", "MX")]
-    Tk = ["TOP%d" % k for k in range(16)]
-    jk = ["junk%d" % m for m in range(NA, 16, 2)]
-    TRIM = T.PD[:, L:2 * L]
+    Gk, Ek, Mk, Tk = [["%s%d" % (s, c) for c in range(n)] for s, n in (("G", 2 * NCH), ("E", 4 * NCH), ("MX", NCH), ("TOP", 4 * NCH))]
+    U = [((T.PU0, T.PU1)[i // 2][:, 512 * (i % 2):512 * (i % 2) + 512], "U%d" % i) for i in range(4)]
+    PM = ((T.PC[:, 0:4 * CH], "PC"), (T.PD[:, 0:4 * CH], "PD"))
 
-    def holdings():
-        sel16(T.PC[:, 0:64], lambda r: T.XR[:, r:B:16], ["XR", "SELF"], ["PC"], mat=T.SELF, c=4.0)
-        cp(T.HL[:], T.PC[:, 0:64], ["PC"], ["HL"])
+    def holdings(piece=16):
+        for r1 in range(0, 16, piece):
+            block(lambda: [mm(U[1][0][:, 0:64], T.SELF[:, 16 - r:144 - r], T.XR[:, r:B:16], r == 0, r == 15, [], [], c=4.0) for r in range(r1, r1 + piece)], ["XR", "SELF"], ["U1"])
 
     def check(w0, nv=T.NV, k="NV"):
         h = w0 or B // 2
@@ -259,105 +276,112 @@ def rank_program(g, core, T, topo):
     h = V // 2
     dma("s", C[:, ao:ao + h], T.al[:, 0:h], "dal", [], ["Aown"], final=32)
     dma("a", C[:, ao + h:ao + V], T.al[:, h:V], "dal", [], ["Aown2"], final=32)
-    dma("s", T.hnI[:], T.hn[:], "dhn", [], ["hnI"])
     ms(T.XI[:], 0, ["XI"])
-    dma("s", T.XI[0:128:16, :], T.hb[:], "dhb", [], ["XI"])
-    dma("s", T.TX[:, 0:B], T.ft[:], "dft", [], ["TX"], final=32)
-    dma("s", T.TX[:, B:TW], T.ft[:, 0:TW - B], "dft", [], ["TX2"], final=32)
-    dma("s", T.TU[:, 0:B], T.ut[:], "dut", [], ["TU"], final=32)
-    dma("s", T.TU[:, B:TW], T.ut[:, 0:TW - B], "dut", [], ["TU2"], final=32)
-    dma("s", T.monb[:], T.mon[:], "dmon", ["hnI"], ["monb"])
+    dma("s", T.XI[0:128:16, :], T.hb[:], "dhb", [], ["XI", "~s"])
+    dma("s", T.hnI[:], T.hn[:], "dhn", [], ["hnI", "~s"])
+    dma("s", T.TX[:, 0:B], T.ft[:], "dft", [], ["TX", "~s"], final=32)
+    dma("s", T.TX[:, B:B + 32], T.ft[:, 0:32], "dft", [], ["TX2", "~s"], final=32)
+    dma("s", T.TU[:, 0:B], T.ut[:], "dut", [], ["TU", "~s"], final=32)
+    dma("s", T.TU[:, B:B + 32], T.ut[:, 0:32], "dut", [], ["TU2", "~s"], final=32)
+    dma("s", T.TX[:, B + 32:TW], T.ft[:, 32:TW - B], "dmon", ["TX", "TU"], ["TX3"], final=48)
+    dma("s", T.TU[:, B + 32:TW], T.ut[:, 32:TW - B], "dmon", ["TX", "TU"], ["TU3"], final=48)
+    dma("s", T.monb[:], T.mon[:], "dmon", ["TX", "TU"], ["monb"], final=48)
 
     iota(T.cI[:, 0:1], [[0, 1]], 0, 1, ["cI"], small=False)
     iota(TMP[:], [[1, 144]], 0, 0, ["TMP"])
     iota(T.C16[:], [[0, 16], [1, 16]], 0, 0, ["C16"])
+    iota(IO[:, 0:L], [[1, L]], 0, 0, ["IO"])
     snd = _senders(core, topo)
     pcs = [[_piece(T, part, me, i, len(snd)) for i in range(len(snd))] for part in range(2)]
-    send(snd[1:], pcs[0][1:], pcs[0][1:], "feed0", ["Aown", "Aown2"])
+    send(snd[1:], pcs[0][1:], pcs[0][1:], "feed0", ["Aown", "Aown2", "IO", "C16"], 2.0)
     send(peers, [pcs[0][0]] * 4, [pcs[0][0]] * 4, "ag0", [])
-    arrive("A", "ag0", 4 * len(snd) * KE, 12.0)
-    iota(IO[:, 0:B], [[1, B]], 0, 0, ["IO"])
-    iota(IO[:, B:TW], [[1, TW - B]], 0, 0, ["IO2"])
+    arrive("A", "ag0", 4 * len(snd) * KE, 6.0)
+    for c0, c9, b0, k in ((L, B, L, "IO1"), (B, TW, 0, "IO2")):
+        iota(IO[:, c0:c9], [[1, c9 - c0]], b0, 0, [k, "~sent"])
 
     ts(T.cI[:, 1:2], T.cI[:, 0:1], 15, Op.bitwise_and, ["cI"], ["cI1"])
     ts(T.cI[:, 2:3], T.cI[:, 0:1], 112, Op.bitwise_and, ["cI"], ["cI2"])
     cp(T.cF[:, 0:2], T.cI[:, 1:3], ["cI1", "cI2"], ["cF"])
     ms(T.ONE[:], 1.0, ["ONE"])
-    ms(C[:, W:HO], 0.0, ["Az"])
-    ms(C[:, HO + W:DO], 1.0, ["Hz"])
     ts(REL, TMP[:, 0:128], g16, Op.subtract, ["TMP", "cF"], ["REL"])
-    ts(ebias, rcol, 136.0, Op.add, ["cF"], ["eb"], -math.log(2.0), Op.mult)
+    ts(r0, rcol, 0.0, Op.is_equal, ["cF"], ["r0"])
+    ts(SEL, TMP[:], -16.0, Op.add, ["TMP", "cF"], ["SEL"], g16, Op.is_equal)
     ts(IDN, REL, rcol, Op.is_equal, ["REL"], ["IDN"])
     ts(TM2, REL, 0.0, Op.is_ge, ["REL"], ["TM2"])
     ts(BLK, REL, 16.0, Op.is_lt, ["REL"], ["BLK"])
+    ts(NUP, REL, rcol, Op.is_lt, ["REL"], ["NUP"], -1.0, Op.mult)
     ts(T.EK[:], TMP[:, 0:16], rcol, Op.is_equal, ["TMP", "cF"], ["EK"])
-    tt(BLK, BLK, TM2, Op.mult, ["TM2", "BLK"], ["BLK"])
+    tt(BLK, BLK, TM2, Op.mult, ["TM2", "BLK"], ["BLK"], c=2)
+    ts(J16, TMP[:, 0:16], 16.0, Op.mult, ["TMP", "cF"], ["J16"], rcol, Op.add)
+    ts(T.EQ[:], T.XI[:], W - 0.5, Op.is_lt, ["XI", "r0"], ["EQ0", "EQ1"], r0, Op.mult)
+    tt(NUP, NUP, BLK, Op.mult, ["NUP", "BLK"], ["NUP"], c=2)
+    ts(JB, J16, 0.5, Op.add, ["J16"], ["JB"])
     act(pw4, rcol, ["cF"], ["pw4"], func=AF.Exp, scale=-math.log(4.0), c=1500.0)
+    act(T.SCL[:], T.C16[:], ["C16", "pw4"], ["SCL"], func=AF.Exp, scale=8.0 * math.log(2.0), bias=-60.0 * math.log(2.0))
     hf, ab, c1, c2 = T.G[:, 0:V], T.MX[:, 0:V], T.TOP[:, 0:V], T.TOP[:, B:B + V]
     cp(hf, T.hnI[:], ["hnI"], Gk)
-    ts(c1, T.hnI[:], 0.5, Op.is_gt, ["hnI"], ["TOP0"], -float(TAG), Op.mult)
-    ts(c2, T.hnI[:], N * B + 0.5, Op.is_gt, ["hnI"], ["TOP1"], -6.0 * TAG, Op.mult)
+    ts(c1, T.hnI[:], 0.5, Op.is_gt, ["hnI"], Tk[0:4], -float(TAG), Op.mult)
+    ts(c2, T.hnI[:], N * B + 0.5, Op.is_gt, ["hnI"], Tk[4:8], -6.0 * TAG, Op.mult)
     act(ab, hf, Gk, Mk, func=AF.Abs)
     for c0, c9, k in ((0, 512, "U2"), (512, V, "U3")):
-        mm(T.PU1[:, c0:c9], IDN, T.TOP[:, c0:c9], True, False, ["TOP0", "IDN"], [k])
-        mm(T.PU1[:, c0:c9], IDN, T.TOP[:, B + c0:B + c9], False, True, ["TOP1"], [k])
+        mm(T.PU1[:, c0:c9], IDN, T.TOP[:, c0:c9], True, False, Tk[0:4] + ["IDN"], [k])
+        mm(T.PU1[:, c0:c9], IDN, T.TOP[:, B + c0:B + c9], False, True, Tk[4:8], [k])
     tt(C[:, ho:ho + V], T.PU1[:, 0:V], ab, Op.subtract, ["U2", "U3"] + Mk, ["Hown"])
     send(snd[1:], pcs[1][1:], pcs[1][1:], "feed1", ["Hown"])
     send(peers, [pcs[1][0]] * 4, [pcs[1][0]] * 4, "ag1", ["A"])
     arrive("H", "ag1", 4 * len(snd) * KE, 7.0)
-    ts(SEL, TMP[:], -16.0, Op.add, ["TMP", "cF"], ["SEL"], g16, Op.is_equal)
-    ts(r0, rcol, 0.0, Op.is_equal, ["cF"], ["r0"])
-    ts(rh, rcol, 0.5, Op.mult, ["cF"], ["rh"])
-    cp(T.XR[:, 0:B], T.XI[:], ["XI"], ["XR"])
-    ts(T.SELF[:], SEL, r0, Op.mult, ["SEL", "r0"], ["SELF"])
     block(lambda: [act(T.BRD[:, k, :], BLK, [], [], scale=T.EK[:, k:k + 1]) for k in range(16)], ["BLK", "EK"], ["BRD"])
-    ts(NUP, REL, rcol, Op.is_lt, ["REL"], ["NUP"], -1.0, Op.mult)
-    tt(NUP, NUP, BLK, Op.mult, ["NUP", "BLK"], ["NUP"])
     ms(T.RS64[:], 1.0, ["RS64"])
+    ms(C[:, W:HO], 0.0, ["Az"])
+    ms(C[:, HO + W:DO], 1.0, ["Hz"])
     ms(T.RS64[:, 0:B:64], 0.0, ["RS64"])
-    ms(T.RST[:], 1.0, ["RST"])
-    ms(T.RST[:, 0:B:16], 0.0, ["RST"])
-    ts(J16, TMP[:, 0:16], 16.0, Op.mult, ["TMP", "cF"], ["J16"], rcol, Op.add)
-    ts(JB, J16, 0.5, Op.add, ["J16"], ["JB"])
-    holdings()
-    ts(T.hz[:], T.PC[:, 0:64], W - 0.5, Op.is_lt, ["PC"], ["hz"])
-    ts(D2M, IDN, 2.0, Op.mult, ["IDN"], ["D2M"])
-    ts(c192, rcol, 192.0, Op.add, ["cF"], ["c192"])
-    tt(D2M, D2M, BLK, Op.subtract, ["D2M", "BLK"], ["D2M"])
-    ts(DUM, J16, float(DO), Op.add, ["J16"], ["DUM"])
-    ts(JD, J16, float(B), Op.add, ["J16"], ["JD"])
-    ts(T.JH[:], J16, 16.0, Op.mult, ["J16"], ["JH"], 60.0, Op.add)
-    cp(T.SELH[:], SEL, ["SEL"], ["SELH"])
-    ts(SELK, SEL, rh, Op.mult, ["SEL", "rh"], ["SELK"])
-    ts(SELN, SEL, -HO / 2, Op.mult, ["SEL"], ["SELN"])
-    cp(BLKH, BLK, ["BLK"], ["BLKH"])
-    cp(IDNH, IDN, ["IDN"], ["IDNH"])
-    cp(T.IDNF[:], IDN, ["IDN"], ["IDNF"])
-    ts(TRIM, T.C16[:], rcol, Op.is_gt, ["C16", "cF"], ["PD"])
-    ts(T.SG[:, 0, :], TMP[:, 0:8], rcol, Op.is_lt, ["TMP", "cF"], ["SG0"], 2.0, Op.mult)
-    ts(T.SG[:, 0, :], T.SG[:, 0, :], -1.0, Op.add, ["SG0"], ["SG0"])
-    ts(T.SG[:, 1, :], T.SG[:, 0, :], -0.0625, Op.mult, ["SG0"], ["SG1"])
-    act(pw4f, pw4, ["pw4"], ["pw4f"], scale=-(2.0 ** 80))
-    act(NL1, D2M, ["D2M", "pw4f"], ["NL1"], scale=pw4f)
-    act(NL2, NL1, ["NL1"], ["NL2"], scale=2.0 ** -32)
-    block(lambda: [act(m, BLK, [], [], scale=c) for m, c in (
-        (B4K, TAG / 2), (B9, -9.0 * TAG / 16), (BN24, -(2.0 ** 24)), (BN8, -float(TAG)), (B05, 0.5), (BNC, -12.0 * TAG), (BCP, -(CAP + 0.5) / 16),
-        (B2K, HO / 2))], ["BLK"], ["BX"])
-    act(I8K, IDN, ["IDN"], ["I8K"], scale=float(TAG))
-    act(T.NV[:, 0:B], IO[:, 0:B], ["IO"], ["NV"], func=AF.Identity, scale=-1.0, bias=-float(name0))
-    act(T.NV1[:], IO[:, 0:B], ["IO"], ["NV1"], func=AF.Identity, scale=-1.0, bias=-float(TAG + name0))
+    act(T.IDNF[:], IDN, ["IDN"], ["IDNF"])
+
+    def constants():
+        ts(T.XR[:, 0:B], T.XI[:], -float(MID), Op.add, ["XI"], ["XR"])
+        ts(T.SELF[:], SEL, r0, Op.mult, ["SEL", "r0"], ["SELF"])
+        ts(ebias, rcol, -120.0, Op.add, ["cF"], ["eb"], -math.log(2.0), Op.mult)
+        ts(rh, rcol, 0.5, Op.mult, ["cF"], ["rh"])
+        ts(D2M, IDN, 2.0, Op.mult, ["IDN"], ["D2M"])
+        ts(c192, rcol, 192.0, Op.add, ["cF"], ["c192"])
+        tt(D2M, D2M, BLK, Op.subtract, ["D2M", "BLK"], ["D2M"], c=2)
+        ts(DUM, J16, float(DO), Op.add, ["J16"], ["DUM"])
+        ts(JD, J16, float(B), Op.add, ["J16"], ["JD"])
+        ts(T.JH[:], J16, 16.0, Op.mult, ["J16"], ["JH"], 60.0, Op.add)
+        ts(T.SELH[:], SEL, 1.0 - OHS / 2, Op.mult, ["SEL"], ["SELH"])
+        ts(SELK, SEL, rh, Op.mult, ["SEL", "rh"], ["SELK"])
+        ts(BLKH, BLK, 1.0 - OHS / 2, Op.mult, ["BLK"], ["BLKH"])
+        cp(IDNH, IDN, ["IDN"], ["IDNH"])
+        ts(T.TRI[:], T.C16[:], rcol, Op.is_le, ["C16", "cF"], ["TRI"], float(TAG), Op.mult, c=0.5)
+        ts(T.dg[:], T.C16[:], rcol, Op.not_equal, ["C16", "cF"], ["dg"], 8.0 * HO, Op.mult, c=0.5)
+        ms(T.RSY[:], -65536.0, ["RSY"])
+        cp(T.C256[:], IO[:, 0:L], ["IO"], ["C256"])
+        ts(T.NEM[:], T.dg[:], float(MID), Op.add, ["dg"], ["NEM"], c=0.5)
+        ts(T.RSY[:, 0:L:16], DUM, -8.0 * HO, Op.add, ["DUM"], ["RSY"])
+        ts(T.SG[:, 0, :], TMP[:, 0:8], rcol, Op.is_lt, ["TMP", "cF"], ["SG0"], 0.125, Op.mult)
+        ts(T.SG[:, 1, :], T.SG[:, 0, :], -0.0625, Op.add, ["SG0"], ["SG1"])
+        ts(T.SG[:, 0, :], T.SG[:, 1, :], 15.0, Op.mult, ["SG1"], ["SG0"])
+        act(pw4f, pw4, ["pw4"], ["pw4f"], scale=-(2.0 ** 80))
+        act(NL1, D2M, ["D2M", "pw4f"], ["NL1"], scale=pw4f)
+        act(NL2, NL1, ["NL1"], ["NL2"], scale=2.0 ** -32)
+        block(lambda: [act(m, BLK, [], [], scale=c) for m, c in (
+            (B4K, TAG / 2), (B9, -9.0 * TAG / 16), (BN24, -(2.0 ** 24)), (BN8, -float(TAG)), (B05, 0.5), (BNC, -12.0 * TAG), (BBG, 4.0 * HO),
+            (BN2K, -HO / 2))], ["BLK"], ["BX"])
+        act(I8K, IDN, ["IDN"], ["I8K"], scale=float(TAG))
+        act(T.NV[:, 0:B], IO[:, 0:B], ["IO", "IO1"], ["NV"], func=AF.Identity, scale=-1.0, bias=-float(name0))
+        act(T.NV1[:], IO[:, 0:B], ["IO", "IO1"], ["NV1"], func=AF.Identity, scale=-1.0, bias=-float(TAG + name0))
+        holdings(2)
+        ts(T.HL[:], U[1][0][:, 0:64], float(MID), Op.add, ["U1"], ["HL"])
 
     for t in range(RO):
         w0 = (L * t) % B
         win = slice(w0, w0 + 1056)
         if t > 0:
             check(w0)
-            sel16(T.PC[:, 0:64], lambda r: T.EQ[:, r:B:16], ["EQ0", "EQ1"], ["PC"])
-            hz, hk = T.PC[:, 0:64], "PC"
-        else:
-            hz, hk = T.hz[:], "hz"
-        scan(T.inc[:], T.ONE[:, 0:64], hz, 0.0, Op.add, Op.subtract, [hk, "ONE"], ["inc"])
-        ts(T.hl[:], hz, 0.5, Op.is_lt, [hk], ["hl"])
+        hz = T.PC[:, 0:64]
+        sel16(hz, lambda r: T.EQ[:, r:B:16], ["EQ0", "EQ1"], ["PC"])
+        scan(T.inc[:], T.ONE[:, 0:64], hz, 0.0, Op.add, Op.subtract, ["PC", "ONE"], ["inc"])
+        ts(T.hl[:], hz, 0.5, Op.is_lt, ["PC"], ["hl"])
         mm(T.PA[:, 0:64], BLK, T.inc[:], True, True, ["inc", "BLK"], ["PA"])
         mm(T.PD[:, 0:64], BLK, T.inc[:], True, True, ["inc", "BLK"], ["PD"])
         mm(T.PB[:, 64:65], BLK, T.inc[:, 63:64], True, True, ["inc", "BLK"], ["PB"])
@@ -369,129 +393,177 @@ def rank_program(g, core, T, topo):
             block(lambda: [act(T.junk[:, 64 * m:64 * m + 64], T.PA[:, 0:64], [], [], func=AF.Sign, scale=-1.0, bias=JB[:, m:m + 1], c=1.4,
                                accum_out=T.acc[:, m:m + 1]) for m in range(m0, ma)], ["PA", "JB"], ["acc" + s])
             if m0:
-                for m in range(NA, 16, 2):
-                    block(lambda: [ts(T.junk[:, 64 * x:64 * x + 64], T.PD[:, 0:64], JB[:, x:x + 1], Op.is_lt, [], [], 16.0, Op.mult) for x in (m, m + 1)],
-                          ["PD", "JB"], ["junk%d" % m])
-                scan(T.cs[:, 64 * NA:B], T.RS64[:, 64 * NA:B], T.junk[:, 64 * NA:B], 0.0, Op.mult, Op.add, jk + ["RS64"], ["cs"], c=0.5)
+                for x in range(NA, 16, 2):
+                    block(lambda: [ts(T.junk[:, 64 * m:64 * m + 64], T.PD[:, 0:64], JB[:, m:m + 1], Op.is_lt, [], [], 16.0, Op.mult) for m in (x, x + 1)],
+                          ["PD", "JB"], ["junk%d" % x])
+                scan(T.cs[:, 64 * NA:B], T.RS64[:, 64 * NA:B], T.junk[:, 64 * NA:B], 0.0, Op.mult, Op.add, ["junk%d" % x for x in range(NA, 16, 2)] + ["RS64"], ["cs"], c=0.5)
                 ts(T.cL[:, NA:16], T.cs[:, 64 * NA + 63:B:64], 0.0625, Op.mult, ["cs"], ["cL2"])
             ts(T.cL[:, m0:ma], T.acc[:, m0:ma], 64.0, Op.add, ["acc" + s], ["cL" + s], 0.5, Op.mult)
-            tt(T.cmp[:, c], T.P[:, 0:65].indirect(T.cL[:, m0:m1]), IO[:, c], Op.is_le, ["P", "IO", "cL" + s] + ["cL2"] * m0, ["cmp" + s], c=GA)
             ts(T.cs[:, 64 * m0 + 63:64 * ma:64], T.acc[:, m0:ma], 64.0, Op.add, ["acc" + s], ["cs" + s], 8.0, Op.mult)
-            sel16(ps[:, m0:m1], lambda r: T.cmp[:, 16 * m0 + r:16 * m1:16], ["cmp" + s], [k], sp=False)
-            mm(ps[:, m0:m1], IDN, T.cs[:, 64 * m0 + 63:64 * m1:64], False, True, ["cs" + s, "IDN"] + ["cs"] * m0, [k])
+            tt(T.cmp[:, c], T.P[:, 0:65].indirect(T.cL[:, m0:m1]), IO[:, c], Op.is_le, ["P", "IO", "cL" + s] + ["cL2"] * m0, ["cmp" + s], c=GA)
+            mm(ps[:, m0:m1], IDN, T.cs[:, 64 * m0 + 63:64 * m1:64], True, False, ["cs" + s, "IDN"] + ["cs"] * m0, [k])
+            sel16(ps[:, m0:m1], lambda r: T.cmp[:, 16 * m0 + r:16 * m1:16], ["cmp" + s], [k], st=False)
             cp(T.bL[:, m0:m1], ps[:, m0:m1], [k], ["bL" + s])
-            cp(T.FO[:, c], T.TX[:, win].indirect(T.bL[:, m0:m1]), ["TX", "TX2", "bL" + s], ["FO" + s], c=GA)
-            act(T.ug[:, c], T.TU[:, win].indirect(T.bL[:, m0:m1]), ["TU", "TU2", "bL" + s], ["ug" + s], c=GA)
-        def largest(ci):
-            c = slice(16 * CHUNKS[ci][0], 16 * (CHUNKS[ci][0] + CHUNKS[ci][1]))
-            scan(T.MX[:, c], T.RST[:, 0:16 * CHUNKS[ci][1]], T.E[:, c], 0.0, Op.mult, Op.max, [Ek[ci], "RST"], [Mk[ci]])
-
-        for ci, (j0, nj, b0) in enumerate(CHUNKS):
-            c = slice(16 * j0, 16 * (j0 + nj))
-            pu = (T.PU0, T.PU1)[b0 // 2][:, 512 * (b0 % 2):512 * (b0 % 2) + 16 * nj]
-            banks = ["U%d" % (b0 + i) for i in range((nj + 31) // 32)]
-            s = "0" if j0 < 16 * M0 else "1"
-            act(T.G[:, c], Aw.indirect(T.FO[:, j0:j0 + nj]), Ar + ["FO" + s], [Gk[ci], "~G"], func=AF.Abs, c=GA)
-            for i, k0 in enumerate(banks):
-                n1 = min(32, nj - 32 * i)
-                block(lambda: [mm(pu[:, 512 * i + k:512 * i + 16 * n1:16], T.BRD[:, k, :], T.ug[:, j0 + 32 * i:j0 + 32 * i + n1], True, True, [], [])
-                               for k in range(16)], ["ug" + s, "BRD"], [k0])
-            tt(T.E[:, c], T.G[:, c], pu, Op.mult, [Gk[ci]] + banks, [Ek[ci]])
-            if ci:
-                largest(ci - 1)
-        largest(len(CHUNKS) - 1)
-        jl = CHUNKS[-1][0]
-        act(T.PB[:, 0:jl], T.MX[:, 15:16 * jl:16], Mk[:-1], ["PB"])
-        cp(T.PB[:, jl:L], T.MX[:, 16 * jl + 15:16 * L:16], Mk[-1:], ["PB"])
-        ts(T.xc[:], T.FO[:], -float(MID), Op.add, ["FO0", "FO1"], ["xc"], c=0.5)
+            cp(T.FO[:, c], T.TX[:, win].indirect(T.bL[:, m0:m1]), ["TX", "TX2", "bL" + s] + ["TX3"] * t, ["FO" + s], c=GA)
+            tt(T.ug[:, c], T.TU[:, win].indirect(T.bL[:, m0:m1]), T.SCL[:, c], Op.mult, ["TU", "TU2", "SCL", "bL" + s] + ["TU3"] * t, ["ug" + s], c=GA)
+        if t == 0:
+            constants()
         ts(invL, J16, T.P[:, 64:65], Op.is_ge, ["J16", "P"], ["invL"], 2.0 * TAG, Op.mult)
-        act(T.nv[:], IO[:, win].indirect(T.bL[:]), ["IO", "IO2", "bL0", "bL1"], ["nv"], func=AF.Identity, scale=-1.0, bias=-float(TAG * (t + 2) + name0), c=GA)
-        for k in range(16):
-            tt(T.TOP[:, k:4096:16], T.E[:, k:4096:16], T.PB[:, 0:L], Op.is_equal, Ek + ["PB"], [Tk[k]])
-            mm(T.PA[:, 0:L], SEL[:, 16 - k:144 - k], T.TOP[:, k:4096:16], k == 0, k == 15, [Tk[k], "SEL"], ["PA"])
-        D1, OH, D2, TK = T.PC[:, 0:L], T.PC[:, L:2 * L], T.PD[:, 0:L], T.PD[:, 0:16]
-        XV, XS, XP, TH = T.PU0[:, 0:L], T.PU0[:, 512:512 + L], T.PU1[:, 0:16], T.PU1[:, 512:512 + L]
-        FA, DN, RR, Y = XV, OH, T.PA[:, L:2 * L], T.PB[:, L:L + 16]
-        act(T.w[:], T.PA[:, 0:L], ["PA", "eb"], ["w"], func=AF.Exp, scale=16.0 * math.log(2.0), bias=ebias)
-        mm(D1, D2M, T.w[:], True, True, ["w", "D2M"], ["PC"])
-        mm(D2, D2M, T.w[:], True, True, ["w", "D2M"], ["PD"])
-        ts(OH, D1, 0.0, Op.is_ge, ["PC"], ["PC"])
-        act(T.sg[:], D2, ["PD"], ["sg"], func=AF.Sign)
-        tt(T.Z[:], OH, T.xc[:], Op.mult, ["PC", "xc"], ["Z"])
-        sel16(XP, lambda c: T.Z[:, c:L:16], ["Z", "SELH"], ["U2", "~x"], mat=T.SELH)
-        mm(XV, BLKH, T.Z[:], True, True, ["Z", "BLKH"], ["U0"])
-        mm(XS, BLKH, T.Z[:], True, True, ["Z", "BLKH"], ["U1"])
-        ts(T.XL[:], XP, float(MID), Op.add, ["U2"], ["XL"])
-        cp(T.Hc[:], Hw.indirect(T.XL[:]), Hr + ["XL"], ["Hc"], c=GA)
-        ts(T.xr[:], XV, float(MID), Op.add, ["U0"], ["xr"])
-        ts(T.XLf[:], XP, float(MID), Op.add, ["U2"], ["XLf"])
-        mm(TK, IDNH, T.JH[:], True, False, ["IDNH", "JH"], ["PD"])
-        sel16(TK, lambda c: T.sg[:, c:L:16], ["sg", "SELK"], ["PD", "~x"], st=False, mat=SELK)
-        cp(T.tk[:], TK, ["PD"], ["tk"])
-        act(T.SA[:], Aw.indirect(T.XL[:]), Ar + ["XL"], ["SA"], func=AF.Sign, c=GA)
-        act(T.EM[:], Hw.indirect(T.XL[:]), Hr + ["XL"], ["EM"], func=AF.Relu, bias=1.0, c=GA)
-        mm(TH, B9, T.ONE[:, 0:L], True, False, ["BX", "ONE"], ["U3"])
-        mm(TH, B4K, T.SA[:], False, True, ["SA"], ["U3"])
-        tt(T.AV[:], T.Hc[:], TH, Op.is_gt, ["Hc", "U3"], ["AV"])
-        mm(DN, BLK, T.ONE[:, 0:L], True, False, ["ONE"], ["PC"])
-        mm(DN, NL1, T.EM[:], False, False, ["EM", "NL1"], ["PC"])
-        mm(DN, NL2, T.AV[:], False, True, ["AV", "NL2"], ["PC"])
-        act(T.fc[:], T.TOP[:].indirect(T.tk[:]), ["tk", "SG0", "SG1"] + Tk, ["fc"], func=AF.Identity, scale=T.SG[:, 1, t:t + 1], bias=T.SG[:, 0, t:t + 1], c=GA)
-        act(T.AA[:], Aw.indirect(T.XL[:]), Ar + ["XL"], ["AA"], func=AF.Abs, c=GA)
-        block(lambda: [mm(FA, IDN, T.fc[:], True, False, [], []), mm(FA, BN24, T.AV[:], False, True, [], [])], ["AV", "fc"], ["U0"])
+        ts(T.xc[:], T.FO[:], -float(MID), Op.add, ["FO0", "FO1"], ["xc"], c=0.5)
+        ts(T.inv[:], T.C256[:], T.P[:, 64:65], Op.is_ge, ["C256", "P"], ["inv"], 2.0, Op.mult, c=0.5)
+
+        def products(ci):
+            s, (ua, ka), (ub, kb) = "01"[ci > 0], U[2 * ci % 4], U[2 * ci % 4 + 1]
+            j0, n1 = CH * ci, CH // PARTS[ci]
+            for o, (u1, k1) in enumerate(((ua, ka), (ub, kb))):
+                block(lambda: [mm(u1[:, k:512:8], T.BRD[:, 2 * k + o, :], T.ug[:, j0:j0 + CH], True, True, [], []) for k in range(8)], ["ug" + s, "BRD"], [k1])
+            for j in (j0, j0 + 32):
+                act(T.G[:, 16 * j:16 * j + 512], Aw.indirect(T.FO[:, j:j + 32]), Ar + ["FO" + s], [Gk[j // 32], "~G"], func=AF.Abs, c=GA)
+            for j in range(j0, j0 + CH, n1):
+                gk, c, ek = Gk[j // 32:(j + n1 + 31) // 32], slice(8 * (j - j0), 8 * (j - j0 + n1)), Ek[j // 16:(j + n1) // 16]
+                tt(T.E[:, 16 * j:16 * (j + n1):2], T.G[:, 16 * j:16 * (j + n1):2], ua[:, c], Op.mult, gk + [ka], ek[0::2])
+                if KEEP[ci]:
+                    tt(ub[:, c], T.G[:, 16 * j + 1:16 * (j + n1):2], ub[:, c], Op.mult, gk + [kb], [kb])
+                else:
+                    tt(T.E[:, 16 * j + 1:16 * (j + n1):2], T.G[:, 16 * j + 1:16 * (j + n1):2], ub[:, c], Op.mult, gk + [kb], ek[1::2])
+
+        def largest(ci):
+            j0, (ub, kb), (pm, km), r = CH * ci, U[2 * ci % 4 + 1], PM[ci % 2], REP[ci]
+            block(lambda: [scan(T.MX[:, 8 * j:8 * j + 128], T.E[:, 16 * j:16 * j + 256:2], ub[:, 8 * (j - j0):8 * (j - j0) + 128] if KEEP[ci] else T.E[:, 16 * j + 1:16 * j + 256:2],
+                                0.0, Op.max, Op.max, [], []) for j in range(j0, j0 + CH, 16)], Ek[4 * ci:4 * ci + 4] + [kb] * KEEP[ci], [Mk[ci]])
+            block(lambda: [mm(pm[:, i:r * CH:r], T.IDNF[:], T.MX[:, 8 * j0 + 7:8 * (j0 + CH):8], True, True, [], [], c=4.0) for i in range(r)], [Mk[ci], "IDNF"], [km])
+
+        def marks(ci):
+            j0, (ub, kb), (pm, km), r = CH * ci, U[2 * ci % 4 + 1], PM[ci % 2], REP[ci]
+            c0, c9 = 16 * j0, 16 * (j0 + CH)
+            if KEEP[ci]:
+                M = T.MX[:, 8 * j0 + 7:8 * (j0 + CH):8]
+                block(lambda: [tt(T.TOP[:, c0 + 2 * k + 1:c9:16], ub[:, k:512:8], M, Op.is_lt, [], []) for k in range(8)], [kb, Mk[ci]], [Tk[4 * ci + 1], Tk[4 * ci + 3]])
+            for x, o in enumerate((1, 3, 0, 2) if KEEP[ci] else (0, 1, 2, 3)):
+                if not (KEEP[ci] and o % 2):
+                    block(lambda: [tt(T.TOP[:, c0 + i:c9:16 // r], T.E[:, c0 + i:c9:16 // r], pm[:, 0:r * CH], Op.is_lt, [], []) for i in range(o, 16 // r, 4)],
+                          [km] + Ek[4 * ci:4 * ci + 4], [Tk[4 * ci + o]])
+                block(lambda: [mm(T.PA[:, j0:j0 + CH] if j0 < LA else U[2][0][:, 0:CH], SEL[:, 16 - k:144 - k], T.TOP[:, c0 + k:c9:16], x == 0 and k == o,
+                                  x == 3 and k == 12 + o, [], []) for k in range(o, 16, 4)], [Tk[4 * ci + o], "SEL"], ["PA" if j0 < LA else "U2"])
+
+        def choose(s):
+            lo, hi = (0, LA) if s == "A" else (LA, L)
+            n, c, m = hi - lo, slice(lo, hi), slice(lo // 16, hi // 16)
+            k = lambda *x: [y + s for y in x]
+            at = lambda b, c0, w=n: ({"PA": T.PA, "PB": T.PB, "PC": T.PC, "PD": T.PD}.get(b) or U[int(b[1])][0])[:, c0:c0 + w]
+            if s == "A":
+                kv, k2, ko, kp, kt, kx, ks = "PA", "PB", "PC", "U1", "PB", "U0", "PA"
+                VT, D2, OH, D3, XP, TK, XS = at(kv, 0), at(k2, 0), at(ko, L), at(ko, 0), at(kp, 0, n // 16), at(kt, L, n // 16), at(ks, L)
+            else:
+                kv, k2, ko, kp, kt, kx, ks = "U2", "U2", "U3", "PD", "U2", "U3", "U2"
+                VT, D2, OH, D3, XP, TK, XS = at(kv, 0), at(k2, n), at(ko, 0), at(ko, n), at(kp, 0, n // 16), at(kt, L, n // 16), at(ks, 2 * n)
+            XV, FA, TH, DN, one = at(kx, lo), at(kx, L + lo), at(kp, L + lo), OH, T.ONE[:, 0:n]
+            XL, TKL = T.XL[:, m], T.tk[:, m]
+            act(T.w[:, c], VT, [kv, "eb"], k("w"), func=AF.Exp, scale=-16.0 * math.log(2.0), bias=ebias)
+            if s == "A":
+                sel16(XP, lambda r: T.xc[:, r:hi:16], ["xc", "SELH"], [kp], mat=T.SELH, sp=False)
+                mm(XV, BLKH, T.xc[:, c], True, False, ["xc", "BLKH"], [kx])
+                mm(D2, D2M, T.w[:, c], True, True, k("w") + ["D2M"], [k2])
+                mm(XS, BLKH, T.xc[:, c], True, False, ["xc", "BLKH"], [ks])
+                act(OH, D2, [k2], [ko], func=AF.Sign)
+            else:
+                mm(D3, D2M, T.w[:, c], True, True, k("w") + ["D2M"], [ko])
+                mm(D2, D2M, T.w[:, c], True, True, k("w") + ["D2M"], [k2])
+                ts(OH, D3, 0.0, Op.is_ge, [ko], [ko], 2.0, Op.mult)
+            act(T.sg[:, c], D2, [k2], k("sg"), func=AF.Sign)
+            tt(T.Z[:, c], OH, T.xc[:, c], Op.mult, [ko, "xc"], k("Z"))
+            sel16(XP, lambda r: T.Z[:, lo + r:hi:16], k("Z") + ["SELH"], [kp], mat=T.SELH, st=s == "B")
+            mm(XV, BLKH, T.Z[:, c], s == "B", True, k("Z"), [kx])
+            mm(XS, BLKH, T.Z[:, c], s == "B", True, k("Z"), [ks])
+            ts(XL, XP, float(MID), Op.add, [kp], k("XL"))
+            cp(T.XLf[:, m], XP, [kp], k("XLf"))
+            cp(T.XLh[:, m], XP, [kp], k("XLh"))
+            cp(T.xr[:, c], XV, [kx], k("xr"))
+            mm(TK, IDNH, T.JH[:, 0:n // 16], True, False, ["IDNH", "JH"], [kt])
+            sel16(TK, lambda r: T.sg[:, lo + r:hi:16], k("sg") + ["SELK"], [kt], st=False, mat=SELK)
+            act(T.SA[:, c], Aw.indirect(XL), Ar + k("XL"), k("SA"), func=AF.Sign, c=GA)
+            if HCS and s == "A":
+                act(T.Hc[:, c], Hw.indirect(XL), Hr + k("XL"), k("Hc"), c=GA)
+            else:
+                cp(T.Hc[:, c], Hw.indirect(XL), Hr + k("XL"), k("Hc"), c=GA)
+            cp(TKL, TK, [kt], k("tk"))
+            act(T.EM[:, c], Hw.indirect(XL), Hr + k("XL"), k("EM"), func=AF.Relu, bias=1.0, c=GA)
+            mm(TH, B9, one, True, False, ["BX", "ONE"], [kp])
+            mm(TH, B4K, T.SA[:, c], False, True, k("SA"), [kp])
+            tt(T.AV[:, c], T.Hc[:, c], TH, Op.is_gt, k("Hc") + [kp], k("AV"))
+            mm(DN, BLK, one, True, False, ["ONE"], [ko])
+            mm(DN, NL1, T.EM[:, c], False, False, k("EM") + ["NL1"], [ko])
+            mm(DN, NL2, T.AV[:, c], False, True, k("AV") + ["NL2"], [ko])
+            act(T.fc[:, c], T.TOP[:, 16 * lo:16 * hi].indirect(TKL), k("tk") + ["SG0", "SG1"] + Tk[m], k("fc"), func=AF.Identity,
+                scale=T.SG[:, 1, t:t + 1], bias=T.SG[:, 0, t:t + 1], c=GA)
+            act(T.AA[:, c], Aw.indirect(XL), Ar + k("XL"), k("AA"), func=AF.Abs, c=GA)
+            block(lambda: [mm(FA, IDN, T.fc[:, c], True, False, [], []), mm(FA, BN24, T.AV[:, c], False, True, [], [])], k("AV", "fc"), [kx])
+            tt(D3, DN, T.nv[:, c], Op.max, [ko, "nv"], [ko])
+            tt(FA, FA, T.AA[:, c], Op.mult, [kx] + k("AA"), [kx])
+            tt(T.X[:, c], D3, T.Hc[:, c], Op.min, [ko] + k("Hc"), k("X"))
+            tt(pl[:, c], FA, T.X[:, c], Op.max, [kx] + k("X"), k("PLo"))
+            send(peers, [pl[:, c]] * 4, [pl[:, c]] * 4, "ea%d" % t, k("PLo"))
+            arrive("PL" + s, "ea%d" % t, 8 * KE, LINK[s == "B"])
+            act(T.own[:, c], XS, [ks], k("own"), func=AF.Identity, scale=1.0 / V, bias=(MID + 0.5) / V + 191.5)
+            act(T.sF[:, c], DN, [ko], k("sF"), func=AF.Sign)
+
         pl, ol = T.PL[:, t, me, :], T.OL[:, t, me, :]
-        tt(D1, DN, T.nv[:], Op.max, ["PC", "nv"], ["PC"])
-        tt(T.X[:], D1, T.Hc[:], Op.min, ["PC", "Hc"], ["X"])
-        tt(FA, FA, T.AA[:], Op.mult, ["U0", "AA"], ["U0"])
-        tt(pl, FA, T.X[:], Op.max, ["U0", "X"], ["PLo"])
-        send(peers, [pl] * 4, [pl] * 4, "ea%d" % t, ["PLo"])
-        arrive("PL", "ea%d" % t, 4 * KE, 4.0)
-        act(T.own[:], XS, ["U1"], ["own"], func=AF.Identity, scale=1.0 / V, bias=(MID + 0.5) / V + 191.5)
-        act(T.sF[:], DN, ["PC"], ["sF"], func=AF.Sign)
-        ts(T.ind[:], T.own[:], c192, Op.is_equal, ["own", "c192"], ["ind"], c=0.5)
-        mm(RR, BCP, T.ONE[:, 0:L], True, False, ["BX", "ONE"], ["PA"])
-        for m in range(16):
-            if m == 5:
-                scan(T.cn[:], T.ind[:], T.ind[:], 0.0, Op.add, Op.max, ["ind"], ["cn"], c=0.5)
-            if m == 8:
-                tt(T.q1[:], T.ind[:], T.cn[:], Op.mult, ["ind", "cn"], ["q1"])
-            ts(T.E3[:, m, 0:L - 16 * m], T.xr[:, 16 * m:L], T.XLf[:, m:m + 1], Op.is_equal, ["xr", "XLf"], ["E3%d" % m], 256.0, Op.mult, c=0.5)
-            if m < 15:
-                mm(RR[:, 16 * m + 16:L], BLK, T.E3[:, m, 16:L - 16 * m], False, False, ["E3%d" % m], ["PA"])
-        mm(RR, BLK, T.q1[:], False, False, ["q1"], ["PA"])
-        tt(T.dg[:], T.E3[:, :, 0:16], TRIM, Op.mult, ["E3%d" % m for m in range(16)] + ["PD"], ["dg"])
-        mm(RR, BLK, T.dg[:], False, True, ["dg"], ["PA"])
-        act(T.Rb[:], RR, ["PA"], ["Rb"], func=AF.Relu, scale=2048.0)
-        mm(Y, B2K, T.ONE[:, 0:16], True, False, ["BX", "ONE"], ["PB"])
-        mm(Y, T.IDNF[:], invL, False, False, ["IDNF", "invL"], ["PB"], c=4.0)
-        mm(Y, T.IDNF[:], T.XLf[:], False, False, ["XLf"], ["PB"], c=4.0)
-        sel16(Y, lambda c: T.sF[:, c:L:16], ["sF", "SELN"], ["PB"], st=False, sp=False, mat=SELN)
-        sel16(Y, lambda c: T.Rb[:, c:L:16], ["Rb"], ["PB"], st=False)
-        tt(lc, Y, DUM, Op.min, ["PB", "DUM"], ["lc"])
-        cp(ol, lc, ["lc"], ["OLo"])
+        for ci in range(NCH):
+            products(ci)
+            if ci:
+                marks(ci - 1)
+            largest(ci)
+        act(T.nv[:], IO[:, win].indirect(T.bL[:]), ["IO", "IO1", "IO2", "bL0", "bL1"], ["nv"], func=AF.Identity, scale=-1.0, bias=-float(TAG * (t + 2) + name0), c=GA)
+        marks(NCH - 1)
+        choose("A")
+        choose("B")
+        RR, XB = T.PA[:, L:2 * L], T.PB[:, L:2 * L]
+        AB = lambda x: [x + "A", x + "B"]
+        ts(T.ind[:], T.own[:], c192, Op.is_equal, AB("own") + ["c192"], ["ind"], c=0.5)
+        scan(T.cn[:], T.ONE[:, 0:L], T.ind[:], 0.0, Op.mult, Op.subtract, ["ind"], ["cn"], c=0.5)
+        scan(T.q1[:], T.ind[:], T.cn[:], 0.0, Op.max, Op.mult, ["ind", "cn"], ["q1"], c=0.5)
+        ts(T.Rb[:], T.q1[:], -(CAP + 0.5), Op.is_lt, ["q1"], ["Rb"], c=0.5)
+        mm(XB, IDN, T.TRI[:], True, False, ["TRI"], ["PB"])
+        block(lambda: [mm(XB[:, c:L:16], IDNH, T.XLh[:], False, c == 15, [], []) for c in range(16)], AB("XLh"), ["PB"])
+        tt(T.dg[:], T.xr[:], XB, Op.is_equal, AB("xr") + ["PB"], ["dg"])
+        block(lambda: [mm(RR, IDNH, T.NEM[:], True, False, [], []), mm(RR, I8K, T.inv[:], False, False, [], []), mm(RR, IDNH, T.xr[:], False, False, [], [])],
+              ["NEM", "inv", "I8K"] + AB("xr"), ["PA"])
+        for m in range(15):
+            ts(T.E3[:, m, 0:L - 16 * m - 16], T.xr[:, 16 * m + 16:L], T.XLf[:, m:m + 1], Op.is_equal, AB("xr") + AB("XLf"), ["E3%d" % m], c=0.5)
+            mm(RR[:, 16 * m + 16:L], BBG, T.E3[:, m, 0:L - 16 * m - 16], False, False, ["E3%d" % m], ["PA"])
+            if m == 7:
+                mm(RR, BBG, T.dg[:], False, False, ["dg"], ["PA"])
+        mm(RR, BBG, T.Rb[:], False, False, ["Rb"], ["PA"])
+        mm(RR, BN2K, T.sF[:], False, True, AB("sF"), ["PA"])
+        scan(T.YO[:], T.RSY[:], RR, -65536.0, Op.max, Op.min, ["PA", "RSY"], ["YO"])
+        ts(ol, T.YO[:, 15:L:16], 8.0 * HO, Op.add, ["YO"], ["OLo"])
         send(peers, [ol] * 4, [ol] * 4, "eb%d" % t, ["OLo"])
-        arrive("OL", "eb%d" % t, 4 * KE, 0.5)
+        arrive("OL", "eb%d" % t, 4 * KE, 0.3)
         ts(T.li[:, 0, :], T.bL[:], float(w0), Op.add, ["bL0", "bL1"], ["li0"])
         ts(T.li[:, 1, :], T.li[:, 0, :], B - 1, Op.bitwise_and, ["li0"], ["li1"])
         tt(la, T.li[:, 1, :], invL, Op.add, ["li1", "invL"], ["la"])
         tt(lb, la, JD, Op.min, ["la", "JD"], ["lb"])
         cp(T.pos[:], lb, ["lb"], ["pos"])
         if t == 0:
-            wr["NV1"] = wr["NV1"] + wr["dg"]
+            wr["NV1"] = wr["NV1"] + wr["E314"]
             check(0, T.NV1, "NV1")
             for c in range(2):
                 mm(T.PU0[:, 512 * c:512 * c + 512], BN8, T.EQ[:, 512 * c:512 * c + 512], True, True, ["EQ%d" % (1 - c), "BX"], ["U%d" % c])
-        scatter(T.XR[:], T.pos[:], T.xr[:], ["pos", "xr", "dg"], ["XR"])
-        scatter(T.NV[:], T.pos[:], T.nv[:], ["pos", "nv", "OLo" if t else "dg"], ["NV"])
-        if t == 0:
             tt(T.NV[:, 0:B], T.PU0[:], T.NV[:, 0:B], Op.add, ["U0", "U1"], ["NV"])
+        for x in range(XRQ):
+            scatter(T.XR[:], T.pos[:, 16 * x // XRQ:16 * (x + 1) // XRQ], T.xr[:, L * x // XRQ:L * (x + 1) // XRQ], ["pos", "xrA", "xrB", "OLo"], ["XR"])
         holdings()
         for q in range(N - 1, -1, -1):
-            scatter(C[:], T.OL[:, t, q, :], T.PL[:, t, q, :], ["PL", "PLo", "OL", "OLo", "NV", "HL"] + Ar + Hr, ["C"])
+            if NVQ == 1 and q == N - 1:
+                scatter(T.NV[:], T.pos[:], T.nv[:], ["pos", "nv", "OLo"], ["NV", "~C"])
+            scatter(C[:], T.OL[:, t, q, :], T.PL[:, t, q, :], ["PLA", "PLB", "PLoA", "PLoB", "OL", "OLo"] + Ar + Hr, ["C", "~C"])
+            if NVQ == 4 and q:
+                scatter(T.NV[:], T.pos[:, 4 * q - 4:4 * q], T.nv[:, 64 * q - 64:64 * q], ["pos", "nv"], ["NV", "~C"])
+        ts(T.HL[:], U[1][0][:, 0:64], float(MID), Op.add, ["U1"], ["HL", "~C"])
 
     check(0)
     tg, sa = T.junk[:, 0:V], T.TU[:, 0:V]
-    act(tg, C[:, ho:ho + V], ["C"], ["junk", "acc0", "acc1"] + jk, func=AF.Identity, scale=-1.0 / TAG, bias=192.0 - 0.3125)
+    act(tg, C[:, ho:ho + V], ["C"], ["junk", "acc0", "acc1"] + ["junk%d" % x for x in range(NA, 16, 2)], func=AF.Identity, scale=-1.0 / TAG, bias=192.0 - 0.3125)
     act(sa, C[:, ao:ao + V], ["C"], ["TU"], func=AF.Sign)
     act(T.MX[:, 0:V], C[:, ao:ao + V], ["C"], Mk, func=AF.Abs)
     dma("s", T.yal[:], T.MX[:, 0:V], "dout", Mk, [], final=80)

@@ -1,4 +1,5 @@
 import math
+import numpy as np
 from concourse.bass import DstId, RemoteDMATransfer
 from concourse.mybir import AluOpType, ActivationFunctionType
 
@@ -9,16 +10,26 @@ HO = 4096
 DO = 2 * HO
 TAG = 8192
 MID = W // 2
-TW = 768 + 1056
-PW = (128, 272)
+LW = B + L + 32
+TW = 768 + LW
+PW = (144, 264)
 CH, NCH = 64, 4
-PARTS = (2, 1, 1, 1)
-KEEP, REP = (0, 0, 0, 1), (4, 4, 4, 4)
-M0, NA = 4, 8
-CYC, PEC, FIX, VFIX, HOP, SELF = 0.00083, 0.52, 0.05, 0.015, 0.15, 0.2
-WAIT, TURNS = 0.5, 2
-OHS, HCS, NVQ, XRQ = 1, 0, 4, 1
-LA, LINK = 192, (2.9, 0.95)
+PARTS = (2, 2, 1, 1)
+KEEP, REP = (0, 0, 0, 1), (4, 4, 4, 2)
+FAR = (0, 0, 0, 0)
+UB, BK = ((0, 1, 4), (2, 3, 5), (0, 1, 4), (0, 1, 4)), ((2, 3), (0, 1))
+M0, NS = 4, (4, 4)
+LEAST, ACT, PCALL, F32 = 64, 0.085, 0.0, 5
+CYC, PEC, FIX = 0.00083, 0.52, 0.05
+CASES = ((1.1, 1.4, 2.8, 0.25, 0.005, 1.0), (1.3, 1.8, 4.5, 0.22, 0.01, 1.3), (1.0, 1.25, 2.0, 0.28, 0.0, 0.8))
+TURNS, TRIES, MOVES, STEP, SEED = 4, 2000, 6, 1.0, 1
+KEPT = {}
+VB, AL, PMS, PST, OLA, EMV, DGG = 0, 0, ("PC", "PD", "PB", "PD"), 0, 0, "B", 0
+NVC = (0, 8, 12, 16)
+CHM, TKX, PSC, SEG = "B", "A", 0, (0, 22, 43, 64)
+OHS, HCS, CAPS, XLS = 1, "", 1, 0
+STG = {"A": (0, 128, "PC", "U3", "U2"), "B": (128, 256, "U1", "PD", "U0")}
+LA, LINK = 128, 0.0135
 
 f32, bf, f16, i32, u16 = "float32", "bfloat16", "float16", "int32", "uint16"
 
@@ -29,23 +40,22 @@ def _sb(shape, d):
 
 SCRATCH = {
     "C": _sb([DO + L], f32), "PL": _sb([RO, N, L], f32), "OL": _sb([RO, N, 16], u16),
-    "XR": _sb([B + L], f32), "NV": _sb([B + L], f32), "NV1": _sb([B], f32), "HL": _sb([64], u16), "EQ": _sb([B], bf),
+    "XR": _sb([B + LW], f32), "NV": _sb([B + LW], f32), "NV1": _sb([B], f32), "HL": _sb([64], u16), "EQ": _sb([B], bf),
     "XI": _sb([B], i32), "hnI": _sb([V], i32), "IOTA": _sb([TW], f32), "TX": _sb([TW], i32), "TU": _sb([TW], bf), "monb": _sb([B], bf),
     "G": _sb([4096], f32), "E": _sb([4096], f32), "MX": _sb([2048], f32), "TOP": _sb([4096], bf), "E3": _sb([16, L], bf),
     "SCL": _sb([L], bf), "ONE": _sb([512], bf), "C16": _sb([L], bf),
-    "TMP": _sb([144], bf), "SEL": _sb([3, 144], bf), "SELH": _sb([144], f16), "SELF": _sb([144], f32), "IDNF": _sb([128], f32),
-    "BRD": _sb([16, 128], bf), "MAT": _sb([18, 128], bf), "MATH": _sb([2, 128], f16),
+    "TMP": _sb([144], bf), "SEL": _sb([3, 144], bf), "SELH": _sb([144], f16), "SELF": _sb([144], f32), "IDNF": _sb([128], f32), "NIDF": _sb([128], f32),
+    "BRD": _sb([16, 128], bf), "MAT": _sb([22, 128], bf), "MATH": _sb([2, 128], f16),
     "cI": _sb([8], i32), "cF": _sb([12], f32), "cB": _sb([8], bf), "EK": _sb([16], f32), "SG": _sb([2, 8], f32),
-    "JT": _sb([4, 16], f32), "JH": _sb([16], f16),
-    "RS64": _sb([B], bf), "cs": _sb([B], bf), "hl": _sb([64], bf), "inc": _sb([64], bf), "P": _sb([72], f32),
+    "JT": _sb([4, 16], f32), "JH": _sb([32], f16), "JK": _sb([16], f16),
+    "RS64": _sb([B], bf), "cs": _sb([B], bf), "inc": _sb([66], bf), "ends": _sb([64], f32), "six": _sb([64], bf), "I8F": _sb([128], f32), "spare": _sb([16], bf), "P": _sb([72], f32),
     "junk": _sb([B], bf), "acc": _sb([16], f32), "cL": _sb([16], u16), "cmp": _sb([L], bf), "bL": _sb([16], u16),
     "FO": _sb([L], u16), "ug": _sb([L], bf), "xc": _sb([L], f16), "nv": _sb([L], f32), "w": _sb([L], bf), "sg": _sb([L], bf),
-    "Z": _sb([L], f16), "XL": _sb([16], u16), "tk": _sb([16], u16), "XLf": _sb([16], f32), "xr": _sb([L], f16), "XLh": _sb([16], f16),
-    "TRI": _sb([L], bf), "NEM": _sb([L], f16), "RSY": _sb([L], f32), "YO": _sb([L], f32), "inv": _sb([L], bf), "C256": _sb([L], bf),
+    "Z": _sb([2 * L], f16), "xd": _sb([L], f16), "colu": _sb([16], u16), "XL": _sb([16], u16), "tk": _sb([16], u16), "XLf": _sb([16], f32), "xr": _sb([L], f16), "XLh": _sb([16], f16),
+    "TRI": _sb([L], bf), "NEM": _sb([L], f16), "RSY": _sb([L], f32), "YO": _sb([L], f32),
     "SA": _sb([L], bf), "Hc": _sb([L], f32), "EM": _sb([L], bf), "AA": _sb([L], f32), "fc": _sb([L], bf), "own": _sb([L], bf),
     "ind": _sb([L], bf), "cn": _sb([L], bf), "q1": _sb([L], bf), "dg": _sb([L], bf), "X": _sb([L], f32),
     "AV": _sb([L], bf), "sF": _sb([L], bf), "Rb": _sb([L], bf),
-    "li": _sb([2, 16], i32), "lf": _sb([4, 16], f32), "pos": _sb([16], u16),
     "PU0": ("psum", [128, 1024], f32), "PU1": ("psum", [128, 1024], f32),
     "PA": ("psum", [128, 512], f32), "PB": ("psum", [128, 512], f32), "PC": ("psum", [128, 512], f32),
     "PD": ("psum", [128, 512], f32),
@@ -55,10 +65,10 @@ SEMAPHORES = (["sv", "sa", "sp", "sg", "sent", "feed0", "feed1", "ag0", "ag1", "
 PSUM = ("U0", "U1", "U2", "U3", "PA", "PB", "PC", "PD")
 
 
-def _senders(core, topo):
-    out, seen = [core], set()
+def _senders(core, topo, part):
+    out, seen = [core], {topo.addr(core)[2]}
     for c in topo.cores_of(core):
-        if topo.die(c) != topo.die(core) and topo.addr(c)[2] not in seen:
+        if topo.addr(c)[2] not in seen and (part == 0 or topo.die(c) != topo.die(core)):
             seen.add(topo.addr(c)[2])
             out.append(c)
     return out
@@ -80,8 +90,7 @@ def _engines(T, topo, core, dst):
     eng = topo.engines(core, dst)
     if topo.chip(core) == topo.chip(dst):
         far = topo.engines(core, [c for c in T.cores if topo.chip(c) != topo.chip(core)][0])
-        eng = [e for e in eng if e not in far]
-        return eng, len(eng) // 2
+        eng = far + [e for e in eng if e not in far]
     return eng, len(eng) // 4
 
 
@@ -95,57 +104,87 @@ def _spread(g, T, topo, core, dsts, srcs, outs, sem):
     g.remote_dma_fused(tr, local_sem=T.sem["sent"])
 
 
-def helper_program(g, core, T, topo, q, piece, n):
+def helper_program(g, core, T, topo, q):
     peers = [T.cores[(q + 1 + i) % N] for i in range(N - 1)]
-    for part in range(2):
+    parts = [part for part in range(2) if core in _senders(T.cores[q], topo, part)]
+    for part in parts:
+        s = _senders(T.cores[q], topo, part)
         g.wait_ge(T.sem["feed%d" % part], _engines(T, topo, T.cores[q], core)[1])
-        ap = _piece(T, part, q, piece, n)
+        ap = _piece(T, part, q, s.index(core), len(s))
         _spread(g, T, topo, core, peers, [ap] * 4, [ap] * 4, T.sem["ag%d" % part])
-    g.wait_ge(T.sem["sent"], 2 * 4 * (len(topo.engines(core, peers[0])) // 4))
+    g.wait_ge(T.sem["sent"], len(parts) * 4 * (len(topo.engines(core, peers[0])) // 4))
 
 
-def _pass(eng, cost, pre, key):
-    n = len(eng)
-    nxt = [[] for _ in eng]
-    for j in range(n):
+def _pass(eng, cost, pre, key, along):
+    key = list(key)
+    for j in along:
         for i, d in pre[j]:
-            nxt[i].append((j, d))
-    left, start = [len(x) for x in pre], [0.0] * n
-    ready, free, out = {}, {}, []
-    for i in range(n):
-        if not left[i]:
-            ready.setdefault(eng[i], []).append(i)
-    for _ in range(n):
-        t0, e = min((max(free.get(e, 0.0), min(start[i] for i in r)), e) for e, r in ready.items() if r)
-        i = min((i for i in ready[e] if start[i] <= t0), key=lambda x: key[x])
-        i = min((j for j in ready[e] if start[j] <= t0 + WAIT * cost[i]), key=lambda x: key[x])
-        start[i] = max(t0, start[i])
-        ready[e].remove(i)
-        out.append(i)
-        free[e] = start[i] + cost[i]
-        for j, d in nxt[i]:
-            start[j] = max(start[j], free[e] + d)
-            left[j] -= 1
-            if not left[j]:
-                ready.setdefault(eng[j], []).append(j)
-    return out, [start[i] + cost[i] for i in range(n)]
+            if key[i] >= key[j]:
+                key[j] = key[i] + 1e-6
+    start, busy, rank = [0.0] * len(eng), {e: [] for e in set(eng)}, [0] * len(eng)
+    for r, j in enumerate(sorted(along, key=lambda x: key[x])):
+        t, c, b = 0.0, cost[j], busy[eng[j]]
+        for i, d in pre[j]:
+            if start[i] + cost[i] + d > t:
+                t = start[i] + cost[i] + d
+        k = len(b)
+        while k and b[k - 1][1] > t:
+            k -= 1
+        while k < len(b) and b[k][0] < t + c:
+            t = max(t, b[k][1])
+            k += 1
+        b.insert(k, (t, t + c))
+        start[j], rank[j] = t, r
+    return sorted(along, key=lambda x: (start[x], rank[x])), start
 
 
 def _order(nodes):
-    eng, cost = [x["e"] for x in nodes], [x["cost"] for x in nodes]
-    pre, post = [[] for _ in nodes], [[] for _ in nodes]
-    for j, x in enumerate(nodes):
-        for i in x["pre"]:
-            d = nodes[i]["lat"] + (HOP if eng[i] != eng[j] else SELF if eng[i] != "p" else 0.0) if i in x["wait"] else 0.0
-            pre[j].append((i, d))
+    eng, kind = [x["e"] for x in nodes], [x["kind"] for x in nodes]
+    if KEPT.get("kind") == kind:
+        return KEPT["out"]
+    cases = []
+    for f, ga, sc, hop, call, link in CASES:
+        cost = [float(np.dot(x["cost"], (1.0, call, CYC * f, CYC * f * ga, CYC * f * sc, link))) for x in nodes]
+        pre = [[(i, nodes[i]["lat"] + (0.0 if eng[i] == eng[j] == "p" else hop) if i in x["wait"] else 0.0) for i in x["pre"]] for j, x in enumerate(nodes)]
+        cases.append((cost, pre))
+
+    def length(out):
+        s = 0.0
+        for cost, pre in cases:
+            end, free = [0.0] * len(out), dict.fromkeys(eng, 0.0)
+            for j in out:
+                t = free[eng[j]]
+                for i, d in pre[j]:
+                    if end[i] + d > t:
+                        t = end[i] + d
+                end[j] = free[eng[j]] = t + cost[j]
+            s += max(end[i] + x["lat"] for i, x in enumerate(nodes))
+        return s
+
+    cost, pre = cases[0]
+    post = [[] for _ in nodes]
+    for j in range(len(nodes)):
+        for i, d in pre[j]:
             post[i].append((j, d))
-    key, best = list(range(len(nodes))), None
-    for _ in range(TURNS + 1):
-        out, end = _pass(eng, cost, pre, key)
-        t = max(end[i] + x["lat"] for i, x in enumerate(nodes))
-        if best is None or t < best[0]:
-            best = (t, out)
-        key = [-x for x in _pass(eng, cost, post, [-x for x in end])[1]]
+    n = len(nodes)
+    fore, back = list(range(n)), list(range(n - 1, -1, -1))
+    key, best, x = fore, None, SEED
+    for turn in range(TURNS + TRIES):
+        out, start = _pass(eng, cost, pre, key, fore)
+        t = length(out)
+        if best is None or t <= best[0]:
+            best = (t, out, start)
+        shift = {}
+        if turn >= TURNS:
+            start = best[2]
+            for _ in range(MOVES):
+                x = x * 48271 % 2147483647
+                k = kind[x % n]
+                x = x * 48271 % 2147483647
+                shift[k] = (x % 2001 - 1000) * 0.001 * STEP
+        late = _pass(eng, cost, post, [-start[i] - cost[i] - shift.get(kind[i], 0.0) for i in fore], back)[1]
+        key = [-late[i] - cost[i] + shift.get(kind[i], 0.0) for i in fore]
+    KEPT.update(kind=kind, out=best[1], time=best[0])
     return best[1]
 
 
@@ -153,15 +192,14 @@ def rank_program(g, core, T, topo):
     me = T.rank_of(core)
     if me is None:
         for q in range(N):
-            s = _senders(T.cores[q], topo)
-            if core in s:
-                helper_program(g, core, T, topo, q, s.index(core), len(s))
+            if core in _senders(T.cores[q], topo, 0):
+                helper_program(g, core, T, topo, q)
         return
     peers = [T.cores[(me + 1 + i) % N] for i in range(N - 1)]
     KE = len(topo.engines(core, peers[0])) // 4
     Q = {"v": g.vector, "a": g.scalar, "p": g.tensor, "g": g, "s": g.sync}
     v, a, p = g.vector, g.scalar, g.tensor
-    nodes, wr, rd, total, group = [], {}, {}, {}, []
+    nodes, wr, rd, total, group, count, stage = [], {}, {}, {}, [], {}, ["start"]
 
     def node(e, fn, cost, R, Wr, lat=0.0, sem=None):
         if group:
@@ -176,17 +214,24 @@ def rank_program(g, core, T, topo):
             if k in PSUM:
                 pre.update(i for i in rd.get(k, []) if nodes[i]["e"] != e)
         for k in Wr:
-            if k[0] != "~":
+            if k[0] == "+":
+                pre.update(wr[k[1:]][:1])
+            elif k[0] != "~":
                 pre.update(wr.get(k, []) + rd.get(k, []))
         for k in R:
             rd.setdefault(k, []).append(len(nodes))
         for k in Wr:
-            wr[k], rd[k] = [len(nodes)], []
+            if k[0] == "+":
+                wr[k[1:]].append(len(nodes))
+            else:
+                wr[k], rd[k] = [len(nodes)], []
+        name = " ".join([stage[0], e] + R + [">"] + Wr)
+        count[name] = count.get(name, 0) + 1
         nodes.append({"e": e, "calls": fn if isinstance(fn, list) else [fn], "cost": cost, "lat": lat, "pre": sorted(pre.union(after)),
-                      "wait": pre, "sem": sem})
+                      "wait": pre, "sem": sem, "kind": "%s %d" % (name, count[name])})
 
     def block(body, R, Wr):
-        group.append({"cost": 0.0, "calls": []})
+        group.append({"cost": price(), "calls": []})
         body()
         n = group.pop()
         node(n["e"], n["calls"], n["cost"], R, Wr)
@@ -194,20 +239,23 @@ def rank_program(g, core, T, topo):
     def size(ap):
         return math.prod(ap.shape[1:])
 
+    def price(us=0.0, calls=0, cycles=0.0, gathered=0, scattered=0, link=0.0):
+        return np.array([us, calls, cycles, gathered, scattered, link], float)
+
     def vcost(ap, c):
-        return FIX + CYC * c * size(ap) if c > 1.2 and c != 2 else VFIX + CYC * max(64, c * size(ap))
+        return price(FIX, gathered=size(ap)) if c == GA else price(calls=1, cycles=max(LEAST, c * size(ap)))
 
     def dma(e, out, in_, sem, R, Wr, final=16):
         total[sem] = final
-        node(e, lambda: Q[e].dma_start(out, in_).then_inc(T.sem[sem], 16), 0.1, R, Wr, lat=2.2, sem=(sem, final))
+        node(e, lambda: Q[e].dma_start(out, in_).then_inc(T.sem[sem], 16), price(0.1), R, Wr, lat=2.2, sem=(sem, final))
 
     def send(dsts, srcs, outs, sem, R, cost=0.75):
         total["sent"] = total.get("sent", 0) + _engines(T, topo, core, dsts[0])[1] * len(dsts)
-        node("g", lambda: _spread(g, T, topo, core, dsts, srcs, outs, T.sem[sem]), cost, R, ["sent", "~sent"], sem=())
+        node("g", lambda: _spread(g, T, topo, core, dsts, srcs, outs, T.sem[sem]), price(cost), R, ["sent", "~sent"], sem=())
 
-    def arrive(key, sem, val, cost):
+    def arrive(key, sem, val, cost, way="link", lat=0.6):
         total[sem] = val
-        node("link", [], cost, ["sent"], [key, "~link"], lat=0.6, sem=(sem, val))
+        node(way, [], price(0.3, link=cost), ["sent"], [key, "~" + way], lat=lat, sem=(sem, val))
         rd["sent"] = []
 
     def ts(out, in0, s1, o0, R, Wr, s2=None, o1=None, c=1.0):
@@ -223,7 +271,7 @@ def rank_program(g, core, T, topo):
         node("v", lambda: v.tensor_copy(out, in_), vcost(out, c), R, Wr)
 
     def scatter(win, off, in_, R, Wr):
-        node("v", lambda: v.tensor_copy(win.indirect(off), in_), vcost(in_, 3.5), R, Wr)
+        node("v", lambda: v.tensor_copy(win.indirect(off), in_), price(FIX, scattered=size(in_)), R, Wr)
 
     def ms(out, c, Wr):
         node("v", lambda: v.memset(out, c), vcost(out, 0.5), [], Wr)
@@ -232,46 +280,50 @@ def rank_program(g, core, T, topo):
         node("v", lambda: v.tensor_tensor_scan(out, d0, d1, init, o0, o1), vcost(out, c), R, Wr)
 
     def act(out, in_, R, Wr, func=AF.Copy, c=1.0, **kw):
-        node("a", lambda: a.activation(out, in_, func, **kw), 0.065 + CYC * c * size(out), R, Wr)
+        node("a", lambda: a.activation(out, in_, func, **kw), price(0.065, gathered=size(out)) if c == GA else price(ACT, cycles=c * max(LEAST, size(out))), R, Wr)
 
     def mm(out, lhsT, rhs, st, sp, R, Wr, c=1.0):
-        node("p", lambda: p.matmul(out, lhsT, rhs, st, sp), PEC * CYC * c * max(64, size(out)), R, Wr)
+        def last():
+            sp[0] -= 1
+            return sp[0] == 0
+        node("p", lambda: p.matmul(out, lhsT, rhs, st, last() if isinstance(sp, list) else sp), price(calls=PCALL, cycles=PEC * (F32 if c == 4 else c) * max(64, size(out))), R, Wr)
 
     def sel16(out, rhs_of, R, Wr, st=True, sp=True, mat=T.SEL[:, 0, :], c=1.0):
         block(lambda: [mm(out, mat[:, 16 - r:144 - r], rhs_of(r), st and r == 0, sp and r == 15, [], [], c=c) for r in range(16)], R + ["SEL"], Wr)
 
     def iota(out, pat, base, cm, Wr, small=True):
         if small:
-            node("g", lambda: g.iota(out, pat, base, cm, allow_small_or_imprecise_dtypes=True), 0.13 + 2 * CYC * size(out), [], Wr)
+            node("g", lambda: g.iota(out, pat, base, cm, allow_small_or_imprecise_dtypes=True), price(0.13, cycles=2 * size(out)), [], Wr)
         else:
-            node("g", lambda: g.iota(out, pat, base, cm), 0.13 + 2 * CYC * size(out), [], Wr)
+            node("g", lambda: g.iota(out, pat, base, cm), price(0.13, cycles=2 * size(out)), [], Wr)
 
     GA = 1.56
     C, IO, TMP = T.C, T.IOTA, T.TMP
     Aw, Hw = C[:, 0:HO], C[:, HO:DO]
-    REL, BLK, IDN, D2M, NUP, NL1, NL2, B4K, B9, BN24, BN8, B05, I8K, BNC, TM2, BBG, BN2K = [T.MAT[:, i, :] for i in range(17)]
+    REL, BLK, IDN, D2M, NUP, DNM, THM, B4K, B9, BN24, BN8, B05, I8K, BNC, TM2, BBG, BN2K, UPM, I16, B15, DF, DF8 = [T.MAT[:, i, :] for i in range(22)]
     SEL, SELK = [T.SEL[:, i, :] for i in range(2)]
     BLKH, IDNH = T.MATH[:, 0, :], T.MATH[:, 1, :]
-    rcol, g16, ebias, c192, pw4f, r0, rh = [T.cF[:, i:i + 1] for i in range(7)]
-    pw4 = T.cB[:, 0:1]
-    J16, JB, DUM, JD = [T.JT[:, i, :] for i in range(4)]
-    invL, la, lb, lc = [T.lf[:, i, :] for i in range(4)]
+    rcol, g16, ebias, first, r0, rh = [T.cF[:, i:i + 1] for i in range(6)]
+    J16, JB, DUM, J1 = [T.JT[:, i, :] for i in range(4)]
     ao, ho = me * V, HO + me * V
     name0 = me * B + 1
-    Ar, Hr = ["A", "Aown", "Aown2", "Az", "C"], ["H", "Hown", "Hz", "C"]
+    Ar, Hr = ["A", "A2", "Aown", "Aown2", "Az", "C"], ["H", "H2", "Hown", "Hz", "C"]
     Gk, Ek, Mk, Tk = [["%s%d" % (s, c) for c in range(n)] for s, n in (("G", 2 * NCH), ("E", 4 * NCH), ("MX", NCH), ("TOP", 4 * NCH))]
     U = [((T.PU0, T.PU1)[i // 2][:, 512 * (i % 2):512 * (i % 2) + 512], "U%d" % i) for i in range(4)]
-    PM = ((T.PC[:, 0:4 * CH], "PC"), (T.PD[:, 0:4 * CH], "PD"))
+    U += [(T.PB[:], "PB"), (T.PC[:], "PC")]
+    PM = [(T[k][:], k) for k in PMS]
 
-    def holdings(piece=16):
+    AB = lambda x: [x + s for s in STG]
+
+    def holdings(x0, piece=16):
         for r1 in range(0, 16, piece):
-            block(lambda: [mm(U[1][0][:, 0:64], T.SELF[:, 16 - r:144 - r], T.XR[:, r:B:16], r == 0, r == 15, [], [], c=4.0) for r in range(r1, r1 + piece)], ["XR", "SELF"], ["U1"])
+            block(lambda: [mm(U[1][0][:, 0:64], T.SELF[:, 16 - r:144 - r], T.XR[:, x0 + r:x0 + B:16], r == 0, r == 15, [], [], c=4.0) for r in range(r1, r1 + piece)], ["XR", "SELF"], ["U1"])
 
-    def check(w0, nv=T.NV, k="NV"):
-        h = w0 or B // 2
-        e0 = B - h if w0 else 0
-        tt(T.EQ[:, (h - w0) % B:(h - w0) % B + B - h], Hw.indirect(T.HL[:, h // 16:64]), nv[:, h:B], Op.is_equal, Hr + ["HL", k], ["EQ0"], c=GA)
-        tt(T.EQ[:, e0:e0 + h], Hw.indirect(T.HL[:, 0:h // 16]), nv[:, 0:h], Op.is_equal, Hr + ["HL", k], ["EQ1"], c=GA)
+    def check(x0, nv=T.NV, k="NV", parts=2):
+        n = B // parts
+        for c in range(parts):
+            tt(T.EQ[:, n * c:n * c + n], Hw.indirect(T.HL[:, n * c // 16:n * (c + 1) // 16]), nv[:, x0 + n * c:x0 + n * c + n], Op.is_equal, Hr + ["HL", k],
+               ["EQ%d" % c] if parts == 2 else ["EQ0", "EQ1"], c=GA)
 
     h = V // 2
     dma("s", C[:, ao:ao + h], T.al[:, 0:h], "dal", [], ["Aown"], final=32)
@@ -280,22 +332,24 @@ def rank_program(g, core, T, topo):
     dma("s", T.XI[0:128:16, :], T.hb[:], "dhb", [], ["XI", "~s"])
     dma("s", T.hnI[:], T.hn[:], "dhn", [], ["hnI", "~s"])
     dma("s", T.TX[:, 0:B], T.ft[:], "dft", [], ["TX", "~s"], final=32)
-    dma("s", T.TX[:, B:B + 32], T.ft[:, 0:32], "dft", [], ["TX2", "~s"], final=32)
+    dma("s", T.TX[:, B:LW], T.ft[:, 0:LW - B], "dft", [], ["TX2", "~s"], final=32)
     dma("s", T.TU[:, 0:B], T.ut[:], "dut", [], ["TU", "~s"], final=32)
-    dma("s", T.TU[:, B:B + 32], T.ut[:, 0:32], "dut", [], ["TU2", "~s"], final=32)
-    dma("s", T.TX[:, B + 32:TW], T.ft[:, 32:TW - B], "dmon", ["TX", "TU"], ["TX3"], final=48)
-    dma("s", T.TU[:, B + 32:TW], T.ut[:, 32:TW - B], "dmon", ["TX", "TU"], ["TU3"], final=48)
-    dma("s", T.monb[:], T.mon[:], "dmon", ["TX", "TU"], ["monb"], final=48)
+    dma("s", T.TU[:, B:LW], T.ut[:, 0:LW - B], "dut", [], ["TU2", "~s"], final=32)
+    for x, y, k in ((T.TX, T.ft, "TX"), (T.TU, T.ut, "TU")):
+        dma("s", x[:, LW:2 * B], y[:, LW - B:B], "dmon", ["TX", "TU"], [k + "3"], final=80)
+        dma("s", x[:, 2 * B:TW], y[:, 0:TW - 2 * B], "dmon", ["TX", "TU"], [k + "4"], final=80)
+    dma("s", T.monb[:], T.mon[:], "dmon", ["TX", "TU"], ["monb"], final=80)
 
     iota(T.cI[:, 0:1], [[0, 1]], 0, 1, ["cI"], small=False)
     iota(TMP[:], [[1, 144]], 0, 0, ["TMP"])
     iota(T.C16[:], [[0, 16], [1, 16]], 0, 0, ["C16"])
     iota(IO[:, 0:L], [[1, L]], 0, 0, ["IO"])
-    snd = _senders(core, topo)
-    pcs = [[_piece(T, part, me, i, len(snd)) for i in range(len(snd))] for part in range(2)]
+    snd, snd1 = _senders(core, topo, 0), _senders(core, topo, 1)
+    pcs = [[_piece(T, part, me, i, len(x)) for i in range(len(x))] for part, x in enumerate((snd, snd1))]
     send(snd[1:], pcs[0][1:], pcs[0][1:], "feed0", ["Aown", "Aown2", "IO", "C16"], 2.0)
+    arrive("A2", "ag0", 4 * len(snd) * KE, LINK * 1.5 * PW[0], "link2", 4.0)
     send(peers, [pcs[0][0]] * 4, [pcs[0][0]] * 4, "ag0", [])
-    arrive("A", "ag0", 4 * len(snd) * KE, 6.0)
+    arrive("A", "ag0", 4 * len(snd) * KE, LINK * (V - 2.7 * PW[0]))
     for c0, c9, b0, k in ((L, B, L, "IO1"), (B, TW, 0, "IO2")):
         iota(IO[:, c0:c9], [[1, c9 - c0]], b0, 0, [k, "~sent"])
 
@@ -309,111 +363,132 @@ def rank_program(g, core, T, topo):
     ts(IDN, REL, rcol, Op.is_equal, ["REL"], ["IDN"])
     ts(TM2, REL, 0.0, Op.is_ge, ["REL"], ["TM2"])
     ts(BLK, REL, 16.0, Op.is_lt, ["REL"], ["BLK"])
-    ts(NUP, REL, rcol, Op.is_lt, ["REL"], ["NUP"], -1.0, Op.mult)
+    ts(NUP, REL, rcol, Op.is_lt, ["REL"], ["NUP"])
     ts(T.EK[:], TMP[:, 0:16], rcol, Op.is_equal, ["TMP", "cF"], ["EK"])
     tt(BLK, BLK, TM2, Op.mult, ["TM2", "BLK"], ["BLK"], c=2)
     ts(J16, TMP[:, 0:16], 16.0, Op.mult, ["TMP", "cF"], ["J16"], rcol, Op.add)
     ts(T.EQ[:], T.XI[:], W - 0.5, Op.is_lt, ["XI", "r0"], ["EQ0", "EQ1"], r0, Op.mult)
     tt(NUP, NUP, BLK, Op.mult, ["NUP", "BLK"], ["NUP"], c=2)
+    tt(UPM, BLK, NUP, Op.subtract, ["NUP", "BLK"], ["UPM"], c=2)
     ts(JB, J16, 0.5, Op.add, ["J16"], ["JB"])
-    act(pw4, rcol, ["cF"], ["pw4"], func=AF.Exp, scale=-math.log(4.0), c=1500.0)
-    act(T.SCL[:], T.C16[:], ["C16", "pw4"], ["SCL"], func=AF.Exp, scale=8.0 * math.log(2.0), bias=-60.0 * math.log(2.0))
+    ts(J1, J16, 1.0, Op.add, ["J16"], ["J1"])
+    ms(T.inc[:, 0:2], 0.0, ["inc0"])
+    ms(T.six[:], 16.0, ["six"])
+    ts(I16, IDN, 16.0, Op.mult, ["IDN"], ["I16"])
+    ts(T.I8F[:], IDN, 8.0, Op.mult, ["IDN"], ["I8F"])
+    block(lambda: [act(T.SCL[:, x:y], TMP[:, 0:y - x], [], [], func=AF.Exp, scale=8.0 * math.log(2.0), bias=-84.0 * math.log(2.0), c=25.0) for x, y in zip(SEG, SEG[1:])],
+          ["TMP"], ["SCL"])
+    for x in (CH, 2 * CH):
+        act(T.SCL[:, x:2 * x], T.SCL[:, 0:x], ["SCL"], ["SCL"])
     hf, ab, c1, c2 = T.G[:, 0:V], T.MX[:, 0:V], T.TOP[:, 0:V], T.TOP[:, B:B + V]
     cp(hf, T.hnI[:], ["hnI"], Gk)
     ts(c1, T.hnI[:], 0.5, Op.is_gt, ["hnI"], Tk[0:4], -float(TAG), Op.mult)
     ts(c2, T.hnI[:], N * B + 0.5, Op.is_gt, ["hnI"], Tk[4:8], -6.0 * TAG, Op.mult)
-    act(ab, hf, Gk, Mk, func=AF.Abs)
+    MA = Mk + [x + "a" for x in Mk]
+    act(ab, hf, Gk, MA, func=AF.Abs)
     for c0, c9, k in ((0, 512, "U2"), (512, V, "U3")):
         mm(T.PU1[:, c0:c9], IDN, T.TOP[:, c0:c9], True, False, Tk[0:4] + ["IDN"], [k])
         mm(T.PU1[:, c0:c9], IDN, T.TOP[:, B + c0:B + c9], False, True, Tk[4:8], [k])
-    tt(C[:, ho:ho + V], T.PU1[:, 0:V], ab, Op.subtract, ["U2", "U3"] + Mk, ["Hown"])
-    send(snd[1:], pcs[1][1:], pcs[1][1:], "feed1", ["Hown"])
+    tt(C[:, ho:ho + V], T.PU1[:, 0:V], ab, Op.subtract, ["U2", "U3"] + MA, ["Hown"])
+    send(snd1[1:], pcs[1][1:], pcs[1][1:], "feed1", ["Hown"])
+    arrive("H2", "ag1", 4 * len(snd1) * KE, LINK * 3 * PW[1], "link2", 3.0)
     send(peers, [pcs[1][0]] * 4, [pcs[1][0]] * 4, "ag1", ["A"])
-    arrive("H", "ag1", 4 * len(snd) * KE, 7.0)
+    arrive("H", "ag1", 4 * len(snd1) * KE, LINK * 2 * (V - 2 * PW[1]))
     block(lambda: [act(T.BRD[:, k, :], BLK, [], [], scale=T.EK[:, k:k + 1]) for k in range(16)], ["BLK", "EK"], ["BRD"])
     ms(T.RS64[:], 1.0, ["RS64"])
     ms(C[:, W:HO], 0.0, ["Az"])
     ms(C[:, HO + W:DO], 1.0, ["Hz"])
     ms(T.RS64[:, 0:B:64], 0.0, ["RS64"])
     act(T.IDNF[:], IDN, ["IDN"], ["IDNF"])
+    act(T.NIDF[:], IDN, ["IDN"], ["NIDF"], scale=-1.0)
 
     def constants():
         ts(T.XR[:, 0:B], T.XI[:], -float(MID), Op.add, ["XI"], ["XR"])
         ts(T.SELF[:], SEL, r0, Op.mult, ["SEL", "r0"], ["SELF"])
         ts(ebias, rcol, -120.0, Op.add, ["cF"], ["eb"], -math.log(2.0), Op.mult)
-        ts(rh, rcol, 0.5, Op.mult, ["cF"], ["rh"])
         ts(D2M, IDN, 2.0, Op.mult, ["IDN"], ["D2M"])
-        ts(c192, rcol, 192.0, Op.add, ["cF"], ["c192"])
+        ts(first, rcol, float(V), Op.mult, ["cF"], ["first"], -MID - 0.5, Op.add)
+        ts(DF8, REL, 1.0, Op.add, ["REL"], ["DF8"], rcol, Op.is_equal)
+        tt(DF, IDN, DF8, Op.subtract, ["IDN", "DF8"], ["DF"], c=2)
+        act(DF8, DF, ["DF"], ["DF8"], scale=float(TAG))
         tt(D2M, D2M, BLK, Op.subtract, ["D2M", "BLK"], ["D2M"], c=2)
         ts(DUM, J16, float(DO), Op.add, ["J16"], ["DUM"])
-        ts(JD, J16, float(B), Op.add, ["J16"], ["JD"])
-        ts(T.JH[:], J16, 16.0, Op.mult, ["J16"], ["JH"], 60.0, Op.add)
-        ts(T.SELH[:], SEL, 1.0 - OHS / 2, Op.mult, ["SEL"], ["SELH"])
+        ts(T.JH[:, 0:16], J16, 0.0, Op.mult, ["J16"], ["JH0"])
+        ts(T.JH[:, 16:32], J16, 16.0, Op.mult, ["J16"], ["JH"])
+        ts(T.JK[:], J16, 16.0, Op.mult, ["J16"], ["JK"], 60.0, Op.add)
+        ts(rh, rcol, 0.5, Op.mult, ["cF"], ["rh"])
         ts(SELK, SEL, rh, Op.mult, ["SEL", "rh"], ["SELK"])
-        ts(BLKH, BLK, 1.0 - OHS / 2, Op.mult, ["BLK"], ["BLKH"])
+        cp(T.SELH[:], SEL, ["SEL"], ["SELH"])
+        cp(BLKH, BLK, ["BLK"], ["BLKH"])
+        cp(T.colu[:], TMP[:, 0:16], ["TMP"], ["colu"])
         cp(IDNH, IDN, ["IDN"], ["IDNH"])
         ts(T.TRI[:], T.C16[:], rcol, Op.is_le, ["C16", "cF"], ["TRI"], float(TAG), Op.mult, c=0.5)
         ts(T.dg[:], T.C16[:], rcol, Op.not_equal, ["C16", "cF"], ["dg"], 8.0 * HO, Op.mult, c=0.5)
         ms(T.RSY[:], -65536.0, ["RSY"])
-        cp(T.C256[:], IO[:, 0:L], ["IO"], ["C256"])
         ts(T.NEM[:], T.dg[:], float(MID), Op.add, ["dg"], ["NEM"], c=0.5)
         ts(T.RSY[:, 0:L:16], DUM, -8.0 * HO, Op.add, ["DUM"], ["RSY"])
         ts(T.SG[:, 0, :], TMP[:, 0:8], rcol, Op.is_lt, ["TMP", "cF"], ["SG0"], 0.125, Op.mult)
         ts(T.SG[:, 1, :], T.SG[:, 0, :], -0.0625, Op.add, ["SG0"], ["SG1"])
         ts(T.SG[:, 0, :], T.SG[:, 1, :], 15.0, Op.mult, ["SG1"], ["SG0"])
-        act(pw4f, pw4, ["pw4"], ["pw4f"], scale=-(2.0 ** 80))
-        act(NL1, D2M, ["D2M", "pw4f"], ["NL1"], scale=pw4f)
-        act(NL2, NL1, ["NL1"], ["NL2"], scale=2.0 ** -32)
+        tt(DNM, NUP, D2M, Op.add, ["NUP", "D2M"], ["DNM"], c=2)
+        tt(THM, BLK, I16, Op.subtract, ["BLK", "I16"], ["THM"], c=2)
+        act(DNM, DNM, ["DNM"], ["DNM"], scale=-(2.0 ** 18))
+        act(THM, THM, ["THM"], ["THM"], scale=float(TAG))
         block(lambda: [act(m, BLK, [], [], scale=c) for m, c in (
             (B4K, TAG / 2), (B9, -9.0 * TAG / 16), (BN24, -(2.0 ** 24)), (BN8, -float(TAG)), (B05, 0.5), (BNC, -12.0 * TAG), (BBG, 4.0 * HO),
             (BN2K, -HO / 2))], ["BLK"], ["BX"])
+        act(B15, T.BRD[:, 15, :], ["BRD"], ["B15"], scale=2.0 * TAG)
         act(I8K, IDN, ["IDN"], ["I8K"], scale=float(TAG))
         act(T.NV[:, 0:B], IO[:, 0:B], ["IO", "IO1"], ["NV"], func=AF.Identity, scale=-1.0, bias=-float(name0))
         act(T.NV1[:], IO[:, 0:B], ["IO", "IO1"], ["NV1"], func=AF.Identity, scale=-1.0, bias=-float(TAG + name0))
-        holdings(2)
+        holdings(0, 2)
         ts(T.HL[:], U[1][0][:, 0:64], float(MID), Op.add, ["U1"], ["HL"])
 
     for t in range(RO):
-        w0 = (L * t) % B
-        win = slice(w0, w0 + 1056)
+        w0, x0 = (L * t) % B, L * t
+        win = slice(w0, w0 + LW)
+        count.clear()
+        stage[0] = "round" if t else "first"
         if t > 0:
-            check(w0)
+            check(x0, parts=1)
         hz = T.PC[:, 0:64]
+        block(lambda: [mm(T.PA[:, 0:64], BLK, T.EQ[:, r:B:16], r == 0, r == 15, [], []) for r in range(16)], ["EQ0", "EQ1", "BLK"], ["PA"])
+        scan(T.ends[:], T.six[:], T.PA[:, 0:64], 0.0, Op.add, Op.subtract, ["PA", "six"], ["ends"])
         sel16(hz, lambda r: T.EQ[:, r:B:16], ["EQ0", "EQ1"], ["PC"])
-        scan(T.inc[:], T.ONE[:, 0:64], hz, 0.0, Op.add, Op.subtract, ["PC", "ONE"], ["inc"])
-        ts(T.hl[:], hz, 0.5, Op.is_lt, ["PC"], ["hl"])
-        mm(T.PA[:, 0:64], BLK, T.inc[:], True, True, ["inc", "BLK"], ["PA"])
-        mm(T.PD[:, 0:64], BLK, T.inc[:], True, True, ["inc", "BLK"], ["PD"])
-        mm(T.PB[:, 64:65], BLK, T.inc[:, 63:64], True, True, ["inc", "BLK"], ["PB"])
-        mm(T.PB[:, 0:64], BLK, T.inc[:], True, False, ["inc"], ["PB"])
-        mm(T.PB[:, 0:64], NUP, T.hl[:], False, True, ["hl", "NUP"], ["PB"])
-        cp(T.P[:, 0:65], T.PB[:, 0:65], ["PB"], ["P"])
+        inc, inc0 = T.inc[:, 2:66], T.inc[:, 1:65]
+        scan(inc, T.ONE[:, 0:64], hz, 0.0, Op.add, Op.subtract, ["PC", "ONE"], ["inc"])
+        mm(T.PB[:, 64:65], BLK, inc[:, 63:64], True, True, ["inc", "BLK"], ["PB"])
+        mm(T.PB[:, 0:64], UPM, inc, True, False, ["inc", "UPM"], ["PB"])
+        mm(T.PB[:, 0:64], NUP, inc0, False, True, ["inc", "inc0", "NUP"], ["PB"])
+        (act if PSC else cp)(T.P[:, 0:65], T.PB[:, 0:65], ["PB"], ["P"])
+        ts(T.spare[:], J1, T.P[:, 64:65], Op.subtract, ["J1", "P"], ["spare"], 0.0, Op.max)
         for m0, m1, s, ps, k in ((0, M0, "0", T.PC[:, 64:80], "PC"), (M0, 16, "1", T.PB[:, 80:96], "PB")):
-            c, ma = slice(16 * m0, 16 * m1), min(m1, NA)
-            block(lambda: [act(T.junk[:, 64 * m:64 * m + 64], T.PA[:, 0:64], [], [], func=AF.Sign, scale=-1.0, bias=JB[:, m:m + 1], c=1.4,
-                               accum_out=T.acc[:, m:m + 1]) for m in range(m0, ma)], ["PA", "JB"], ["acc" + s])
-            if m0:
-                for x in range(NA, 16, 2):
-                    block(lambda: [ts(T.junk[:, 64 * m:64 * m + 64], T.PD[:, 0:64], JB[:, m:m + 1], Op.is_lt, [], [], 16.0, Op.mult) for m in (x, x + 1)],
-                          ["PD", "JB"], ["junk%d" % x])
-                scan(T.cs[:, 64 * NA:B], T.RS64[:, 64 * NA:B], T.junk[:, 64 * NA:B], 0.0, Op.mult, Op.add, ["junk%d" % x for x in range(NA, 16, 2)] + ["RS64"], ["cs"], c=0.5)
-                ts(T.cL[:, NA:16], T.cs[:, 64 * NA + 63:B:64], 0.0625, Op.mult, ["cs"], ["cL2"])
-            ts(T.cL[:, m0:ma], T.acc[:, m0:ma], 64.0, Op.add, ["acc" + s], ["cL" + s], 0.5, Op.mult)
-            ts(T.cs[:, 64 * m0 + 63:64 * ma:64], T.acc[:, m0:ma], 64.0, Op.add, ["acc" + s], ["cs" + s], 8.0, Op.mult)
-            tt(T.cmp[:, c], T.P[:, 0:65].indirect(T.cL[:, m0:m1]), IO[:, c], Op.is_le, ["P", "IO", "cL" + s] + ["cL2"] * m0, ["cmp" + s], c=GA)
-            mm(ps[:, m0:m1], IDN, T.cs[:, 64 * m0 + 63:64 * m1:64], True, False, ["cs" + s, "IDN"] + ["cs"] * m0, [k])
+            c, ma = slice(16 * m0, 16 * m1), m0 + NS[m0 > 0]
+            mm(ps[:, m0:m1], IDN, T.spare[:, m0:m1], True, False, ["spare", "IDN"], [k])
+            if ma > m0:
+                block(lambda: [act(T.junk[:, 64 * m:64 * m + 64], T.ends[:], [], [], func=AF.Sign, scale=-1.0, bias=JB[:, m:m + 1], c=1.4,
+                                   accum_out=T.acc[:, m:m + 1]) for m in range(m0, ma)], ["ends", "JB"], ["acc" + s, "junkS" + s])
+                ts(T.cL[:, m0:ma], T.acc[:, m0:ma], 64.0, Op.add, ["acc" + s], ["cL" + s], 0.5, Op.mult)
+                mm(ps[:, m0:ma], T.I8F[:], T.acc[:, m0:ma], False, False, ["acc" + s, "I8F"], [k], c=4.0)
+            if ma < m1:
+                for x in range(ma, m1, 2):
+                    block(lambda: [ts(T.junk[:, 64 * m:64 * m + 64], T.ends[:], JB[:, m:m + 1], Op.is_lt, [], [], 0.5, Op.subtract) for m in (x, x + 1)],
+                          ["ends", "JB"], ["junk%d" % x])
+                scan(T.cs[:, 64 * ma:64 * m1], T.RS64[:, 64 * ma:64 * m1], T.junk[:, 64 * ma:64 * m1], 0.0, Op.mult, Op.add, ["junk%d" % x for x in range(ma, m1, 2)] + ["RS64"],
+                     ["cs" + s], c=0.5)
+                ts(T.cL[:, ma:m1], T.cs[:, 64 * ma + 63:64 * m1:64], 32.0, Op.add, ["cs" + s], ["cV" + s])
+                mm(ps[:, ma:m1], I16, T.cs[:, 64 * ma + 63:64 * m1:64], False, False, ["cs" + s, "I16"], [k])
+            tt(T.cmp[:, c], T.P[:, 0:65].indirect(T.cL[:, m0:m1]), IO[:, c], Op.is_le, ["P", "IO", "cL" + s, "cV" + s], ["cmp" + s], c=GA)
             sel16(ps[:, m0:m1], lambda r: T.cmp[:, 16 * m0 + r:16 * m1:16], ["cmp" + s], [k], st=False)
-            cp(T.bL[:, m0:m1], ps[:, m0:m1], [k], ["bL" + s])
-            cp(T.FO[:, c], T.TX[:, win].indirect(T.bL[:, m0:m1]), ["TX", "TX2", "bL" + s] + ["TX3"] * t, ["FO" + s], c=GA)
-            tt(T.ug[:, c], T.TU[:, win].indirect(T.bL[:, m0:m1]), T.SCL[:, c], Op.mult, ["TU", "TU2", "SCL", "bL" + s] + ["TU3"] * t, ["ug" + s], c=GA)
+            ts(T.bL[:, m0:m1], ps[:, m0:m1], 512.0, Op.add, [k], ["bL" + s])
+            cp(T.FO[:, c], T.TX[:, win].indirect(T.bL[:, m0:m1]), ["TX", "TX2", "bL" + s] + ["TX3", "TX4"] * t, ["FO" + s], c=GA)
+            tt(T.ug[:, c], T.TU[:, win].indirect(T.bL[:, m0:m1]), T.SCL[:, c], Op.mult, ["TU", "TU2", "SCL", "bL" + s] + ["TU3", "TU4"] * t, ["ug" + s], c=GA)
         if t == 0:
             constants()
-        ts(invL, J16, T.P[:, 64:65], Op.is_ge, ["J16", "P"], ["invL"], 2.0 * TAG, Op.mult)
         ts(T.xc[:], T.FO[:], -float(MID), Op.add, ["FO0", "FO1"], ["xc"], c=0.5)
-        ts(T.inv[:], T.C256[:], T.P[:, 64:65], Op.is_ge, ["C256", "P"], ["inv"], 2.0, Op.mult, c=0.5)
 
         def products(ci):
-            s, (ua, ka), (ub, kb) = "01"[ci > 0], U[2 * ci % 4], U[2 * ci % 4 + 1]
+            s, (ua, ka), (ub, kb) = "01"[ci > 0], U[UB[ci][0]], U[UB[ci][1]]
             j0, n1 = CH * ci, CH // PARTS[ci]
             for o, (u1, k1) in enumerate(((ua, ka), (ub, kb))):
                 block(lambda: [mm(u1[:, k:512:8], T.BRD[:, 2 * k + o, :], T.ug[:, j0:j0 + CH], True, True, [], []) for k in range(8)], ["ug" + s, "BRD"], [k1])
@@ -426,151 +501,178 @@ def rank_program(g, core, T, topo):
                     tt(ub[:, c], T.G[:, 16 * j + 1:16 * (j + n1):2], ub[:, c], Op.mult, gk + [kb], [kb])
                 else:
                     tt(T.E[:, 16 * j + 1:16 * (j + n1):2], T.G[:, 16 * j + 1:16 * (j + n1):2], ub[:, c], Op.mult, gk + [kb], ek[1::2])
+            if FAR[ci]:
+                mm(U[UB[ci][2]][0][:, 0:4 * CH], T.IDNF[:], T.E[:, 16 * j0 + 1:16 * (j0 + CH):4], True, False, Ek[4 * ci:4 * ci + 4] + ["IDNF"], [U[UB[ci][2]][1]], c=4.0)
 
         def largest(ci):
-            j0, (ub, kb), (pm, km), r = CH * ci, U[2 * ci % 4 + 1], PM[ci % 2], REP[ci]
-            block(lambda: [scan(T.MX[:, 8 * j:8 * j + 128], T.E[:, 16 * j:16 * j + 256:2], ub[:, 8 * (j - j0):8 * (j - j0) + 128] if KEEP[ci] else T.E[:, 16 * j + 1:16 * j + 256:2],
-                                0.0, Op.max, Op.max, [], []) for j in range(j0, j0 + CH, 16)], Ek[4 * ci:4 * ci + 4] + [kb] * KEEP[ci], [Mk[ci]])
-            block(lambda: [mm(pm[:, i:r * CH:r], T.IDNF[:], T.MX[:, 8 * j0 + 7:8 * (j0 + CH):8], True, True, [], [], c=4.0) for i in range(r)], [Mk[ci], "IDNF"], [km])
+            j0, (ub, kb), (pm, km), r = CH * ci, U[UB[ci][1]], PM[ci], REP[ci]
+            cut = list(zip(SEG, SEG[1:]))
+            for part, ek, mk in ((cut[:1], Ek[4 * ci:4 * ci + 2], Mk[ci] + "a"), (cut[1:], Ek[4 * ci:4 * ci + 4], Mk[ci])):
+                block(lambda: [scan(T.MX[:, 8 * (j0 + x):8 * (j0 + y)], T.E[:, 16 * (j0 + x):16 * (j0 + y):2], ub[:, 8 * x:8 * y] if KEEP[ci] else T.E[:, 16 * (j0 + x) + 1:16 * (j0 + y):2],
+                                    0.0, Op.max, Op.max, [], []) for x, y in part], ek + [kb] * KEEP[ci], [mk])
+            block(lambda: [mm(pm[:, i:r * CH:r], T.IDNF[:], T.MX[:, 8 * j0 + 7:8 * (j0 + CH):8], True, True, [], [], c=4.0) for i in range(r)], [Mk[ci], Mk[ci] + "a", "IDNF"], [km])
 
         def marks(ci):
-            j0, (ub, kb), (pm, km), r = CH * ci, U[2 * ci % 4 + 1], PM[ci % 2], REP[ci]
-            c0, c9 = 16 * j0, 16 * (j0 + CH)
+            j0, (ub, kb), (pm, km), r = CH * ci, U[UB[ci][1]], PM[ci], REP[ci]
+            c0, c9, M = 16 * j0, 16 * (j0 + CH), T.MX[:, 8 * j0 + 7:8 * (j0 + CH):8]
             if KEEP[ci]:
-                M = T.MX[:, 8 * j0 + 7:8 * (j0 + CH):8]
-                block(lambda: [tt(T.TOP[:, c0 + 2 * k + 1:c9:16], ub[:, k:512:8], M, Op.is_lt, [], []) for k in range(8)], [kb, Mk[ci]], [Tk[4 * ci + 1], Tk[4 * ci + 3]])
-            for x, o in enumerate((1, 3, 0, 2) if KEEP[ci] else (0, 1, 2, 3)):
-                if not (KEEP[ci] and o % 2):
+                block(lambda: [tt(T.TOP[:, c0 + 2 * k + 1:c9:16], ub[:, k:512:8], M, Op.is_lt, [], []) for k in range(8)], [kb, Mk[ci], Mk[ci] + "a"], [Tk[4 * ci + 1], Tk[4 * ci + 3]])
+            if FAR[ci]:
+                uc, kc = U[UB[ci][2]]
+                block(lambda: [mm(uc[:, k:4 * CH:4], T.NIDF[:], M, False, k == 3, [], [], c=4.0) for k in range(4)], [Mk[ci], Mk[ci] + "a", "NIDF"], [kc])
+                act(T.TOP[:, c0 + 1:c9:4], uc[:, 0:4 * CH], [kc], [Tk[4 * ci + 1]], func=AF.Sign, scale=-1.0)
+            for x, o in enumerate((1, 3, 0, 2) if KEEP[ci] else (0, 2, 3, 1)):
+                if not (KEEP[ci] and o % 2 or FAR[ci] and o == 1):
                     block(lambda: [tt(T.TOP[:, c0 + i:c9:16 // r], T.E[:, c0 + i:c9:16 // r], pm[:, 0:r * CH], Op.is_lt, [], []) for i in range(o, 16 // r, 4)],
                           [km] + Ek[4 * ci:4 * ci + 4], [Tk[4 * ci + o]])
-                block(lambda: [mm(T.PA[:, j0:j0 + CH] if j0 < LA else U[2][0][:, 0:CH], SEL[:, 16 - k:144 - k], T.TOP[:, c0 + k:c9:16], x == 0 and k == o,
-                                  x == 3 and k == 12 + o, [], []) for k in range(o, 16, 4)], [Tk[4 * ci + o], "SEL"], ["PA" if j0 < LA else "U2"])
+                uv, kv = (U[BK[1][0]][0][:, j0 - LA:j0 - LA + CH], U[BK[1][0]][1]) if VB and j0 >= LA else (T.PA[:, j0:j0 + CH], "PA")
+                block(lambda: [mm(uv, SEL[:, 16 - k:144 - k], T.TOP[:, c0 + k:c9:16], x == 0 and k == o,
+                                  x == 3 and k == 12 + o, [], []) for k in range(o, 16, 4)], [Tk[4 * ci + o], "SEL"], [kv])
 
         def choose(s):
-            lo, hi = (0, LA) if s == "A" else (LA, L)
+            lo, hi, ko, kp, kx = STG[s]
             n, c, m = hi - lo, slice(lo, hi), slice(lo // 16, hi // 16)
             k = lambda *x: [y + s for y in x]
             at = lambda b, c0, w=n: ({"PA": T.PA, "PB": T.PB, "PC": T.PC, "PD": T.PD}.get(b) or U[int(b[1])][0])[:, c0:c0 + w]
-            if s == "A":
-                kv, k2, ko, kp, kt, kx, ks = "PA", "PB", "PC", "U1", "PB", "U0", "PA"
-                VT, D2, OH, D3, XP, TK, XS = at(kv, 0), at(k2, 0), at(ko, L), at(ko, 0), at(kp, 0, n // 16), at(kt, L, n // 16), at(ks, L)
-            else:
-                kv, k2, ko, kp, kt, kx, ks = "U2", "U2", "U3", "PD", "U2", "U3", "U2"
-                VT, D2, OH, D3, XP, TK, XS = at(kv, 0), at(k2, n), at(ko, 0), at(ko, n), at(kp, 0, n // 16), at(kt, L, n // 16), at(ks, 2 * n)
-            XV, FA, TH, DN, one = at(kx, lo), at(kx, L + lo), at(kp, L + lo), OH, T.ONE[:, 0:n]
+            kv, kf = "PA", kx
+            VT, OH, D3, XP, TK, XV, FA, TH = at(kv, lo), at(ko, L), at(ko, 0), at(kp, 0, n // 16), at(kp, n // 16, n // 16), at(kx, 0), at(kx, L), at(kp, L)
+            DN, one = OH, T.ONE[:, 0:n]
             XL, TKL = T.XL[:, m], T.tk[:, m]
             act(T.w[:, c], VT, [kv, "eb"], k("w"), func=AF.Exp, scale=-16.0 * math.log(2.0), bias=ebias)
-            if s == "A":
-                sel16(XP, lambda r: T.xc[:, r:hi:16], ["xc", "SELH"], [kp], mat=T.SELH, sp=False)
-                mm(XV, BLKH, T.xc[:, c], True, False, ["xc", "BLKH"], [kx])
-                mm(D2, D2M, T.w[:, c], True, True, k("w") + ["D2M"], [k2])
-                mm(XS, BLKH, T.xc[:, c], True, False, ["xc", "BLKH"], [ks])
-                act(OH, D2, [k2], [ko], func=AF.Sign)
+            Z, ZK, XT = T.Z[:, 2 * lo:2 * lo + n], T.Z[:, 2 * lo + n:2 * hi], at(kp, 0, n // 8)
+            mm(D3, D2M, T.w[:, c], True, True, k("w") + ["D2M"], [ko])
+            kt = kp
+            if s in CHM:
+                mm(XT, IDNH, T.JH[:, 16 - n // 16:16 + n // 16], True, False, ["IDNH", "JH", "JH0"], [kp])
+                ts(OH, D3, 0.0, Op.is_ge, [ko], k("OH"))
+                ts(ZK, D3, 0.0, Op.is_ge, [ko, "cF"], k("ZK"), rcol, Op.mult)
+                tt(Z, OH, T.xc[:, c], Op.mult, [ko, "xc"] + k("OH"), k("Z"))
+                sel16(XT, lambda r: T.Z[:, 2 * lo + r:2 * hi:16], k("Z", "ZK") + ["SELH"], [kp], mat=T.SELH, st=False)
             else:
-                mm(D3, D2M, T.w[:, c], True, True, k("w") + ["D2M"], [ko])
-                mm(D2, D2M, T.w[:, c], True, True, k("w") + ["D2M"], [k2])
-                ts(OH, D3, 0.0, Op.is_ge, [ko], [ko], 2.0, Op.mult)
-            act(T.sg[:, c], D2, [k2], k("sg"), func=AF.Sign)
-            tt(T.Z[:, c], OH, T.xc[:, c], Op.mult, [ko, "xc"], k("Z"))
-            sel16(XP, lambda r: T.Z[:, lo + r:hi:16], k("Z") + ["SELH"], [kp], mat=T.SELH, st=s == "B")
-            mm(XV, BLKH, T.Z[:, c], s == "B", True, k("Z"), [kx])
-            mm(XS, BLKH, T.Z[:, c], s == "B", True, k("Z"), [ks])
+                kt = kx if s in TKX else "PB"
+                TK = at(kt, 2 * L - 16, n // 16)
+                act(T.sg[:, c], D3, [ko], k("sg"), func=AF.Sign)
+                act(OH, T.sg[:, c], k("sg"), [ko], func=AF.Relu)
+                tt(Z, OH, T.xc[:, c], Op.mult, [ko, "xc"], k("Z"))
+                sel16(XP, lambda r: T.Z[:, 2 * lo + r:2 * lo + n:16], k("Z") + ["SELH"], [kp], mat=T.SELH)
+
+            mm(XV, BLKH, Z, True, True, k("Z") + ["BLKH"], [kx])
             ts(XL, XP, float(MID), Op.add, [kp], k("XL"))
-            cp(T.XLf[:, m], XP, [kp], k("XLf"))
-            cp(T.XLh[:, m], XP, [kp], k("XLh"))
+            (act if XLS else cp)(T.XLf[:, m], XP, [kp], k("XLf"))
+            if DGG:
+                tt(T.xd[:, c], XV, T.TRI[:, c], Op.add, [kx, "TRI"], k("xd"))
+            else:
+                cp(T.XLh[:, m], XP, [kp], k("XLh"))
             cp(T.xr[:, c], XV, [kx], k("xr"))
-            mm(TK, IDNH, T.JH[:, 0:n // 16], True, False, ["IDNH", "JH"], [kt])
-            sel16(TK, lambda r: T.sg[:, lo + r:hi:16], k("sg") + ["SELK"], [kt], st=False, mat=SELK)
+            if s not in CHM:
+                mm(TK, IDNH, T.JK[:, 0:n // 16], True, False, ["IDNH", "JK"], [kt])
+                sel16(TK, lambda r: T.sg[:, lo + r:hi:16], k("sg") + ["SELK"], [kt], st=False, mat=SELK)
             act(T.SA[:, c], Aw.indirect(XL), Ar + k("XL"), k("SA"), func=AF.Sign, c=GA)
-            if HCS and s == "A":
+            if s in HCS:
                 act(T.Hc[:, c], Hw.indirect(XL), Hr + k("XL"), k("Hc"), c=GA)
             else:
                 cp(T.Hc[:, c], Hw.indirect(XL), Hr + k("XL"), k("Hc"), c=GA)
             cp(TKL, TK, [kt], k("tk"))
-            act(T.EM[:, c], Hw.indirect(XL), Hr + k("XL"), k("EM"), func=AF.Relu, bias=1.0, c=GA)
+            if s in EMV:
+                ts(T.EM[:, c], Hw.indirect(XL), -0.5, Op.is_gt, Hr + k("XL"), k("EM"), c=GA)
+            else:
+                act(T.EM[:, c], Hw.indirect(XL), Hr + k("XL"), k("EM"), func=AF.Relu, bias=1.0, c=GA)
             mm(TH, B9, one, True, False, ["BX", "ONE"], [kp])
-            mm(TH, B4K, T.SA[:, c], False, True, k("SA"), [kp])
+            left = [2]
+            mm(TH, B4K, T.SA[:, c], False, left, k("SA"), ["+" + kp])
+            mm(TH, THM, T.EM[:, c], False, left, k("EM") + ["THM"], ["+" + kp])
             tt(T.AV[:, c], T.Hc[:, c], TH, Op.is_gt, k("Hc") + [kp], k("AV"))
-            mm(DN, BLK, one, True, False, ["ONE"], [ko])
-            mm(DN, NL1, T.EM[:, c], False, False, k("EM") + ["NL1"], [ko])
-            mm(DN, NL2, T.AV[:, c], False, True, k("AV") + ["NL2"], [ko])
+            block(lambda: [mm(DN, BBG, one, True, False, [], []), mm(DN, T.IDNF[:], T.nv[:, c], False, False, [], [], c=4.0)], ["ONE", "BX", "nv"], [ko])
+            mm(DN, DNM, T.AV[:, c], False, True, k("AV") + ["DNM"], [ko])
             act(T.fc[:, c], T.TOP[:, 16 * lo:16 * hi].indirect(TKL), k("tk") + ["SG0", "SG1"] + Tk[m], k("fc"), func=AF.Identity,
                 scale=T.SG[:, 1, t:t + 1], bias=T.SG[:, 0, t:t + 1], c=GA)
             act(T.AA[:, c], Aw.indirect(XL), Ar + k("XL"), k("AA"), func=AF.Abs, c=GA)
-            block(lambda: [mm(FA, IDN, T.fc[:, c], True, False, [], []), mm(FA, BN24, T.AV[:, c], False, True, [], [])], k("AV", "fc"), [kx])
-            tt(D3, DN, T.nv[:, c], Op.max, [ko, "nv"], [ko])
-            tt(FA, FA, T.AA[:, c], Op.mult, [kx] + k("AA"), [kx])
-            tt(T.X[:, c], D3, T.Hc[:, c], Op.min, [ko] + k("Hc"), k("X"))
-            tt(pl[:, c], FA, T.X[:, c], Op.max, [kx] + k("X"), k("PLo"))
+            block(lambda: [mm(FA, IDN, T.fc[:, c], True, False, [], []), mm(FA, BN24, T.AV[:, c], False, True, [], [])], k("AV", "fc"), [kf])
+            tt(T.X[:, c], DN, T.Hc[:, c], Op.min, [ko] + k("Hc"), k("X"))
+            tt(FA, FA, T.AA[:, c], Op.mult, [kf] + k("AA"), [kf])
+            tt(pl[:, c], FA, T.X[:, c], Op.max, [kf] + k("X"), k("PLo"))
             send(peers, [pl[:, c]] * 4, [pl[:, c]] * 4, "ea%d" % t, k("PLo"))
-            arrive("PL" + s, "ea%d" % t, 8 * KE, LINK[s == "B"])
-            act(T.own[:, c], XS, [ks], k("own"), func=AF.Identity, scale=1.0 / V, bias=(MID + 0.5) / V + 191.5)
+            arrive("PL" + s, "ea%d" % t, 4 * len(STG) * KE, LINK * n)
             act(T.sF[:, c], DN, [ko], k("sF"), func=AF.Sign)
 
+        def places(s):
+            lo, hi = 0 if "A" in s else LA, L if "B" in s else LA
+            n, c = hi - lo, slice(lo, hi)
+            k, k1 = lambda *x: [y + z for y in x for z in s], lambda x: x + s[-1]
+            (RR, kr), (UC, kc) = ((U[BK[0][1]][0][:, 32:32 + n], U[BK[0][1]][1]), (T.PB[:, L + 16:L + 16 + n], "PB")) if s == "A" else (
+                (T.PA[:, L:L + n], "PA"), (U[BK[0][0]][0][:, 0:n], U[BK[0][0]][1]))
+            XB = T.PB[:, 0:n]
+            ts(T.ind[:, c], T.xr[:, c], first, Op.is_ge, k("xr") + ["first"], [k1("ind")], c=0.5)
+            scan(T.cn[:, c], T.ONE[:, 0:n], T.ind[:, c], T.cn[:, lo - 1:lo] if lo else 0.0, Op.mult, Op.add, [k1("ind"), "cnA"], [k1("cn")], c=0.5)
+            mm(UC, DF8, T.ind[:, c], True, False, [k1("ind"), "DF8"], [kc])
+            mm(UC, DF, T.cn[:, c], False, True, [k1("cn"), "DF"], [kc])
+            if CAPS:
+                act(T.Rb[:, c], UC, [kc], [k1("Rb")], func=AF.Relu, bias=-float(TAG + CAP))
+            else:
+                ts(T.Rb[:, c], UC, TAG + CAP + 0.5, Op.is_gt, [kc], [k1("Rb")])
+            if DGG:
+                tt(T.dg[:, c], T.XLf[:].indirect(T.colu[:, lo // 16:hi // 16]), T.xd[:, c], Op.is_equal, k("xd") + AB("XLf")[:1 + (s != "A")] + ["colu"], [k1("dg")], c=GA)
+            else:
+                mm(XB, IDN, T.TRI[:, 0:n], True, False, ["TRI"], ["PB"])
+                block(lambda: [mm(XB[:, x:n:16], IDNH, T.XLh[:, lo // 16:hi // 16], False, x == 15, [], []) for x in range(16)], k("XLh"), ["PB"])
+                tt(T.dg[:, c], T.xr[:, c], XB, Op.is_equal, k("xr") + ["PB"], [k1("dg")])
+            block(lambda: [mm(RR, IDNH, T.NEM[:, c], True, False, [], []), mm(RR, B15, T.cmp[:, c], False, False, [], [])], ["NEM", "cmp0", "cmp1", "B15"], [kr])
+            left = [hi // 16 + 3]
+            mm(RR, IDNH, T.xr[:, c], False, left, k("xr"), ["+" + kr])
+            for m in range(hi // 16 - 1):
+                c0 = max(16 * m + 16, lo)
+                ts(T.E3[:, m, c0:hi], T.xr[:, c0:hi], T.XLf[:, m:m + 1], Op.is_equal, k("xr") + ["XLf" + x for x in STG if STG[x][0] <= 16 * m < STG[x][1]], [k1("E3%d" % m)], c=0.5)
+                mm(RR[:, c0 - lo:n], BBG, T.E3[:, m, c0:hi], False, left, [k1("E3%d" % m)], ["+" + kr])
+            mm(RR, BBG, T.dg[:, c], False, left, [k1("dg")], ["+" + kr])
+            mm(RR, BBG, T.Rb[:, c], False, left, [k1("Rb")], ["+" + kr])
+            mm(RR, BN2K, T.sF[:, c], False, left, k("sF"), ["+" + kr])
+            scan(T.YO[:, c], T.RSY[:, c], RR, -65536.0, Op.max, Op.min, [kr, "RSY"], [k1("YO")])
+            if s != "A" or OLA:
+                o0 = lo if OLA else 0
+                ts(ol[:, o0 // 16:hi // 16], T.YO[:, o0 + 15:hi:16], 8.0 * HO, Op.add, ["YOA", "YOB"] if s != "A" else ["YOA"], ["OLo" if s != "A" else "OLoA"])
+
         pl, ol = T.PL[:, t, me, :], T.OL[:, t, me, :]
-        for ci in range(NCH):
-            products(ci)
+        act(T.nv[:], IO[:, win].indirect(T.bL[:]), ["IO", "IO1", "IO2", "bL0", "bL1"], ["nv"], func=AF.Identity, scale=-1.0, bias=-float(TAG * (t + 2) + name0), c=GA)
+        for ci in range(NCH + 1):
+            if ci < NCH:
+                products(ci)
             if ci:
                 marks(ci - 1)
-            largest(ci)
-        act(T.nv[:], IO[:, win].indirect(T.bL[:]), ["IO", "IO1", "IO2", "bL0", "bL1"], ["nv"], func=AF.Identity, scale=-1.0, bias=-float(TAG * (t + 2) + name0), c=GA)
-        marks(NCH - 1)
-        choose("A")
-        choose("B")
-        RR, XB = T.PA[:, L:2 * L], T.PB[:, L:2 * L]
-        AB = lambda x: [x + "A", x + "B"]
-        ts(T.ind[:], T.own[:], c192, Op.is_equal, AB("own") + ["c192"], ["ind"], c=0.5)
-        scan(T.cn[:], T.ONE[:, 0:L], T.ind[:], 0.0, Op.mult, Op.subtract, ["ind"], ["cn"], c=0.5)
-        scan(T.q1[:], T.ind[:], T.cn[:], 0.0, Op.max, Op.mult, ["ind", "cn"], ["q1"], c=0.5)
-        ts(T.Rb[:], T.q1[:], -(CAP + 0.5), Op.is_lt, ["q1"], ["Rb"], c=0.5)
-        mm(XB, IDN, T.TRI[:], True, False, ["TRI"], ["PB"])
-        block(lambda: [mm(XB[:, c:L:16], IDNH, T.XLh[:], False, c == 15, [], []) for c in range(16)], AB("XLh"), ["PB"])
-        tt(T.dg[:], T.xr[:], XB, Op.is_equal, AB("xr") + ["PB"], ["dg"])
-        block(lambda: [mm(RR, IDNH, T.NEM[:], True, False, [], []), mm(RR, I8K, T.inv[:], False, False, [], []), mm(RR, IDNH, T.xr[:], False, False, [], [])],
-              ["NEM", "inv", "I8K"] + AB("xr"), ["PA"])
-        for m in range(15):
-            ts(T.E3[:, m, 0:L - 16 * m - 16], T.xr[:, 16 * m + 16:L], T.XLf[:, m:m + 1], Op.is_equal, AB("xr") + AB("XLf"), ["E3%d" % m], c=0.5)
-            mm(RR[:, 16 * m + 16:L], BBG, T.E3[:, m, 0:L - 16 * m - 16], False, False, ["E3%d" % m], ["PA"])
-            if m == 7:
-                mm(RR, BBG, T.dg[:], False, False, ["dg"], ["PA"])
-        mm(RR, BBG, T.Rb[:], False, False, ["Rb"], ["PA"])
-        mm(RR, BN2K, T.sF[:], False, True, AB("sF"), ["PA"])
-        scan(T.YO[:], T.RSY[:], RR, -65536.0, Op.max, Op.min, ["PA", "RSY"], ["YO"])
-        ts(ol, T.YO[:, 15:L:16], 8.0 * HO, Op.add, ["YO"], ["OLo"])
-        send(peers, [ol] * 4, [ol] * 4, "eb%d" % t, ["OLo"])
-        arrive("OL", "eb%d" % t, 4 * KE, 0.3)
-        ts(T.li[:, 0, :], T.bL[:], float(w0), Op.add, ["bL0", "bL1"], ["li0"])
-        ts(T.li[:, 1, :], T.li[:, 0, :], B - 1, Op.bitwise_and, ["li0"], ["li1"])
-        tt(la, T.li[:, 1, :], invL, Op.add, ["li1", "invL"], ["la"])
-        tt(lb, la, JD, Op.min, ["la", "JD"], ["lb"])
-        cp(T.pos[:], lb, ["lb"], ["pos"])
+            if ci < NCH:
+                largest(ci)
+            for s in STG:
+                if ci == STG[s][1] // CH:
+                    choose(s)
+        places("".join(STG))
+        send(peers, [ol] * 4, [ol] * 4, "eb%d" % t, ["OLo", "OLoA"])
+        arrive("OL", "eb%d" % t, 4 * KE, 0.1)
         if t == 0:
-            wr["NV1"] = wr["NV1"] + wr["E314"]
+            wr["NV1"] = wr["NV1"] + wr["E314B"]
             check(0, T.NV1, "NV1")
             for c in range(2):
-                mm(T.PU0[:, 512 * c:512 * c + 512], BN8, T.EQ[:, 512 * c:512 * c + 512], True, True, ["EQ%d" % (1 - c), "BX"], ["U%d" % c])
+                mm(T.PU0[:, 512 * c:512 * c + 512], BN8, T.EQ[:, 512 * c:512 * c + 512], True, True, ["EQ%d" % c, "BX"], ["U%d" % c])
             tt(T.NV[:, 0:B], T.PU0[:], T.NV[:, 0:B], Op.add, ["U0", "U1"], ["NV"])
-        for x in range(XRQ):
-            scatter(T.XR[:], T.pos[:, 16 * x // XRQ:16 * (x + 1) // XRQ], T.xr[:, L * x // XRQ:L * (x + 1) // XRQ], ["pos", "xrA", "xrB", "OLo"], ["XR"])
-        holdings()
+        for tab, src, k, R, cut in ((T.XR, T.xr, "XR", AB("xr"), (0, 16)), (T.NV, T.nv, "NV", ["nv"], NVC)):
+            for m0, m1 in zip(cut, cut[1:]):
+                scatter(tab[:, x0:x0 + LW], T.bL[:, m0:m1], src[:, 16 * m0:16 * m1], ["bL0", "bL1", "OLo"] + R, [k, "~X"])
+            if t < RO - 1:
+                act(tab[:, x0 + B:x0 + B + L], tab[:, x0:x0 + L], [k], [k])
+        holdings(min(x0 + L, B))
         for q in range(N - 1, -1, -1):
-            if NVQ == 1 and q == N - 1:
-                scatter(T.NV[:], T.pos[:], T.nv[:], ["pos", "nv", "OLo"], ["NV", "~C"])
-            scatter(C[:], T.OL[:, t, q, :], T.PL[:, t, q, :], ["PLA", "PLB", "PLoA", "PLoB", "OL", "OLo"] + Ar + Hr, ["C", "~C"])
-            if NVQ == 4 and q:
-                scatter(T.NV[:], T.pos[:, 4 * q - 4:4 * q], T.nv[:, 64 * q - 64:64 * q], ["pos", "nv"], ["NV", "~C"])
-        ts(T.HL[:], U[1][0][:, 0:64], float(MID), Op.add, ["U1"], ["HL", "~C"])
+            scatter(C[:], T.OL[:, t, q, :], T.PL[:, t, q, :], AB("PL") + AB("PLo") + ["OL", "OLo"] + Ar + Hr, ["C", "~C"])
+        ts(T.HL[:], U[1][0][:, 0:64], float(MID), Op.add, ["U1"], ["HL"])
 
-    check(0)
+    stage[0] = "end"
+    check(B)
     tg, sa = T.junk[:, 0:V], T.TU[:, 0:V]
-    act(tg, C[:, ho:ho + V], ["C"], ["junk", "acc0", "acc1"] + ["junk%d" % x for x in range(NA, 16, 2)], func=AF.Identity, scale=-1.0 / TAG, bias=192.0 - 0.3125)
+    act(tg, C[:, ho:ho + V], ["C"], ["junk", "junkS0", "junkS1"] + ["junk%d" % x for x in range(0, 16, 2)], func=AF.Identity, scale=-1.0 / TAG, bias=192.0 - 0.3125)
     act(sa, C[:, ao:ao + V], ["C"], ["TU"], func=AF.Sign)
-    act(T.MX[:, 0:V], C[:, ao:ao + V], ["C"], Mk, func=AF.Abs)
-    dma("s", T.yal[:], T.MX[:, 0:V], "dout", Mk, [], final=80)
+    act(T.MX[:, 0:V], C[:, ao:ao + V], ["C"], MA, func=AF.Abs)
+    dma("s", T.yal[:], T.MX[:, 0:V], "dout", MA, [], final=80)
     for c, (c0, c9, ps, k, u) in enumerate(((0, h, T.PA, "PA", "U2"), (h, V, T.PB, "PB", "U3"))):
         cs = slice(512 * c, 512 * c + 512)
         t8 = T.PU1[:, 512 * c:512 * c + h]
-        mm(T.PU0[:, cs], BLK, T.EQ[:, cs], True, True, ["EQ%d" % (1 - c)], ["U%d" % c])
+        mm(T.PU0[:, cs], BLK, T.EQ[:, cs], True, True, ["EQ%d" % c], ["U%d" % c])
         mm(t8, BNC, T.ONE[:, 0:h], True, False, ["ONE", "BX"], [u])
         mm(t8, I8K, tg[:, c0:c9], False, True, ["junk", "I8K"], [u])
         mm(ps[:, 0:h], IDN, tg[:, c0:c9], True, False, ["junk"], [k])
@@ -588,7 +690,7 @@ def rank_program(g, core, T, topo):
     for i in _order(nodes):
         n = nodes[i]
         e = n["e"]
-        if e == "link":
+        if e[:4] == "link":
             continue
         need = {}
         for j in n["wait"]:

import math
import numpy as np
from concourse.bass import DstId, RemoteDMATransfer
from concourse.mybir import AluOpType, ActivationFunctionType

Op, AF = AluOpType, ActivationFunctionType
N, V, B, L, CAP, RO = 5, 816, 1024, 256, 64, 5
W = N * V
HO = 4096
DO = 2 * HO
TAG = 8192
MID = W // 2
LW = B + L + 32
TW = 768 + LW
PW = (144, 264)
CH, NCH = 64, 4
PARTS = (2, 2, 1, 1)
KEEP, REP = (0, 0, 0, 1), (4, 4, 4, 2)
FAR = (0, 0, 0, 0)
UB, BK = ((0, 1, 4), (2, 3, 5), (0, 1, 4), (0, 1, 4)), ((2, 3), (0, 1))
M0, NS = 4, (4, 4)
LEAST, ACT, PCALL, F32 = 64, 0.085, 0.0, 5
CYC, PEC, FIX = 0.00083, 0.52, 0.05
CASES = ((1.1, 1.4, 2.8, 0.25, 0.005, 1.0), (1.3, 1.8, 4.5, 0.22, 0.01, 1.3), (1.0, 1.25, 2.0, 0.28, 0.0, 0.8))
TURNS, TRIES, MOVES, STEP, SEED = 4, 2000, 6, 1.0, 1
KEPT = {}
VB, AL, PMS, PST, OLA, EMV, DGG = 0, 0, ("PC", "PD", "PB", "PD"), 0, 0, "B", 0
NVC = (0, 8, 12, 16)
CHM, TKX, PSC, SEG = "B", "A", 0, (0, 22, 43, 64)
OHS, HCS, CAPS, XLS = 1, "", 1, 0
STG = {"A": (0, 128, "PC", "U3", "U2"), "B": (128, 256, "U1", "PD", "U0")}
LA, LINK = 128, 0.0135

f32, bf, f16, i32, u16 = "float32", "bfloat16", "float16", "int32", "uint16"


def _sb(shape, d):
    return ("sbuf", [128] + list(shape), d)


SCRATCH = {
    "C": _sb([DO + L], f32), "PL": _sb([RO, N, L], f32), "OL": _sb([RO, N, 16], u16),
    "XR": _sb([B + LW], f32), "NV": _sb([B + LW], f32), "NV1": _sb([B], f32), "HL": _sb([64], u16), "EQ": _sb([B], bf),
    "XI": _sb([B], i32), "hnI": _sb([V], i32), "IOTA": _sb([TW], f32), "TX": _sb([TW], i32), "TU": _sb([TW], bf), "monb": _sb([B], bf),
    "G": _sb([4096], f32), "E": _sb([4096], f32), "MX": _sb([2048], f32), "TOP": _sb([4096], bf), "E3": _sb([16, L], bf),
    "SCL": _sb([L], bf), "ONE": _sb([512], bf), "C16": _sb([L], bf),
    "TMP": _sb([144], bf), "SEL": _sb([3, 144], bf), "SELH": _sb([144], f16), "SELF": _sb([144], f32), "IDNF": _sb([128], f32), "NIDF": _sb([128], f32),
    "BRD": _sb([16, 128], bf), "MAT": _sb([22, 128], bf), "MATH": _sb([2, 128], f16),
    "cI": _sb([8], i32), "cF": _sb([12], f32), "cB": _sb([8], bf), "EK": _sb([16], f32), "SG": _sb([2, 8], f32),
    "JT": _sb([4, 16], f32), "JH": _sb([32], f16), "JK": _sb([16], f16),
    "RS64": _sb([B], bf), "cs": _sb([B], bf), "inc": _sb([66], bf), "ends": _sb([64], f32), "six": _sb([64], bf), "I8F": _sb([128], f32), "spare": _sb([16], bf), "P": _sb([72], f32),
    "junk": _sb([B], bf), "acc": _sb([16], f32), "cL": _sb([16], u16), "cmp": _sb([L], bf), "bL": _sb([16], u16),
    "FO": _sb([L], u16), "ug": _sb([L], bf), "xc": _sb([L], f16), "nv": _sb([L], f32), "w": _sb([L], bf), "sg": _sb([L], bf),
    "Z": _sb([2 * L], f16), "xd": _sb([L], f16), "colu": _sb([16], u16), "XL": _sb([16], u16), "tk": _sb([16], u16), "XLf": _sb([16], f32), "xr": _sb([L], f16), "XLh": _sb([16], f16),
    "TRI": _sb([L], bf), "NEM": _sb([L], f16), "RSY": _sb([L], f32), "YO": _sb([L], f32),
    "SA": _sb([L], bf), "Hc": _sb([L], f32), "EM": _sb([L], bf), "AA": _sb([L], f32), "fc": _sb([L], bf), "own": _sb([L], bf),
    "ind": _sb([L], bf), "cn": _sb([L], bf), "q1": _sb([L], bf), "dg": _sb([L], bf), "X": _sb([L], f32),
    "AV": _sb([L], bf), "sF": _sb([L], bf), "Rb": _sb([L], bf),
    "PU0": ("psum", [128, 1024], f32), "PU1": ("psum", [128, 1024], f32),
    "PA": ("psum", [128, 512], f32), "PB": ("psum", [128, 512], f32), "PC": ("psum", [128, 512], f32),
    "PD": ("psum", [128, 512], f32),
}
SEMAPHORES = (["sv", "sa", "sp", "sg", "sent", "feed0", "feed1", "ag0", "ag1", "dal", "dft", "dut", "dhb", "dhn", "dmon", "dout"]
              + ["%s%d" % (k, t) for k in ("ea", "eb") for t in range(RO)])
PSUM = ("U0", "U1", "U2", "U3", "PA", "PB", "PC", "PD")


def _senders(core, topo, part):
    out, seen = [core], {topo.addr(core)[2]}
    for c in topo.cores_of(core):
        if topo.addr(c)[2] not in seen and (part == 0 or topo.die(c) != topo.die(core)):
            seen.add(topo.addr(c)[2])
            out.append(c)
    return out


def _piece(T, part, q, i, n):
    c0, w = part * HO + q * V, PW[part]
    return T.C[:, c0 + (n - 1) * w:c0 + V] if i == 0 else T.C[:, c0 + (i - 1) * w:c0 + i * w]


def _mask(engs):
    m = 0
    for e in engs:
        m |= 1 << e
    return m


def _engines(T, topo, core, dst):
    eng = topo.engines(core, dst)
    if topo.chip(core) == topo.chip(dst):
        far = topo.engines(core, [c for c in T.cores if topo.chip(c) != topo.chip(core)][0])
        eng = far + [e for e in eng if e not in far]
    return eng, len(eng) // 4


def _spread(g, T, topo, core, dsts, srcs, outs, sem):
    eng, k = _engines(T, topo, core, dsts[0])
    tr = []
    for i, d in enumerate(dsts):
        rid, pid, _ = topo.addr(d)
        tr.append(RemoteDMATransfer(dst_ids=[DstId(rid=rid, pnc=pid)], dma_engine_mask=_mask(eng[len(eng) - k * (i + 1):len(eng) - k * i]),
                                    remote_sem=sem, src=srcs[i], dst=outs[i]))
    g.remote_dma_fused(tr, local_sem=T.sem["sent"])


def helper_program(g, core, T, topo, q):
    peers = [T.cores[(q + 1 + i) % N] for i in range(N - 1)]
    parts = [part for part in range(2) if core in _senders(T.cores[q], topo, part)]
    for part in parts:
        s = _senders(T.cores[q], topo, part)
        g.wait_ge(T.sem["feed%d" % part], _engines(T, topo, T.cores[q], core)[1])
        ap = _piece(T, part, q, s.index(core), len(s))
        _spread(g, T, topo, core, peers, [ap] * 4, [ap] * 4, T.sem["ag%d" % part])
    g.wait_ge(T.sem["sent"], len(parts) * 4 * (len(topo.engines(core, peers[0])) // 4))


def _pass(eng, cost, pre, key, along):
    key = list(key)
    for j in along:
        for i, d in pre[j]:
            if key[i] >= key[j]:
                key[j] = key[i] + 1e-6
    start, busy, rank = [0.0] * len(eng), {e: [] for e in set(eng)}, [0] * len(eng)
    for r, j in enumerate(sorted(along, key=lambda x: key[x])):
        t, c, b = 0.0, cost[j], busy[eng[j]]
        for i, d in pre[j]:
            if start[i] + cost[i] + d > t:
                t = start[i] + cost[i] + d
        k = len(b)
        while k and b[k - 1][1] > t:
            k -= 1
        while k < len(b) and b[k][0] < t + c:
            t = max(t, b[k][1])
            k += 1
        b.insert(k, (t, t + c))
        start[j], rank[j] = t, r
    return sorted(along, key=lambda x: (start[x], rank[x])), start


def _order(nodes):
    eng, kind = [x["e"] for x in nodes], [x["kind"] for x in nodes]
    if KEPT.get("kind") == kind:
        return KEPT["out"]
    cases = []
    for f, ga, sc, hop, call, link in CASES:
        cost = [float(np.dot(x["cost"], (1.0, call, CYC * f, CYC * f * ga, CYC * f * sc, link))) for x in nodes]
        pre = [[(i, nodes[i]["lat"] + (0.0 if eng[i] == eng[j] == "p" else hop) if i in x["wait"] else 0.0) for i in x["pre"]] for j, x in enumerate(nodes)]
        cases.append((cost, pre))

    def length(out):
        s = 0.0
        for cost, pre in cases:
            end, free = [0.0] * len(out), dict.fromkeys(eng, 0.0)
            for j in out:
                t = free[eng[j]]
                for i, d in pre[j]:
                    if end[i] + d > t:
                        t = end[i] + d
                end[j] = free[eng[j]] = t + cost[j]
            s += max(end[i] + x["lat"] for i, x in enumerate(nodes))
        return s

    cost, pre = cases[0]
    post = [[] for _ in nodes]
    for j in range(len(nodes)):
        for i, d in pre[j]:
            post[i].append((j, d))
    n = len(nodes)
    fore, back = list(range(n)), list(range(n - 1, -1, -1))
    key, best, x = fore, None, SEED
    for turn in range(TURNS + TRIES):
        out, start = _pass(eng, cost, pre, key, fore)
        t = length(out)
        if best is None or t <= best[0]:
            best = (t, out, start)
        shift = {}
        if turn >= TURNS:
            start = best[2]
            for _ in range(MOVES):
                x = x * 48271 % 2147483647
                k = kind[x % n]
                x = x * 48271 % 2147483647
                shift[k] = (x % 2001 - 1000) * 0.001 * STEP
        late = _pass(eng, cost, post, [-start[i] - cost[i] - shift.get(kind[i], 0.0) for i in fore], back)[1]
        key = [-late[i] - cost[i] + shift.get(kind[i], 0.0) for i in fore]
    KEPT.update(kind=kind, out=best[1], time=best[0])
    return best[1]


def rank_program(g, core, T, topo):
    me = T.rank_of(core)
    if me is None:
        for q in range(N):
            if core in _senders(T.cores[q], topo, 0):
                helper_program(g, core, T, topo, q)
        return
    peers = [T.cores[(me + 1 + i) % N] for i in range(N - 1)]
    KE = len(topo.engines(core, peers[0])) // 4
    Q = {"v": g.vector, "a": g.scalar, "p": g.tensor, "g": g, "s": g.sync}
    v, a, p = g.vector, g.scalar, g.tensor
    nodes, wr, rd, total, group, count, stage = [], {}, {}, {}, [], {}, ["start"]

    def node(e, fn, cost, R, Wr, lat=0.0, sem=None):
        if group:
            n = group[0]
            n["e"], n["cost"] = e, n["cost"] + cost
            n["calls"].append(fn)
            return
        pre = set()
        after = [i for k in Wr if k[0] == "~" for i in wr.get(k, [])]
        for k in R:
            pre.update(wr.get(k, []))
            if k in PSUM:
                pre.update(i for i in rd.get(k, []) if nodes[i]["e"] != e)
        for k in Wr:
            if k[0] == "+":
                pre.update(wr[k[1:]][:1])
            elif k[0] != "~":
                pre.update(wr.get(k, []) + rd.get(k, []))
        for k in R:
            rd.setdefault(k, []).append(len(nodes))
        for k in Wr:
            if k[0] == "+":
                wr[k[1:]].append(len(nodes))
            else:
                wr[k], rd[k] = [len(nodes)], []
        name = " ".join([stage[0], e] + R + [">"] + Wr)
        count[name] = count.get(name, 0) + 1
        nodes.append({"e": e, "calls": fn if isinstance(fn, list) else [fn], "cost": cost, "lat": lat, "pre": sorted(pre.union(after)),
                      "wait": pre, "sem": sem, "kind": "%s %d" % (name, count[name])})

    def block(body, R, Wr):
        group.append({"cost": price(), "calls": []})
        body()
        n = group.pop()
        node(n["e"], n["calls"], n["cost"], R, Wr)

    def size(ap):
        return math.prod(ap.shape[1:])

    def price(us=0.0, calls=0, cycles=0.0, gathered=0, scattered=0, link=0.0):
        return np.array([us, calls, cycles, gathered, scattered, link], float)

    def vcost(ap, c):
        return price(FIX, gathered=size(ap)) if c == GA else price(calls=1, cycles=max(LEAST, c * size(ap)))

    def dma(e, out, in_, sem, R, Wr, final=16):
        total[sem] = final
        node(e, lambda: Q[e].dma_start(out, in_).then_inc(T.sem[sem], 16), price(0.1), R, Wr, lat=2.2, sem=(sem, final))

    def send(dsts, srcs, outs, sem, R, cost=0.75):
        total["sent"] = total.get("sent", 0) + _engines(T, topo, core, dsts[0])[1] * len(dsts)
        node("g", lambda: _spread(g, T, topo, core, dsts, srcs, outs, T.sem[sem]), price(cost), R, ["sent", "~sent"], sem=())

    def arrive(key, sem, val, cost, way="link", lat=0.6):
        total[sem] = val
        node(way, [], price(0.3, link=cost), ["sent"], [key, "~" + way], lat=lat, sem=(sem, val))
        rd["sent"] = []

    def ts(out, in0, s1, o0, R, Wr, s2=None, o1=None, c=1.0):
        if o1 is None:
            node("v", lambda: v.tensor_scalar(out, in0, s1, None, o0), vcost(out, c), R, Wr)
        else:
            node("v", lambda: v.tensor_scalar(out, in0, s1, s2, o0, o1), vcost(out, c), R, Wr)

    def tt(out, in0, in1, o, R, Wr, c=1.0):
        node("v", lambda: v.tensor_tensor(out, in0, in1, o), vcost(out, c), R, Wr)

    def cp(out, in_, R, Wr, c=1.0):
        node("v", lambda: v.tensor_copy(out, in_), vcost(out, c), R, Wr)

    def scatter(win, off, in_, R, Wr):
        node("v", lambda: v.tensor_copy(win.indirect(off), in_), price(FIX, scattered=size(in_)), R, Wr)

    def ms(out, c, Wr):
        node("v", lambda: v.memset(out, c), vcost(out, 0.5), [], Wr)

    def scan(out, d0, d1, init, o0, o1, R, Wr, c=1.0):
        node("v", lambda: v.tensor_tensor_scan(out, d0, d1, init, o0, o1), vcost(out, c), R, Wr)

    def act(out, in_, R, Wr, func=AF.Copy, c=1.0, **kw):
        node("a", lambda: a.activation(out, in_, func, **kw), price(0.065, gathered=size(out)) if c == GA else price(ACT, cycles=c * max(LEAST, size(out))), R, Wr)

    def mm(out, lhsT, rhs, st, sp, R, Wr, c=1.0):
        def last():
            sp[0] -= 1
            return sp[0] == 0
        node("p", lambda: p.matmul(out, lhsT, rhs, st, last() if isinstance(sp, list) else sp), price(calls=PCALL, cycles=PEC * (F32 if c == 4 else c) * max(64, size(out))), R, Wr)

    def sel16(out, rhs_of, R, Wr, st=True, sp=True, mat=T.SEL[:, 0, :], c=1.0):
        block(lambda: [mm(out, mat[:, 16 - r:144 - r], rhs_of(r), st and r == 0, sp and r == 15, [], [], c=c) for r in range(16)], R + ["SEL"], Wr)

    def iota(out, pat, base, cm, Wr, small=True):
        if small:
            node("g", lambda: g.iota(out, pat, base, cm, allow_small_or_imprecise_dtypes=True), price(0.13, cycles=2 * size(out)), [], Wr)
        else:
            node("g", lambda: g.iota(out, pat, base, cm), price(0.13, cycles=2 * size(out)), [], Wr)

    GA = 1.56
    C, IO, TMP = T.C, T.IOTA, T.TMP
    Aw, Hw = C[:, 0:HO], C[:, HO:DO]
    REL, BLK, IDN, D2M, NUP, DNM, THM, B4K, B9, BN24, BN8, B05, I8K, BNC, TM2, BBG, BN2K, UPM, I16, B15, DF, DF8 = [T.MAT[:, i, :] for i in range(22)]
    SEL, SELK = [T.SEL[:, i, :] for i in range(2)]
    BLKH, IDNH = T.MATH[:, 0, :], T.MATH[:, 1, :]
    rcol, g16, ebias, first, r0, rh = [T.cF[:, i:i + 1] for i in range(6)]
    J16, JB, DUM, J1 = [T.JT[:, i, :] for i in range(4)]
    ao, ho = me * V, HO + me * V
    name0 = me * B + 1
    Ar, Hr = ["A", "A2", "Aown", "Aown2", "Az", "C"], ["H", "H2", "Hown", "Hz", "C"]
    Gk, Ek, Mk, Tk = [["%s%d" % (s, c) for c in range(n)] for s, n in (("G", 2 * NCH), ("E", 4 * NCH), ("MX", NCH), ("TOP", 4 * NCH))]
    U = [((T.PU0, T.PU1)[i // 2][:, 512 * (i % 2):512 * (i % 2) + 512], "U%d" % i) for i in range(4)]
    U += [(T.PB[:], "PB"), (T.PC[:], "PC")]
    PM = [(T[k][:], k) for k in PMS]

    AB = lambda x: [x + s for s in STG]

    def holdings(x0, piece=16):
        for r1 in range(0, 16, piece):
            block(lambda: [mm(U[1][0][:, 0:64], T.SELF[:, 16 - r:144 - r], T.XR[:, x0 + r:x0 + B:16], r == 0, r == 15, [], [], c=4.0) for r in range(r1, r1 + piece)], ["XR", "SELF"], ["U1"])

    def check(x0, nv=T.NV, k="NV", parts=2):
        n = B // parts
        for c in range(parts):
            tt(T.EQ[:, n * c:n * c + n], Hw.indirect(T.HL[:, n * c // 16:n * (c + 1) // 16]), nv[:, x0 + n * c:x0 + n * c + n], Op.is_equal, Hr + ["HL", k],
               ["EQ%d" % c] if parts == 2 else ["EQ0", "EQ1"], c=GA)

    h = V // 2
    dma("s", C[:, ao:ao + h], T.al[:, 0:h], "dal", [], ["Aown"], final=32)
    dma("a", C[:, ao + h:ao + V], T.al[:, h:V], "dal", [], ["Aown2"], final=32)
    ms(T.XI[:], 0, ["XI"])
    dma("s", T.XI[0:128:16, :], T.hb[:], "dhb", [], ["XI", "~s"])
    dma("s", T.hnI[:], T.hn[:], "dhn", [], ["hnI", "~s"])
    dma("s", T.TX[:, 0:B], T.ft[:], "dft", [], ["TX", "~s"], final=32)
    dma("s", T.TX[:, B:LW], T.ft[:, 0:LW - B], "dft", [], ["TX2", "~s"], final=32)
    dma("s", T.TU[:, 0:B], T.ut[:], "dut", [], ["TU", "~s"], final=32)
    dma("s", T.TU[:, B:LW], T.ut[:, 0:LW - B], "dut", [], ["TU2", "~s"], final=32)
    for x, y, k in ((T.TX, T.ft, "TX"), (T.TU, T.ut, "TU")):
        dma("s", x[:, LW:2 * B], y[:, LW - B:B], "dmon", ["TX", "TU"], [k + "3"], final=80)
        dma("s", x[:, 2 * B:TW], y[:, 0:TW - 2 * B], "dmon", ["TX", "TU"], [k + "4"], final=80)
    dma("s", T.monb[:], T.mon[:], "dmon", ["TX", "TU"], ["monb"], final=80)

    iota(T.cI[:, 0:1], [[0, 1]], 0, 1, ["cI"], small=False)
    iota(TMP[:], [[1, 144]], 0, 0, ["TMP"])
    iota(T.C16[:], [[0, 16], [1, 16]], 0, 0, ["C16"])
    iota(IO[:, 0:L], [[1, L]], 0, 0, ["IO"])
    snd, snd1 = _senders(core, topo, 0), _senders(core, topo, 1)
    pcs = [[_piece(T, part, me, i, len(x)) for i in range(len(x))] for part, x in enumerate((snd, snd1))]
    send(snd[1:], pcs[0][1:], pcs[0][1:], "feed0", ["Aown", "Aown2", "IO", "C16"], 2.0)
    arrive("A2", "ag0", 4 * len(snd) * KE, LINK * 1.5 * PW[0], "link2", 4.0)
    send(peers, [pcs[0][0]] * 4, [pcs[0][0]] * 4, "ag0", [])
    arrive("A", "ag0", 4 * len(snd) * KE, LINK * (V - 2.7 * PW[0]))
    for c0, c9, b0, k in ((L, B, L, "IO1"), (B, TW, 0, "IO2")):
        iota(IO[:, c0:c9], [[1, c9 - c0]], b0, 0, [k, "~sent"])

    ts(T.cI[:, 1:2], T.cI[:, 0:1], 15, Op.bitwise_and, ["cI"], ["cI1"])
    ts(T.cI[:, 2:3], T.cI[:, 0:1], 112, Op.bitwise_and, ["cI"], ["cI2"])
    cp(T.cF[:, 0:2], T.cI[:, 1:3], ["cI1", "cI2"], ["cF"])
    ms(T.ONE[:], 1.0, ["ONE"])
    ts(REL, TMP[:, 0:128], g16, Op.subtract, ["TMP", "cF"], ["REL"])
    ts(r0, rcol, 0.0, Op.is_equal, ["cF"], ["r0"])
    ts(SEL, TMP[:], -16.0, Op.add, ["TMP", "cF"], ["SEL"], g16, Op.is_equal)
    ts(IDN, REL, rcol, Op.is_equal, ["REL"], ["IDN"])
    ts(TM2, REL, 0.0, Op.is_ge, ["REL"], ["TM2"])
    ts(BLK, REL, 16.0, Op.is_lt, ["REL"], ["BLK"])
    ts(NUP, REL, rcol, Op.is_lt, ["REL"], ["NUP"])
    ts(T.EK[:], TMP[:, 0:16], rcol, Op.is_equal, ["TMP", "cF"], ["EK"])
    tt(BLK, BLK, TM2, Op.mult, ["TM2", "BLK"], ["BLK"], c=2)
    ts(J16, TMP[:, 0:16], 16.0, Op.mult, ["TMP", "cF"], ["J16"], rcol, Op.add)
    ts(T.EQ[:], T.XI[:], W - 0.5, Op.is_lt, ["XI", "r0"], ["EQ0", "EQ1"], r0, Op.mult)
    tt(NUP, NUP, BLK, Op.mult, ["NUP", "BLK"], ["NUP"], c=2)
    tt(UPM, BLK, NUP, Op.subtract, ["NUP", "BLK"], ["UPM"], c=2)
    ts(JB, J16, 0.5, Op.add, ["J16"], ["JB"])
    ts(J1, J16, 1.0, Op.add, ["J16"], ["J1"])
    ms(T.inc[:, 0:2], 0.0, ["inc0"])
    ms(T.six[:], 16.0, ["six"])
    ts(I16, IDN, 16.0, Op.mult, ["IDN"], ["I16"])
    ts(T.I8F[:], IDN, 8.0, Op.mult, ["IDN"], ["I8F"])
    block(lambda: [act(T.SCL[:, x:y], TMP[:, 0:y - x], [], [], func=AF.Exp, scale=8.0 * math.log(2.0), bias=-84.0 * math.log(2.0), c=25.0) for x, y in zip(SEG, SEG[1:])],
          ["TMP"], ["SCL"])
    for x in (CH, 2 * CH):
        act(T.SCL[:, x:2 * x], T.SCL[:, 0:x], ["SCL"], ["SCL"])
    hf, ab, c1, c2 = T.G[:, 0:V], T.MX[:, 0:V], T.TOP[:, 0:V], T.TOP[:, B:B + V]
    cp(hf, T.hnI[:], ["hnI"], Gk)
    ts(c1, T.hnI[:], 0.5, Op.is_gt, ["hnI"], Tk[0:4], -float(TAG), Op.mult)
    ts(c2, T.hnI[:], N * B + 0.5, Op.is_gt, ["hnI"], Tk[4:8], -6.0 * TAG, Op.mult)
    MA = Mk + [x + "a" for x in Mk]
    act(ab, hf, Gk, MA, func=AF.Abs)
    for c0, c9, k in ((0, 512, "U2"), (512, V, "U3")):
        mm(T.PU1[:, c0:c9], IDN, T.TOP[:, c0:c9], True, False, Tk[0:4] + ["IDN"], [k])
        mm(T.PU1[:, c0:c9], IDN, T.TOP[:, B + c0:B + c9], False, True, Tk[4:8], [k])
    tt(C[:, ho:ho + V], T.PU1[:, 0:V], ab, Op.subtract, ["U2", "U3"] + MA, ["Hown"])
    send(snd1[1:], pcs[1][1:], pcs[1][1:], "feed1", ["Hown"])
    arrive("H2", "ag1", 4 * len(snd1) * KE, LINK * 3 * PW[1], "link2", 3.0)
    send(peers, [pcs[1][0]] * 4, [pcs[1][0]] * 4, "ag1", ["A"])
    arrive("H", "ag1", 4 * len(snd1) * KE, LINK * 2 * (V - 2 * PW[1]))
    block(lambda: [act(T.BRD[:, k, :], BLK, [], [], scale=T.EK[:, k:k + 1]) for k in range(16)], ["BLK", "EK"], ["BRD"])
    ms(T.RS64[:], 1.0, ["RS64"])
    ms(C[:, W:HO], 0.0, ["Az"])
    ms(C[:, HO + W:DO], 1.0, ["Hz"])
    ms(T.RS64[:, 0:B:64], 0.0, ["RS64"])
    act(T.IDNF[:], IDN, ["IDN"], ["IDNF"])
    act(T.NIDF[:], IDN, ["IDN"], ["NIDF"], scale=-1.0)

    def constants():
        ts(T.XR[:, 0:B], T.XI[:], -float(MID), Op.add, ["XI"], ["XR"])
        ts(T.SELF[:], SEL, r0, Op.mult, ["SEL", "r0"], ["SELF"])
        ts(ebias, rcol, -120.0, Op.add, ["cF"], ["eb"], -math.log(2.0), Op.mult)
        ts(D2M, IDN, 2.0, Op.mult, ["IDN"], ["D2M"])
        ts(first, rcol, float(V), Op.mult, ["cF"], ["first"], -MID - 0.5, Op.add)
        ts(DF8, REL, 1.0, Op.add, ["REL"], ["DF8"], rcol, Op.is_equal)
        tt(DF, IDN, DF8, Op.subtract, ["IDN", "DF8"], ["DF"], c=2)
        act(DF8, DF, ["DF"], ["DF8"], scale=float(TAG))
        tt(D2M, D2M, BLK, Op.subtract, ["D2M", "BLK"], ["D2M"], c=2)
        ts(DUM, J16, float(DO), Op.add, ["J16"], ["DUM"])
        ts(T.JH[:, 0:16], J16, 0.0, Op.mult, ["J16"], ["JH0"])
        ts(T.JH[:, 16:32], J16, 16.0, Op.mult, ["J16"], ["JH"])
        ts(T.JK[:], J16, 16.0, Op.mult, ["J16"], ["JK"], 60.0, Op.add)
        ts(rh, rcol, 0.5, Op.mult, ["cF"], ["rh"])
        ts(SELK, SEL, rh, Op.mult, ["SEL", "rh"], ["SELK"])
        cp(T.SELH[:], SEL, ["SEL"], ["SELH"])
        cp(BLKH, BLK, ["BLK"], ["BLKH"])
        cp(T.colu[:], TMP[:, 0:16], ["TMP"], ["colu"])
        cp(IDNH, IDN, ["IDN"], ["IDNH"])
        ts(T.TRI[:], T.C16[:], rcol, Op.is_le, ["C16", "cF"], ["TRI"], float(TAG), Op.mult, c=0.5)
        ts(T.dg[:], T.C16[:], rcol, Op.not_equal, ["C16", "cF"], ["dg"], 8.0 * HO, Op.mult, c=0.5)
        ms(T.RSY[:], -65536.0, ["RSY"])
        ts(T.NEM[:], T.dg[:], float(MID), Op.add, ["dg"], ["NEM"], c=0.5)
        ts(T.RSY[:, 0:L:16], DUM, -8.0 * HO, Op.add, ["DUM"], ["RSY"])
        ts(T.SG[:, 0, :], TMP[:, 0:8], rcol, Op.is_lt, ["TMP", "cF"], ["SG0"], 0.125, Op.mult)
        ts(T.SG[:, 1, :], T.SG[:, 0, :], -0.0625, Op.add, ["SG0"], ["SG1"])
        ts(T.SG[:, 0, :], T.SG[:, 1, :], 15.0, Op.mult, ["SG1"], ["SG0"])
        tt(DNM, NUP, D2M, Op.add, ["NUP", "D2M"], ["DNM"], c=2)
        tt(THM, BLK, I16, Op.subtract, ["BLK", "I16"], ["THM"], c=2)
        act(DNM, DNM, ["DNM"], ["DNM"], scale=-(2.0 ** 18))
        act(THM, THM, ["THM"], ["THM"], scale=float(TAG))
        block(lambda: [act(m, BLK, [], [], scale=c) for m, c in (
            (B4K, TAG / 2), (B9, -9.0 * TAG / 16), (BN24, -(2.0 ** 24)), (BN8, -float(TAG)), (B05, 0.5), (BNC, -12.0 * TAG), (BBG, 4.0 * HO),
            (BN2K, -HO / 2))], ["BLK"], ["BX"])
        act(B15, T.BRD[:, 15, :], ["BRD"], ["B15"], scale=2.0 * TAG)
        act(I8K, IDN, ["IDN"], ["I8K"], scale=float(TAG))
        act(T.NV[:, 0:B], IO[:, 0:B], ["IO", "IO1"], ["NV"], func=AF.Identity, scale=-1.0, bias=-float(name0))
        act(T.NV1[:], IO[:, 0:B], ["IO", "IO1"], ["NV1"], func=AF.Identity, scale=-1.0, bias=-float(TAG + name0))
        holdings(0, 2)
        ts(T.HL[:], U[1][0][:, 0:64], float(MID), Op.add, ["U1"], ["HL"])

    for t in range(RO):
        w0, x0 = (L * t) % B, L * t
        win = slice(w0, w0 + LW)
        count.clear()
        stage[0] = "round" if t else "first"
        if t > 0:
            check(x0, parts=1)
        hz = T.PC[:, 0:64]
        block(lambda: [mm(T.PA[:, 0:64], BLK, T.EQ[:, r:B:16], r == 0, r == 15, [], []) for r in range(16)], ["EQ0", "EQ1", "BLK"], ["PA"])
        scan(T.ends[:], T.six[:], T.PA[:, 0:64], 0.0, Op.add, Op.subtract, ["PA", "six"], ["ends"])
        sel16(hz, lambda r: T.EQ[:, r:B:16], ["EQ0", "EQ1"], ["PC"])
        inc, inc0 = T.inc[:, 2:66], T.inc[:, 1:65]
        scan(inc, T.ONE[:, 0:64], hz, 0.0, Op.add, Op.subtract, ["PC", "ONE"], ["inc"])
        mm(T.PB[:, 64:65], BLK, inc[:, 63:64], True, True, ["inc", "BLK"], ["PB"])
        mm(T.PB[:, 0:64], UPM, inc, True, False, ["inc", "UPM"], ["PB"])
        mm(T.PB[:, 0:64], NUP, inc0, False, True, ["inc", "inc0", "NUP"], ["PB"])
        (act if PSC else cp)(T.P[:, 0:65], T.PB[:, 0:65], ["PB"], ["P"])
        ts(T.spare[:], J1, T.P[:, 64:65], Op.subtract, ["J1", "P"], ["spare"], 0.0, Op.max)
        for m0, m1, s, ps, k in ((0, M0, "0", T.PC[:, 64:80], "PC"), (M0, 16, "1", T.PB[:, 80:96], "PB")):
            c, ma = slice(16 * m0, 16 * m1), m0 + NS[m0 > 0]
            mm(ps[:, m0:m1], IDN, T.spare[:, m0:m1], True, False, ["spare", "IDN"], [k])
            if ma > m0:
                block(lambda: [act(T.junk[:, 64 * m:64 * m + 64], T.ends[:], [], [], func=AF.Sign, scale=-1.0, bias=JB[:, m:m + 1], c=1.4,
                                   accum_out=T.acc[:, m:m + 1]) for m in range(m0, ma)], ["ends", "JB"], ["acc" + s, "junkS" + s])
                ts(T.cL[:, m0:ma], T.acc[:, m0:ma], 64.0, Op.add, ["acc" + s], ["cL" + s], 0.5, Op.mult)
                mm(ps[:, m0:ma], T.I8F[:], T.acc[:, m0:ma], False, False, ["acc" + s, "I8F"], [k], c=4.0)
            if ma < m1:
                for x in range(ma, m1, 2):
                    block(lambda: [ts(T.junk[:, 64 * m:64 * m + 64], T.ends[:], JB[:, m:m + 1], Op.is_lt, [], [], 0.5, Op.subtract) for m in (x, x + 1)],
                          ["ends", "JB"], ["junk%d" % x])
                scan(T.cs[:, 64 * ma:64 * m1], T.RS64[:, 64 * ma:64 * m1], T.junk[:, 64 * ma:64 * m1], 0.0, Op.mult, Op.add, ["junk%d" % x for x in range(ma, m1, 2)] + ["RS64"],
                     ["cs" + s], c=0.5)
                ts(T.cL[:, ma:m1], T.cs[:, 64 * ma + 63:64 * m1:64], 32.0, Op.add, ["cs" + s], ["cV" + s])
                mm(ps[:, ma:m1], I16, T.cs[:, 64 * ma + 63:64 * m1:64], False, False, ["cs" + s, "I16"], [k])
            tt(T.cmp[:, c], T.P[:, 0:65].indirect(T.cL[:, m0:m1]), IO[:, c], Op.is_le, ["P", "IO", "cL" + s, "cV" + s], ["cmp" + s], c=GA)
            sel16(ps[:, m0:m1], lambda r: T.cmp[:, 16 * m0 + r:16 * m1:16], ["cmp" + s], [k], st=False)
            ts(T.bL[:, m0:m1], ps[:, m0:m1], 512.0, Op.add, [k], ["bL" + s])
            cp(T.FO[:, c], T.TX[:, win].indirect(T.bL[:, m0:m1]), ["TX", "TX2", "bL" + s] + ["TX3", "TX4"] * t, ["FO" + s], c=GA)
            tt(T.ug[:, c], T.TU[:, win].indirect(T.bL[:, m0:m1]), T.SCL[:, c], Op.mult, ["TU", "TU2", "SCL", "bL" + s] + ["TU3", "TU4"] * t, ["ug" + s], c=GA)
        if t == 0:
            constants()
        ts(T.xc[:], T.FO[:], -float(MID), Op.add, ["FO0", "FO1"], ["xc"], c=0.5)

        def products(ci):
            s, (ua, ka), (ub, kb) = "01"[ci > 0], U[UB[ci][0]], U[UB[ci][1]]
            j0, n1 = CH * ci, CH // PARTS[ci]
            for o, (u1, k1) in enumerate(((ua, ka), (ub, kb))):
                block(lambda: [mm(u1[:, k:512:8], T.BRD[:, 2 * k + o, :], T.ug[:, j0:j0 + CH], True, True, [], []) for k in range(8)], ["ug" + s, "BRD"], [k1])
            for j in (j0, j0 + 32):
                act(T.G[:, 16 * j:16 * j + 512], Aw.indirect(T.FO[:, j:j + 32]), Ar + ["FO" + s], [Gk[j // 32], "~G"], func=AF.Abs, c=GA)
            for j in range(j0, j0 + CH, n1):
                gk, c, ek = Gk[j // 32:(j + n1 + 31) // 32], slice(8 * (j - j0), 8 * (j - j0 + n1)), Ek[j // 16:(j + n1) // 16]
                tt(T.E[:, 16 * j:16 * (j + n1):2], T.G[:, 16 * j:16 * (j + n1):2], ua[:, c], Op.mult, gk + [ka], ek[0::2])
                if KEEP[ci]:
                    tt(ub[:, c], T.G[:, 16 * j + 1:16 * (j + n1):2], ub[:, c], Op.mult, gk + [kb], [kb])
                else:
                    tt(T.E[:, 16 * j + 1:16 * (j + n1):2], T.G[:, 16 * j + 1:16 * (j + n1):2], ub[:, c], Op.mult, gk + [kb], ek[1::2])
            if FAR[ci]:
                mm(U[UB[ci][2]][0][:, 0:4 * CH], T.IDNF[:], T.E[:, 16 * j0 + 1:16 * (j0 + CH):4], True, False, Ek[4 * ci:4 * ci + 4] + ["IDNF"], [U[UB[ci][2]][1]], c=4.0)

        def largest(ci):
            j0, (ub, kb), (pm, km), r = CH * ci, U[UB[ci][1]], PM[ci], REP[ci]
            cut = list(zip(SEG, SEG[1:]))
            for part, ek, mk in ((cut[:1], Ek[4 * ci:4 * ci + 2], Mk[ci] + "a"), (cut[1:], Ek[4 * ci:4 * ci + 4], Mk[ci])):
                block(lambda: [scan(T.MX[:, 8 * (j0 + x):8 * (j0 + y)], T.E[:, 16 * (j0 + x):16 * (j0 + y):2], ub[:, 8 * x:8 * y] if KEEP[ci] else T.E[:, 16 * (j0 + x) + 1:16 * (j0 + y):2],
                                    0.0, Op.max, Op.max, [], []) for x, y in part], ek + [kb] * KEEP[ci], [mk])
            block(lambda: [mm(pm[:, i:r * CH:r], T.IDNF[:], T.MX[:, 8 * j0 + 7:8 * (j0 + CH):8], True, True, [], [], c=4.0) for i in range(r)], [Mk[ci], Mk[ci] + "a", "IDNF"], [km])

        def marks(ci):
            j0, (ub, kb), (pm, km), r = CH * ci, U[UB[ci][1]], PM[ci], REP[ci]
            c0, c9, M = 16 * j0, 16 * (j0 + CH), T.MX[:, 8 * j0 + 7:8 * (j0 + CH):8]
            if KEEP[ci]:
                block(lambda: [tt(T.TOP[:, c0 + 2 * k + 1:c9:16], ub[:, k:512:8], M, Op.is_lt, [], []) for k in range(8)], [kb, Mk[ci], Mk[ci] + "a"], [Tk[4 * ci + 1], Tk[4 * ci + 3]])
            if FAR[ci]:
                uc, kc = U[UB[ci][2]]
                block(lambda: [mm(uc[:, k:4 * CH:4], T.NIDF[:], M, False, k == 3, [], [], c=4.0) for k in range(4)], [Mk[ci], Mk[ci] + "a", "NIDF"], [kc])
                act(T.TOP[:, c0 + 1:c9:4], uc[:, 0:4 * CH], [kc], [Tk[4 * ci + 1]], func=AF.Sign, scale=-1.0)
            for x, o in enumerate((1, 3, 0, 2) if KEEP[ci] else (0, 2, 3, 1)):
                if not (KEEP[ci] and o % 2 or FAR[ci] and o == 1):
                    block(lambda: [tt(T.TOP[:, c0 + i:c9:16 // r], T.E[:, c0 + i:c9:16 // r], pm[:, 0:r * CH], Op.is_lt, [], []) for i in range(o, 16 // r, 4)],
                          [km] + Ek[4 * ci:4 * ci + 4], [Tk[4 * ci + o]])
                uv, kv = (U[BK[1][0]][0][:, j0 - LA:j0 - LA + CH], U[BK[1][0]][1]) if VB and j0 >= LA else (T.PA[:, j0:j0 + CH], "PA")
                block(lambda: [mm(uv, SEL[:, 16 - k:144 - k], T.TOP[:, c0 + k:c9:16], x == 0 and k == o,
                                  x == 3 and k == 12 + o, [], []) for k in range(o, 16, 4)], [Tk[4 * ci + o], "SEL"], [kv])

        def choose(s):
            lo, hi, ko, kp, kx = STG[s]
            n, c, m = hi - lo, slice(lo, hi), slice(lo // 16, hi // 16)
            k = lambda *x: [y + s for y in x]
            at = lambda b, c0, w=n: ({"PA": T.PA, "PB": T.PB, "PC": T.PC, "PD": T.PD}.get(b) or U[int(b[1])][0])[:, c0:c0 + w]
            kv, kf = "PA", kx
            VT, OH, D3, XP, TK, XV, FA, TH = at(kv, lo), at(ko, L), at(ko, 0), at(kp, 0, n // 16), at(kp, n // 16, n // 16), at(kx, 0), at(kx, L), at(kp, L)
            DN, one = OH, T.ONE[:, 0:n]
            XL, TKL = T.XL[:, m], T.tk[:, m]
            act(T.w[:, c], VT, [kv, "eb"], k("w"), func=AF.Exp, scale=-16.0 * math.log(2.0), bias=ebias)
            Z, ZK, XT = T.Z[:, 2 * lo:2 * lo + n], T.Z[:, 2 * lo + n:2 * hi], at(kp, 0, n // 8)
            mm(D3, D2M, T.w[:, c], True, True, k("w") + ["D2M"], [ko])
            kt = kp
            if s in CHM:
                mm(XT, IDNH, T.JH[:, 16 - n // 16:16 + n // 16], True, False, ["IDNH", "JH", "JH0"], [kp])
                ts(OH, D3, 0.0, Op.is_ge, [ko], k("OH"))
                ts(ZK, D3, 0.0, Op.is_ge, [ko, "cF"], k("ZK"), rcol, Op.mult)
                tt(Z, OH, T.xc[:, c], Op.mult, [ko, "xc"] + k("OH"), k("Z"))
                sel16(XT, lambda r: T.Z[:, 2 * lo + r:2 * hi:16], k("Z", "ZK") + ["SELH"], [kp], mat=T.SELH, st=False)
            else:
                kt = kx if s in TKX else "PB"
                TK = at(kt, 2 * L - 16, n // 16)
                act(T.sg[:, c], D3, [ko], k("sg"), func=AF.Sign)
                act(OH, T.sg[:, c], k("sg"), [ko], func=AF.Relu)
                tt(Z, OH, T.xc[:, c], Op.mult, [ko, "xc"], k("Z"))
                sel16(XP, lambda r: T.Z[:, 2 * lo + r:2 * lo + n:16], k("Z") + ["SELH"], [kp], mat=T.SELH)

            mm(XV, BLKH, Z, True, True, k("Z") + ["BLKH"], [kx])
            ts(XL, XP, float(MID), Op.add, [kp], k("XL"))
            (act if XLS else cp)(T.XLf[:, m], XP, [kp], k("XLf"))
            if DGG:
                tt(T.xd[:, c], XV, T.TRI[:, c], Op.add, [kx, "TRI"], k("xd"))
            else:
                cp(T.XLh[:, m], XP, [kp], k("XLh"))
            cp(T.xr[:, c], XV, [kx], k("xr"))
            if s not in CHM:
                mm(TK, IDNH, T.JK[:, 0:n // 16], True, False, ["IDNH", "JK"], [kt])
                sel16(TK, lambda r: T.sg[:, lo + r:hi:16], k("sg") + ["SELK"], [kt], st=False, mat=SELK)
            act(T.SA[:, c], Aw.indirect(XL), Ar + k("XL"), k("SA"), func=AF.Sign, c=GA)
            if s in HCS:
                act(T.Hc[:, c], Hw.indirect(XL), Hr + k("XL"), k("Hc"), c=GA)
            else:
                cp(T.Hc[:, c], Hw.indirect(XL), Hr + k("XL"), k("Hc"), c=GA)
            cp(TKL, TK, [kt], k("tk"))
            if s in EMV:
                ts(T.EM[:, c], Hw.indirect(XL), -0.5, Op.is_gt, Hr + k("XL"), k("EM"), c=GA)
            else:
                act(T.EM[:, c], Hw.indirect(XL), Hr + k("XL"), k("EM"), func=AF.Relu, bias=1.0, c=GA)
            mm(TH, B9, one, True, False, ["BX", "ONE"], [kp])
            left = [2]
            mm(TH, B4K, T.SA[:, c], False, left, k("SA"), ["+" + kp])
            mm(TH, THM, T.EM[:, c], False, left, k("EM") + ["THM"], ["+" + kp])
            tt(T.AV[:, c], T.Hc[:, c], TH, Op.is_gt, k("Hc") + [kp], k("AV"))
            block(lambda: [mm(DN, BBG, one, True, False, [], []), mm(DN, T.IDNF[:], T.nv[:, c], False, False, [], [], c=4.0)], ["ONE", "BX", "nv"], [ko])
            mm(DN, DNM, T.AV[:, c], False, True, k("AV") + ["DNM"], [ko])
            act(T.fc[:, c], T.TOP[:, 16 * lo:16 * hi].indirect(TKL), k("tk") + ["SG0", "SG1"] + Tk[m], k("fc"), func=AF.Identity,
                scale=T.SG[:, 1, t:t + 1], bias=T.SG[:, 0, t:t + 1], c=GA)
            act(T.AA[:, c], Aw.indirect(XL), Ar + k("XL"), k("AA"), func=AF.Abs, c=GA)
            block(lambda: [mm(FA, IDN, T.fc[:, c], True, False, [], []), mm(FA, BN24, T.AV[:, c], False, True, [], [])], k("AV", "fc"), [kf])
            tt(T.X[:, c], DN, T.Hc[:, c], Op.min, [ko] + k("Hc"), k("X"))
            tt(FA, FA, T.AA[:, c], Op.mult, [kf] + k("AA"), [kf])
            tt(pl[:, c], FA, T.X[:, c], Op.max, [kf] + k("X"), k("PLo"))
            send(peers, [pl[:, c]] * 4, [pl[:, c]] * 4, "ea%d" % t, k("PLo"))
            arrive("PL" + s, "ea%d" % t, 4 * len(STG) * KE, LINK * n)
            act(T.sF[:, c], DN, [ko], k("sF"), func=AF.Sign)

        def places(s):
            lo, hi = 0 if "A" in s else LA, L if "B" in s else LA
            n, c = hi - lo, slice(lo, hi)
            k, k1 = lambda *x: [y + z for y in x for z in s], lambda x: x + s[-1]
            (RR, kr), (UC, kc) = ((U[BK[0][1]][0][:, 32:32 + n], U[BK[0][1]][1]), (T.PB[:, L + 16:L + 16 + n], "PB")) if s == "A" else (
                (T.PA[:, L:L + n], "PA"), (U[BK[0][0]][0][:, 0:n], U[BK[0][0]][1]))
            XB = T.PB[:, 0:n]
            ts(T.ind[:, c], T.xr[:, c], first, Op.is_ge, k("xr") + ["first"], [k1("ind")], c=0.5)
            scan(T.cn[:, c], T.ONE[:, 0:n], T.ind[:, c], T.cn[:, lo - 1:lo] if lo else 0.0, Op.mult, Op.add, [k1("ind"), "cnA"], [k1("cn")], c=0.5)
            mm(UC, DF8, T.ind[:, c], True, False, [k1("ind"), "DF8"], [kc])
            mm(UC, DF, T.cn[:, c], False, True, [k1("cn"), "DF"], [kc])
            if CAPS:
                act(T.Rb[:, c], UC, [kc], [k1("Rb")], func=AF.Relu, bias=-float(TAG + CAP))
            else:
                ts(T.Rb[:, c], UC, TAG + CAP + 0.5, Op.is_gt, [kc], [k1("Rb")])
            if DGG:
                tt(T.dg[:, c], T.XLf[:].indirect(T.colu[:, lo // 16:hi // 16]), T.xd[:, c], Op.is_equal, k("xd") + AB("XLf")[:1 + (s != "A")] + ["colu"], [k1("dg")], c=GA)
            else:
                mm(XB, IDN, T.TRI[:, 0:n], True, False, ["TRI"], ["PB"])
                block(lambda: [mm(XB[:, x:n:16], IDNH, T.XLh[:, lo // 16:hi // 16], False, x == 15, [], []) for x in range(16)], k("XLh"), ["PB"])
                tt(T.dg[:, c], T.xr[:, c], XB, Op.is_equal, k("xr") + ["PB"], [k1("dg")])
            block(lambda: [mm(RR, IDNH, T.NEM[:, c], True, False, [], []), mm(RR, B15, T.cmp[:, c], False, False, [], [])], ["NEM", "cmp0", "cmp1", "B15"], [kr])
            left = [hi // 16 + 3]
            mm(RR, IDNH, T.xr[:, c], False, left, k("xr"), ["+" + kr])
            for m in range(hi // 16 - 1):
                c0 = max(16 * m + 16, lo)
                ts(T.E3[:, m, c0:hi], T.xr[:, c0:hi], T.XLf[:, m:m + 1], Op.is_equal, k("xr") + ["XLf" + x for x in STG if STG[x][0] <= 16 * m < STG[x][1]], [k1("E3%d" % m)], c=0.5)
                mm(RR[:, c0 - lo:n], BBG, T.E3[:, m, c0:hi], False, left, [k1("E3%d" % m)], ["+" + kr])
            mm(RR, BBG, T.dg[:, c], False, left, [k1("dg")], ["+" + kr])
            mm(RR, BBG, T.Rb[:, c], False, left, [k1("Rb")], ["+" + kr])
            mm(RR, BN2K, T.sF[:, c], False, left, k("sF"), ["+" + kr])
            scan(T.YO[:, c], T.RSY[:, c], RR, -65536.0, Op.max, Op.min, [kr, "RSY"], [k1("YO")])
            if s != "A" or OLA:
                o0 = lo if OLA else 0
                ts(ol[:, o0 // 16:hi // 16], T.YO[:, o0 + 15:hi:16], 8.0 * HO, Op.add, ["YOA", "YOB"] if s != "A" else ["YOA"], ["OLo" if s != "A" else "OLoA"])

        pl, ol = T.PL[:, t, me, :], T.OL[:, t, me, :]
        act(T.nv[:], IO[:, win].indirect(T.bL[:]), ["IO", "IO1", "IO2", "bL0", "bL1"], ["nv"], func=AF.Identity, scale=-1.0, bias=-float(TAG * (t + 2) + name0), c=GA)
        for ci in range(NCH + 1):
            if ci < NCH:
                products(ci)
            if ci:
                marks(ci - 1)
            if ci < NCH:
                largest(ci)
            for s in STG:
                if ci == STG[s][1] // CH:
                    choose(s)
        places("".join(STG))
        send(peers, [ol] * 4, [ol] * 4, "eb%d" % t, ["OLo", "OLoA"])
        arrive("OL", "eb%d" % t, 4 * KE, 0.1)
        if t == 0:
            wr["NV1"] = wr["NV1"] + wr["E314B"]
            check(0, T.NV1, "NV1")
            for c in range(2):
                mm(T.PU0[:, 512 * c:512 * c + 512], BN8, T.EQ[:, 512 * c:512 * c + 512], True, True, ["EQ%d" % c, "BX"], ["U%d" % c])
            tt(T.NV[:, 0:B], T.PU0[:], T.NV[:, 0:B], Op.add, ["U0", "U1"], ["NV"])
        for tab, src, k, R, cut in ((T.XR, T.xr, "XR", AB("xr"), (0, 16)), (T.NV, T.nv, "NV", ["nv"], NVC)):
            for m0, m1 in zip(cut, cut[1:]):
                scatter(tab[:, x0:x0 + LW], T.bL[:, m0:m1], src[:, 16 * m0:16 * m1], ["bL0", "bL1", "OLo"] + R, [k, "~X"])
            if t < RO - 1:
                act(tab[:, x0 + B:x0 + B + L], tab[:, x0:x0 + L], [k], [k])
        holdings(min(x0 + L, B))
        for q in range(N - 1, -1, -1):
            scatter(C[:], T.OL[:, t, q, :], T.PL[:, t, q, :], AB("PL") + AB("PLo") + ["OL", "OLo"] + Ar + Hr, ["C", "~C"])
        ts(T.HL[:], U[1][0][:, 0:64], float(MID), Op.add, ["U1"], ["HL"])

    stage[0] = "end"
    check(B)
    tg, sa = T.junk[:, 0:V], T.TU[:, 0:V]
    act(tg, C[:, ho:ho + V], ["C"], ["junk", "junkS0", "junkS1"] + ["junk%d" % x for x in range(0, 16, 2)], func=AF.Identity, scale=-1.0 / TAG, bias=192.0 - 0.3125)
    act(sa, C[:, ao:ao + V], ["C"], ["TU"], func=AF.Sign)
    act(T.MX[:, 0:V], C[:, ao:ao + V], ["C"], MA, func=AF.Abs)
    dma("s", T.yal[:], T.MX[:, 0:V], "dout", MA, [], final=80)
    for c, (c0, c9, ps, k, u) in enumerate(((0, h, T.PA, "PA", "U2"), (h, V, T.PB, "PB", "U3"))):
        cs = slice(512 * c, 512 * c + 512)
        t8 = T.PU1[:, 512 * c:512 * c + h]
        mm(T.PU0[:, cs], BLK, T.EQ[:, cs], True, True, ["EQ%d" % c], ["U%d" % c])
        mm(t8, BNC, T.ONE[:, 0:h], True, False, ["ONE", "BX"], [u])
        mm(t8, I8K, tg[:, c0:c9], False, True, ["junk", "I8K"], [u])
        mm(ps[:, 0:h], IDN, tg[:, c0:c9], True, False, ["junk"], [k])
        mm(ps[:, 0:h], B05, sa[:, c0:c9], False, True, ["TU"], [k])
        tt(T.PU0[:, cs], T.PU0[:, cs], T.monb[:, cs], Op.mult, ["U%d" % c, "monb"], ["U%d" % c])
        tt(T.E[:, c0:c9], t8, C[:, ho + c0:ho + c9], Op.add, [u, "C"] + Ek, ["Y0%d" % c])
        act(T.G[:, cs], Aw.indirect(T.HL[:, 32 * c:32 * c + 32]), ["C", "HL"] + Gk, ["Ga%d" % c], func=AF.Abs, c=GA)
        act(ps[:, 0:h], ps[:, 0:h], [k], [k], func=AF.Sign, scale=-1.0, bias=200.5)
        tt(T.E[:, 2 * B + 512 * c:2 * B + 512 * c + 512], T.PU0[:, cs], T.G[:, cs], Op.mult, ["U%d" % c, "Ga%d" % c], ["Yp%d" % c])
        dma("s", T.yp[:, cs], T.E[:, 2 * B + 512 * c:2 * B + 512 * c + 512], "dout", ["Yp%d" % c], [], final=80)
        tt(T.E[:, B + c0:B + c9], ps[:, 0:h], T.E[:, c0:c9], Op.mult, [k, "Y0%d" % c], ["Y%d" % c])
        dma("s", T.yh[:, c0:c9], T.E[:, B + c0:B + c9], "dout", ["Y%d" % c], [], final=80)

    seen = {}
    for i in _order(nodes):
        n = nodes[i]
        e = n["e"]
        if e[:4] == "link":
            continue
        need = {}
        for j in n["wait"]:
            if nodes[j]["sem"] and not (e == "p" and nodes[j]["e"] == "p"):
                sem, val = nodes[j]["sem"]
                need[sem] = max(need.get(sem, 0), val)
        for sem, val in need.items():
            if seen.get((e, sem), 0) < val:
                Q[e].wait_ge(T.sem[sem], val)
                seen[(e, sem)] = val
        for fn in n["calls"]:
            ins = fn()
        if n["sem"] is None:
            total["s" + e] = total.get("s" + e, 0) + 1
            n["sem"] = ("s" + e, total["s" + e])
            ins.then_inc(T.sem["s" + e], 1)
    for sem, val in total.items():
        g.wait_ge(T.sem[sem], val)
